import numpy as np, ml_dtypes
CORES = [6,15,38,47]
N = 4
BF = ml_dtypes.bfloat16
VX, VY, C, B, LE = 4096, 4096, 256, 4, 6
def parts(rng):
    X = rng.integers(0, 256, (N, 8, 16, VX)); Y = rng.integers(0, 256, (N, 8, 16, VY))
    K = rng.integers(0, VX, (N, 8, 16, C)); G = rng.integers(0, VY, (N, 8, 16, B * C)); W = rng.integers(0, VX, (N, 8, 16, B * C))
    z = rng.integers(0, 256, (N, 8, 16, C)); w = rng.integers(0, 64, (N, 8, 16, 1)); t = rng.integers(1000, 1451, (N, 8, 16, 1))
    return X, Y, K, G, W, z, w, t
def pack(X, Y, K, G, W, z, w, t):
    fl = lambda a: np.ascontiguousarray(np.reshape(a, (N, 128, -1))).astype(np.float32).astype(BF)
    wh = lambda a: np.ascontiguousarray(np.reshape(a, (N, 128, -1))).astype(np.int32)
    return {"gx": fl(X), "sy": fl(Y), "rk": wh(K), "rt": wh(G), "wr": wh(W), "z0": fl(z), "wt": fl(w), "th": wh(t)}
def setup_inputs(rng):
    return pack(*parts(rng))
def uneven(rng, top, bits, shape):
    v = np.exp2(bits * rng.random(shape)).astype(np.int64) - 1
    return np.minimum(np.maximum(np.where(rng.random(shape) < 0.5, v, top - v), 0), top)
def setup_inputs_spread(rng):
    X, Y, K, G, W, z, w, t = parts(rng)
    X = (np.exp2(8 * rng.random((N, 8, 1, VX))) * rng.random(X.shape)).astype(np.int64)
    Y = (np.exp2(8 * rng.random((N, 8, 1, VY))) * rng.random(Y.shape)).astype(np.int64)
    z = (np.exp2(8 * rng.random((N, 8, 1, C))) * rng.random(z.shape)).astype(np.int64)
    lx = VX.bit_length() - 1; ly = VY.bit_length() - 1
    K = uneven(rng, VX - 1, lx, K.shape); W = uneven(rng, VX - 1, lx, W.shape); G = uneven(rng, VY - 1, ly, G.shape)
    w = uneven(rng, 63, 6, w.shape); t = rng.integers(0, 4081, t.shape)
    return pack(X, Y, K, G, W, z, w, t)
def setup_inputs_ends(rng):
    sh = np.array([0.0, 0.1, 0.5, 0.9, 1.0])
    X = 255 * (rng.random((N, 8, 16, VX)) < rng.choice(sh, (N, 8, 1, VX))); Y = 255 * (rng.random((N, 8, 16, VY)) < rng.choice(sh, (N, 8, 1, VY)))
    K = (VX - 1) * rng.integers(0, 2, (N, 8, 16, C)); G = (VY - 1) * rng.integers(0, 2, (N, 8, 16, B * C)); W = (VX - 1) * rng.integers(0, 2, (N, 8, 16, B * C))
    z = 255 * rng.integers(0, 2, (N, 8, 16, C)); w = 63 * rng.integers(0, 2, (N, 8, 16, 1)); t = 4080 * (rng.random((N, 8, 16, 1)) < 0.75)
    w[:, :, 0] = 63; w[:, 0, 1] = 0; t[:, 0] = 4080; t[:, 3, :4] = 0
    for q in range(N):
        for g in range(7):
            m = (q + g) % 4
            if m == 0: X[q, g, :, 0] = 0; X[q, g, :, VX - 1] = 255
            if m == 1: X[q, g, :, 0] = 255; X[q, g, :, VX - 1] = 0
            if m == 2: X[q, g, :, 0] = 255 * rng.integers(0, 2, 16); X[q, g, :, VX - 1] = 255
            if m == 3: X[q, g, :, 0] = 255 * rng.integers(0, 2, 16); X[q, g, :, VX - 1] = 255 * rng.integers(0, 2, 16)
    m1 = [m for m in range(1, 17) if (((((255 * 63 * m) & 4095) ** 2) >> 5) & (B - 1)) == B - 1][0]
    s1 = (VY - 1 + 37 * ((255 * 63 * m1) & 4095)) & (VY - 1)
    X[:, 7, :, 0] = 0; X[:, 7, :, VX - 1] = 255; Y[:, 7, :, 0] = 0; Y[:, 7, :, VY - 1] = 255; Y[:, 7, :, s1] = 255; w[:, 7] = 63; t[:, 7] = 4080
    for i, m in ((C - 1, m1), (C - 2, 0), (C - 3, 13), (C - 4, 16), (0, m1), (1, 0), (2, 16)):
        z[:, 7, :, i] = 255 * (np.arange(16) < m)
        K[:, 7, 15, i] = 0; K[:, 7, 14, i] = VX - 1; K[:, 7, 0, i] = 0; G[:, 7, 14:, B * i:B * i + B] = VY - 1; G[:, 7, 0, B * i:B * i + B] = VY - 1
    return pack(X, Y, K, G, W, z, w, t)
def setup_inputs_corners(rng):
    X, Y, K, G, W, z, w, t = parts(rng); h = VX // 2; v = VY // 4
    X[..., :h] = rng.integers(0, 48, (N, 8, 16, h)); X[..., h:] = rng.integers(208, 256, (N, 8, 16, VX - h)); Y[..., :v] = rng.integers(0, 48, (N, 8, 16, v))
    kind = rng.integers(0, 8, (N, 8, 1, C)); kind[..., :8] = np.arange(8); kind[..., C - 8:] = np.arange(8)
    k = np.arange(16)[:, None]; lane = rng.integers(0, 16, (N, 8, 1, C))
    up = ((kind == 1) & (k == 0)) | ((kind == 2) & (k == 15)) | ((kind == 3) & (k == lane)) | ((kind == 4) & (k <= lane))
    lh = np.where(up, rng.integers(h, VX, K.shape), rng.integers(0, h, K.shape))
    K = np.where(kind == 7, (VX - 1) * rng.integers(0, 2, K.shape), np.where(kind == 6, K, lh))
    z = np.where(kind < 5, rng.integers(64, 96, z.shape), np.where(kind == 5, 255, np.where(kind == 6, 0, z)))
    M = np.zeros((8, 16), np.int64); M[1] = 4080; M[7] = 4080; M[2, 15] = 4080; M[3, 0] = 4080; M[4, ::2] = 4080; M[5, :15] = 4080
    mode = (np.arange(N)[:, None] + np.arange(8)) % 8
    t = np.where((mode == 6)[:, :, None, None], rng.choice(np.array([0, 1, 4079, 4080, 1300]), t.shape), M[mode][..., None])
    q = rng.permutation(N); t[q[0]] = 0; t[q[1]] = 4080
    a = rng.integers(0, 3, (N, 8, 1, 1)); a[:, 0] = 0; a[:, 7] = 1; w = np.where(a == 0, 0, np.where(a == 1, 63, w))
    W = np.where(rng.random((N, 8, 1, 1)) < 0.4, (VX - 1) * rng.integers(0, 2, W.shape), W)
    G = np.where(rng.random((N, 8, 1, 1)) < 0.4, (VY - 1) * rng.integers(0, 2, G.shape), G)
    z[q[1], ::2] = 0
    e = int(q[2])
    X[e] = np.minimum(X[e], 254); Y[e] = rng.integers(0, 61, Y[e].shape); K[e] = rng.integers(0, h, K[e].shape); z[e] = 255; t[e] = rng.integers(2900, 3301, t[e].shape)
    b = int(q[3]); gb = (7 - b) % 8
    X[b, gb] = np.minimum(X[b, gb], 254); z[b, gb] = 255
    return pack(X, Y, K, G, W, z, w, t)
def setup_inputs_ties(rng):
    X, Y, K, G, W, z, w, t = parts(rng)
    X[:, ::2] = 128 * rng.integers(0, 2, (N, 4, 16, VX)); Y[:, ::2] = 128 * rng.integers(0, 2, (N, 4, 16, VY))
    X[:, 1::2] = 85 * rng.integers(0, 4, (N, 4, 16, VX)); Y[:, 1::2] = 85 * rng.integers(0, 4, (N, 4, 16, VY))
    z[:, ::2] = 16 * rng.integers(0, 9, (N, 4, 16, C)); z[:, 1::2] = np.maximum(85 * rng.integers(0, 4, (N, 4, 16, C)) - 16 * rng.integers(0, 8, (N, 4, 16, C)), 0)
    t[:, ::2] = 128 * rng.integers(6, 12, (N, 4, 16, 1)); t[:, 1::2] = 85 * rng.integers(17, 24, (N, 4, 16, 1))
    t = t + rng.integers(-1, 2, t.shape) * (rng.random(t.shape) < 0.5)
    X[:, 5] = rng.integers(200, 256, (N, 16, VX)); Y[:, 5] = rng.integers(0, 61, (N, 16, VY))
    X[:, 6] = rng.integers(0, 61, (N, 16, VX)); Y[:, 6] = rng.integers(200, 256, (N, 16, VY))
    t[:, 5:7] = 3160 + rng.integers(-300, 151, (N, 2, 16, 1))
    return pack(X, Y, K, G, W, z, w, t)
def setup_inputs_alike(rng):
    X, Y, K, G, W, z, w, t = parts(rng)
    K[:, ::2] = K[:, ::2, :1, :].copy(); K[:, 1] = K[:, 1, :, :1].copy(); W[:, 1] = W[:, 1, :, :1].copy()
    W[:, 2:4] = np.repeat(K[:, 2:4], B, axis=-1); G[:, 4] = G[:, 4, :1, :1].copy(); z[:, 5] = z[:, 5, :, :1].copy()
    few = np.array([0, VX - 1, VX // 2, 3]); K[:, 7] = rng.choice(few, (N, 16, C)); W[:, 7] = rng.choice(few, (N, 16, B * C))
    return pack(X, Y, K, G, W, z, w, t)
def check_inputs(d):
    bad = []
    for k, hi in (("gx", 255), ("sy", 255), ("rk", VX - 1), ("rt", VY - 1), ("wr", VX - 1), ("z0", 255), ("wt", 63), ("th", 4080)):
        a = np.asarray(d[k]).astype(np.float64)
        if not (np.min(a) >= 0 and np.max(a) <= hi): bad.append("range of " + k)
        elif not np.all(a == np.floor(a)): bad.append("whole numbers of " + k)
    return bad
def reference(gx, sy, rk, rt, wr, z0, wt, th):
    ints = lambda a, n: a.astype(np.float32).astype(np.int32).reshape(N, 8, 16, n)
    X, Y, z, w = ints(gx, VX), ints(sy, VY), ints(z0, C), ints(wt, 1)
    K = rk.astype(np.int64).reshape(N, 8, 16, C); G = rt.astype(np.int64).reshape(N, 8, 16, B * C); W = wr.astype(np.int64).reshape(N, 8, 16, B * C)
    t = th.astype(np.int64).reshape(N, 8, 16, 1); A = np.zeros((N, 1, 1, 1), np.int64)
    margin = (16 * ((15 - np.arange(16)) >> 1)).astype(np.int32)[:, None]
    for lead in range(LE):
        if lead > 0: K = np.roll(K, 1, axis=0); z = np.roll(z, 1, axis=0)
        u = np.add.reduce(w.astype(np.int64) * z, axis=2) & 4095
        c = B * np.arange(C) + (((u * u) >> 5) & (B - 1)); cc = np.broadcast_to(c[:, :, None, :], K.shape)
        route = np.take_along_axis(G, cc, 3); old = np.take_along_axis(W, cc, 3)
        s = (((route * K) >> 5) + route + 37 * u[:, :, None, :]) & (VY - 1)
        x = np.take_along_axis(X, K.reshape(N, 8, 1, 16 * C), 3).reshape(N, 8, 16, 16, C)
        y = np.take_along_axis(Y, s.reshape(N, 8, 1, 16 * C), 3).reshape(N, 8, 16, 16, C)
        placed = np.add.reduce(np.abs(x - y), axis=2) < t + A
        hold = placed & (np.count_nonzero(x >= z[:, :, :, None, :] + margin, axis=2) >= 9)
        stop = np.logical_or.accumulate(hold[:, :, ::-1], axis=2)[:, :, ::-1]
        held = placed & stop; fail = placed & ~stop
        h, f, o = held.astype(np.int64), fail.astype(np.int64), 1 - placed.astype(np.int64)
        nh = np.add.reduce(h, axis=2)[:, :, None]; nf = np.add.reduce(f, axis=2)[:, :, None]
        over = np.add.accumulate(h[:, :, ::-1], axis=2)[:, :, ::-1] - h
        pos = np.where(held, over, np.where(fail, nh + np.add.accumulate(f, axis=2) - f, nh + nf + np.add.accumulate(o, axis=2) - o))
        new = np.zeros_like(K); np.put_along_axis(new, pos, np.where(fail, old, K), 2)
        np.put_along_axis(W, cc, np.where(fail, K, old), 3)
        z = np.abs(z - np.maximum.reduce(np.where(held[:, :, None], x, 0), axis=3))
        A = 16 * (np.add.reduce(f, axis=(1, 2, 3)) & 31).reshape(N, 1, 1, 1)
        K = new
    return {"yk": K.reshape(N, 128, C).astype(np.float32), "yw": W.reshape(N, 128, B * C).astype(np.float32), "yz": z.reshape(N, 128, C).astype(np.float32).astype(BF)}

@@ -1,0 +1,583 @@
+import numpy as np
+from concourse.bass import DstId, RemoteDMATransfer
+from concourse.mybir import dt, AluOpType, AxisListType, ActivationFunctionType
+
+A = AluOpType
+AF = ActivationFunctionType
+LE = 6
+SLOTS = ["ones", "BD0", "BD", "ID", "ID64", "NID", "IDm32", "IDh", "TGE", "SLT", "SGT", "SD0", "SD", "NBD", "NSLT", "ID16",
+         "ID64t", "DE", "DX", "DK", "DKL"]
+
+SCRATCH = {
+    "X": ("sbuf", [128, 4096], "bfloat16"), "Y": ("sbuf", [128, 4096], "bfloat16"),
+    "Gf": ("sbuf", [128, 1024], "float32"), "Wf": ("sbuf", [128, 1024], "float32"),
+    "rti": ("sbuf", [128, 1024], "int32"), "wri": ("sbuf", [128, 1024], "int32"), "rki": ("sbuf", [128, 256], "int32"),
+    "thi": ("sbuf", [128, 1], "int32"), "wtb": ("sbuf", [128, 1], "bfloat16"),
+    "Z4": ("sbuf", [128, 12 * 512], "bfloat16"), "HL": ("sbuf", [128, 12 * 256], "bfloat16"),
+    "HS": ("sbuf", [128, 12 * 256], "bfloat16"), "ZS": ("sbuf", [128, 12 * 128], "bfloat16"),
+    "TB": ("sbuf", [128, 128 * len(SLOTS)], "bfloat16"),
+    "IDF": ("sbuf", [128, 128], "float32"), "ONE16": ("sbuf", [128, 128], "float32"),
+    "L1": ("sbuf", [128, 2048], "bfloat16"), "L2": ("sbuf", [128, 2048], "bfloat16"),
+    "PQ": ("sbuf", [128, 2048], "bfloat16"), "WL": ("sbuf", [128, 2048], "bfloat16"),
+    "W37": ("sbuf", [128, 128], "float16"),
+    "COL": ("sbuf", [128, 16], "float32"), "kk": ("sbuf", [128, 16], "float32"), "RK": ("sbuf", [128, 16], "float32"),
+    "rowi": ("sbuf", [128, 2], "int32"), "r15": ("sbuf", [128, 2], "int32"),
+    "I4a": ("sbuf", [128, 8], "int32"), "I4": ("sbuf", [128, 8], "int32"),
+    "Fi": ("sbuf", [128, 1], "int32"), "Fj": ("sbuf", [128, 1], "int32"),
+    "YK": ("sbuf", [128, 256], "float32"), "hI": ("sbuf", [128, 256], "int32"), "lI": ("sbuf", [128, 256], "int32"),
+}
+for _c in range(2):
+    for _n, _w, _d in (("K16", 128, "uint16"), ("x", 2048, "bfloat16"), ("d", 2048, "bfloat16"), ("sg", 2048, "bfloat16"),
+                       ("ua", 8, "int32"), ("ub", 8, "int32"), ("uc", 8, "int32"), ("ud", 8, "int32"), ("ue", 8, "int32"),
+                       ("c16", 8, "uint16"), ("Gs", 128, "float32"), ("Wo", 128, "float32"), ("dk", 128, "float32"),
+                       ("dl", 128, "float32"), ("val", 128, "float32"), ("p1", 128, "int32"), ("pr", 128, "int32"),
+                       ("s1", 128, "int32"), ("s2", 128, "int32"), ("s16", 128, "uint16"), ("o", 128, "bfloat16"),
+                       ("hd", 128, "bfloat16"), ("eo", 128, "bfloat16"), ("f", 128, "bfloat16"), ("h", 128, "bfloat16"),
+                       ("m", 128, "bfloat16"), ("h64", 128, "bfloat16"), ("WW", 256, "float16"),
+                       ("CL", 15 * 256, "float16"), ("AC", 256, "float16"), ("mz", 128, "float16"), ("Fs", 1, "float32")):
+        SCRATCH[_n + str(_c)] = ("sbuf", [128, _w], _d)
+for _b in range(8):
+    SCRATCH["ps%d" % _b] = ("psum", [128, 512], "float32")
+
+SEMAPHORES = ["eV", "eS", "eT", "eG", "loc"] + ["ld%d" % _i for _i in range(20)] + ["st%d" % _i for _i in range(8)]
+for _e in range(LE):
+    for _c in range(2):
+        SEMAPHORES += ["zr%d_%d" % (_e, _c), "ah%d_%d" % (_e, _c), "az%d_%d" % (_e, _c)]
+
+CY = 0.83e-3 * 1.25
+TC = 0.42e-3 * 1.25
+GAT = 1.55
+SCA = 3.8
+YS = ()
+NOISE, SEED, WIN, BON = 0.0, 0, 0.02, 0.0
+_OFF = [
+    [15, 31, -2, -25, 55, 35, 8, 160, 63, 53, 15, 11, 25, 37, -30, 33, -3, 8, 48, 22, 15, 7, 8, 30, -5, -6, 11, 52, 2, 83, -6, 11, -5, 40, 8, -23, 61, 98, 2, 36, 32, 67, 21, 54, 23, 37, 62, 43, 47, 44, -12, -25, 18, 67, -4, 64, 35, 31, -69, 33, 9, 51, -23, 46, -6, 24, 10, 77, 36, -46, -65, 60, 31, 47, -6, 19, 2, 11, 23, 23, -11, 9, -34, -43, -11, -13, -20, 25, 21, 65, 4, 31, 1, 52, -15, 51, -57, 30, -74, -30, 44, 28, 22, 10, -43, -3, -24, 33, 14, 65, 18, 0, -13, 4],
+    [-42, -73, 42, 3, 40, 4, -27, 28, 27, -103, -24, 68, 5, 34, 66, -27, -22, -38, 24, -14, -14, -24, -21, -40, -40, 47, -2, 35, 23, -30, -84, -68, -82, -70, -72, -72, 35, -51, -108, -26, -28, -25, -65, -80, -5, -54, -111, -32, -11, -69, -6, -24, -20, 36, -80, -14, -111, 33, 50, 68, 2, 45, 26, 24, 92, 84, 105, -5, 38, -4, 16, 17, 14, 23, 6, 19, 43, 4, 9, 4, -1, 103, 6, 30, -3, -1, 23, 46, 13, -2, -28, -73, 0, -79, -50, 11, -48, -12, -13, 8, 7, 5, -16, -5, 67, -46, -49, -5, 11, 30, -48, 82, -67, -41, -64]]
+OFFS = {(_c, _i): float(_v) for _c in range(2) for _i, _v in enumerate(_OFF[_c])}
+HOP = 0.08
+
+
+def rank_program(g, core, T, topo):
+    rank = T.rank_of(core)
+    if rank is None:
+        return
+    cores = list(T.cores)
+    dst = cores[(rank + 1) % len(cores)]
+    rid, pid, _s = topo.addr(dst)
+    engines = topo.engines(core, dst)
+    emask = topo.mask(core, dst)
+    neng = len(engines)
+
+    V, S, TE, SY = g.vector, g.scalar, g.tensor, g.sync
+    QS = {"V": V, "S": S, "T": TE, "G": g, "Y": SY}
+    ops, acc = [], {}
+    cur = [-1, -1, 0]
+
+    def add(q, dur, emit, R=(), W=(), kind="c", sem=None, val=0, lat=0.0, extra=()):
+        i = len(ops)
+        deps = {}
+        for j in extra:
+            deps[j] = False
+        for isw, regs in ((False, R), (True, W)):
+            for buf, lo, hi in regs:
+                lst = acc.setdefault(buf, [])
+                ps = buf[:2] == "ps"
+                keep = []
+                for a in lst:
+                    j, l, h, aw = a
+                    if j == i:
+                        keep.append(a)
+                        continue
+                    over = ps or (l < hi and lo < h)
+                    same = ops[j]["q"] == q and ops[j]["kind"] == "c" and kind == "c"
+                    if over:
+                        if ps:
+                            deps[j] = deps.get(j, False) or not same
+                        elif isw or aw:
+                            deps[j] = deps.get(j, False) or (aw if same else True)
+                    if ps and same:
+                        continue
+                    if isw and (not ps) and l >= lo and h <= hi:
+                        continue
+                    keep.append(a)
+                keep.append((i, lo, hi, isw))
+                acc[buf] = keep
+        ops.append({"q": q, "dur": dur, "emit": emit, "deps": deps, "kind": kind, "sem": sem, "val": val, "lat": lat,
+                    "key": (cur[0], cur[1], i - cur[2])})
+        return i
+
+    def vt(n, rate=1.0):
+        return 0.03 + max(64, n * rate) * CY
+
+    def tt(n, cnt=1, f=1):
+        return 0.02 + cnt * max(64, n) * TC * f
+
+    def sl(n):
+        s = SLOTS.index(n)
+        return T.TB[:, 128 * s:128 * s + 128]
+
+    def rs(n):
+        s = SLOTS.index(n)
+        return ("TB", 128 * s, 128 * s + 128)
+
+    def col(i):
+        return T.COL[:, i:i + 1]
+
+    def rc(i):
+        return ("COL", i, i + 1)
+
+    def mm(o, l, r, a, b):
+        return TE.matmul(o, l, r, a, b)
+
+    def ts(out, in0, s1, s2, op0, op1=None):
+        if op1 is None:
+            return V.tensor_scalar(out, in0, s1, None, op0)
+        return V.tensor_scalar(out, in0, s1, s2, op0, op1)
+
+    nld = [0]
+
+    def load(q, out, in_, reg, dur, lat):
+        s = "ld%d" % nld[0]
+        nld[0] += 1
+        eng = QS[q]
+        add(q, dur, lambda: eng.dma_start(out, in_), (), (reg,), kind="d", sem=s, val=16, lat=lat)
+
+    load("Y", T.rki[:, :], T.rk[:, :], ("rki", 0, 256), 0.1, 2.2)
+    load("S", T.Z4[:, 0:128], T.z0[:, 0:128], ("Z4", 0, 128), 0.1, 2.2)
+    load("S", T.wtb[:, :], T.wt[:, :], ("wtb", 0, 1), 0.1, 2.2)
+    load("Y", T.rti[:, 0:512], T.rt[:, 0:512], ("rti", 0, 512), 0.1, 3.5)
+    load("S", T.X[:, :], T.gx[:, :], ("X", 0, 4096), 0.1, 6.5)
+    load("S", T.Z4[:, 512:640], T.z0[:, 128:256], ("Z4", 512, 640), 0.1, 6.5)
+    load("Y", T.Y[:, :], T.sy[:, :], ("Y", 0, 4096), 0.1, 9.5)
+    load("Y", T.thi[:, :], T.th[:, :], ("thi", 0, 1), 0.1, 9.5)
+    load("Y", T.wri[:, 0:512], T.wr[:, 0:512], ("wri", 0, 512), 0.1, 10.5)
+    load("Y", T.rti[:, 512:1024], T.rt[:, 512:1024], ("rti", 512, 1024), 0.1, 11.5)
+    load("Y", T.wri[:, 512:1024], T.wr[:, 512:1024], ("wri", 512, 1024), 0.1, 12.5)
+
+    add("V", vt(128, .5), lambda: V.memset(sl("ones"), 1.0), (), (rs("ones"),))
+    add("G", .4, lambda: g.iota(T.rowi[:, 0:1], [[0, 1]], 0, 1), (), (("rowi", 0, 1),))
+    add("G", .4, lambda: g.affine_select(sl("BD0"), sl("ones"), [[-16, 8], [0, 16]], A.is_ge, 0.0, 0, 1), (rs("ones"),), (rs("BD0"),))
+    add("G", .4, lambda: g.affine_select(sl("BD"), sl("BD0"), [[16, 8], [0, 16]], A.is_ge, 0.0, 15, -1), (rs("BD0"),), (rs("BD"),))
+    add("G", .4, lambda: g.affine_select(sl("ID"), sl("ones"), [[-1, 128]], A.is_equal, 0.0, 0, 1), (rs("ones"),), (rs("ID"),))
+    add("G", .2, lambda: g.iota(T.I4a[:, :], [[64, 8]], 0, 0), (), (("I4a", 0, 8),))
+    add("G", .2, lambda: g.iota(T.kk[:, :], [[1, 16]], 0, 0, allow_small_or_imprecise_dtypes=True), (), (("kk", 0, 16),))
+    add("G", .4, lambda: g.affine_select(sl("TGE"), sl("BD"), [[-1, 128]], A.is_ge, 0.0, 0, 1), (rs("BD"),), (rs("TGE"),))
+    add("V", vt(1), lambda: ts(T.r15[:, 0:1], T.rowi[:, 0:1], 15, None, A.bitwise_and), (("rowi", 0, 1),), (("r15", 0, 1),))
+    add("V", vt(1), lambda: V.tensor_copy(col(0), T.r15[:, 0:1]), (("r15", 0, 1),), (rc(0),))
+
+    def lin(o, i, a, b):
+        add("V", vt(1), lambda: ts(col(o), col(i), float(a), float(b), A.mult, A.add), (rc(i),), (rc(o),))
+    lin(10, 0, 4, 0)
+    add("V", vt(8), lambda: ts(T.I4[:, :], T.I4a[:, :], col(10), None, A.add), (("I4a", 0, 8), rc(10)), (("I4", 0, 8),))
+
+    def scl(o, i, a):
+        add("S", vt(128), lambda: S.activation(sl(o), sl(i), AF.Copy, scale=float(a)), (rs(i),), (rs(o),))
+    scl("ID64", "ID", 64)
+    add("V", vt(2048, .5), lambda: V.memset(T.L1[:, :], 0.0), (), (("L1", 0, 2048),))
+
+    def cpy(buf, base, off, src):
+        a = 128 * SLOTS.index(src)
+        add("S", vt(8), lambda: S.activation(T[buf][:, base + off:base + 128:16], T.TB[:, a + off:a + 128:16], AF.Copy),
+            (rs(src),), ((buf, base + off, base + off + 113),))
+    for k in range(16):
+        cpy("L1", 128 * k, k, "BD")
+    add("V", vt(2048, .5), lambda: ts(T.WL[:, :], T.L1[:, :], T.wtb[:, 0:1], None, A.mult), (("L1", 0, 2048), ("wtb", 0, 1)), (("WL", 0, 2048),))
+    add("V", vt(1), lambda: ts(col(7), T.wtb[:, 0:1], 37.0, None, A.mult), (("wtb", 0, 1),), (rc(7),))
+    add("V", vt(1), lambda: ts(col(8), col(7), 2048.0, -4096.0, A.is_gt, A.mult), (rc(7),), (rc(8),))
+    add("V", vt(1), lambda: V.tensor_tensor(col(9), col(7), col(8), A.add), (rc(7), rc(8)), (rc(9),))
+    add("V", vt(128, .5), lambda: ts(T.W37[:, :], sl("BD"), col(9), None, A.mult), (rs("BD"), rc(9)), (("W37", 0, 128),))
+    add("V", vt(128), lambda: V.tensor_copy(T.IDF[:, :], sl("ID")), (rs("ID"),), (("IDF", 0, 128),))
+
+    def hl0(c):
+        a, b = 128 * c, 128 * c + 128
+        add("V", vt(128), lambda: ts(T.hI[:, a:b], T.rki[:, a:b], 6, None, A.arith_shift_right), (("rki", 0, 256),), (("hI", a, b),))
+        add("V", vt(128), lambda: ts(T.lI[:, a:b], T.rki[:, a:b], 63, None, A.bitwise_and), (("rki", 0, 256),), (("lI", a, b),))
+        add("V", vt(128), lambda: V.tensor_copy(T.HL[:, 256 * c:256 * c + 128], T.hI[:, a:b]), (("hI", a, b),), (("HL", 256 * c, 256 * c + 128),))
+        add("V", vt(128), lambda: V.tensor_copy(T.HL[:, 256 * c + 128:256 * c + 256], T.lI[:, a:b]), (("lI", a, b),), (("HL", 256 * c + 128, 256 * c + 256),))
+    hl0(0)
+    hl0(1)
+
+    def conv(dst_, src, c):
+        a, b = 512 * c, 512 * c + 512
+        add("V", vt(512), lambda: V.tensor_copy(T[dst_][:, a:b], T[src][:, a:b]), ((src, a, b),), ((dst_, a, b),))
+    conv("Gf", "rti", 0)
+    conv("Wf", "wri", 0)
+    conv("Gf", "rti", 1)
+    conv("Wf", "wri", 1)
+    add("V", vt(1), lambda: V.tensor_copy(col(11), T.thi[:, 0:1]), (("thi", 0, 1),), (rc(11),))
+    lin(1, 0, -1, 15)
+    lin(2, 0, -2, 15)
+    lin(3, 0, 64, 0)
+    lin(4, 0, 64, 8256)
+    lin(5, 0, 64, -960)
+    scl("NID", "ID", -1)
+    scl("IDm32", "ID", -1 / 32)
+    scl("IDh", "ID", 0.5)
+    scl("ID16", "ID", 1 / 16)
+    scl("ID64t", "ID", 1 / 64)
+    scl("NBD", "BD", -1)
+    add("G", .4, lambda: g.affine_select(sl("SLT"), sl("BD"), [[1, 128]], A.is_ge, 0.0, -1, -1), (rs("BD"),), (rs("SLT"),))
+    add("G", .4, lambda: g.affine_select(sl("SGT"), sl("BD"), [[-1, 128]], A.is_ge, 0.0, -1, 1), (rs("BD"),), (rs("SGT"),))
+    add("V", vt(128, 2), lambda: V.tensor_tensor(sl("SD0"), sl("SLT"), sl("SGT"), A.subtract), (rs("SLT"), rs("SGT")), (rs("SD0"),))
+    scl("SD", "SD0", 1 / 1024)
+    scl("NSLT", "SLT", -1 / 16)
+    for nm, ci in (("DE", 1), ("DX", 2), ("DK", 3), ("DKL", 4)):
+        def dg(nm=nm, ci=ci):
+            add("S", vt(128), lambda: S.activation(sl(nm), sl("ID"), AF.Copy, scale=col(ci)), (rs("ID"), rc(ci)), (rs(nm),))
+        dg()
+    add("V", vt(128), lambda: V.memset(T.ONE16[:, :], 16.0), (), (("ONE16", 0, 128),))
+    add("V", vt(16), lambda: ts(T.RK[:, :], T.kk[:, :], col(0), 256.0, A.is_equal, A.mult), (("kk", 0, 16), rc(0)), (("RK", 0, 16),))
+    for k in range(16):
+        def l2(k=k):
+            add("S", vt(128), lambda: S.activation(T.L2[:, 128 * k:128 * k + 128], sl("BD"), AF.Copy, scale=T.RK[:, k:k + 1]),
+                (rs("BD"), ("RK", 0, 16)), (("L2", 128 * k, 128 * k + 128),))
+        l2()
+    add("V", vt(2048, .5), lambda: V.memset(T.PQ[:, :], 0.0), (), (("PQ", 0, 2048),))
+    for k in range(16):
+        cpy("PQ", 128 * k, k, "BD")
+        if k < 15:
+            cpy("PQ", 128 * k, k + 1, "NBD")
+
+    for e in range(LE):
+        for c in range(2):
+            cur[0], cur[1], cur[2] = e, c, len(ops) + (0 if e else -2)
+            _lead(e, c, T, g, V, S, TE, SY, add, vt, tt, sl, rs, col, rc, mm, ts, rid, pid, emask, neng, ops)
+
+    n = len(ops)
+    succ = [[] for _ in range(n)]
+    cnt = [0] * n
+    for i, o in enumerate(ops):
+        for j in o["deps"]:
+            succ[j].append(i)
+        cnt[i] = len(o["deps"])
+    tail = [0.0] * n
+    for i in range(n - 1, -1, -1):
+        o = ops[i]
+        tail[i] = o["dur"] + o["lat"] + max([tail[k] + HOP for k in succ[i]] + [0.0])
+    rng = np.random.RandomState(SEED)
+    for i in range(n):
+        tail[i] = tail[i] + NOISE * float(rng.rand()) + (OFFS.get(ops[i]["key"][1:], 0.0) if ops[i]["key"][0] >= 0 else 0.0)
+    free = {}
+    ready = [0.0] * n
+    cand = {}
+    for i in range(n):
+        if cnt[i] == 0:
+            cand.setdefault(ops[i]["q"], []).append(i)
+    order = []
+    while True:
+        best = None
+        for q, lst in cand.items():
+            if not lst:
+                continue
+            fq = free.get(q, 0.0)
+            st = min(max(fq, ready[i]) for i in lst)
+            pick = max((i for i in lst if max(fq, ready[i]) <= st + WIN), key=lambda i: (tail[i], -i))
+            if best is None or st < best[0]:
+                best = (st, q, pick)
+        if best is None:
+            break
+        _st, q, i = best
+        cand[q].remove(i)
+        start = max(free.get(q, 0.0), ready[i])
+        if ops[i]["kind"] == "r":
+            end = start
+        else:
+            end = start + ops[i]["dur"]
+            free[q] = end
+        end += ops[i]["lat"]
+        order.append(i)
+        for k in succ[i]:
+            inorder = ops[k]["q"] == q and not ops[k]["deps"][i]
+            ready[k] = max(ready[k], end if inorder else end + HOP)
+            cnt[k] -= 1
+            if cnt[k] == 0:
+                cand.setdefault(ops[k]["q"], []).append(k)
+    if len(order) != n:
+        raise ValueError("cycle")
+
+    count = {"V": 0, "S": 0, "T": 0, "G": 0}
+    known = {q: {} for q in ("V", "S", "T", "G", "Y")}
+    nsend = 0
+    for i in order:
+        o = ops[i]
+        q = o["q"]
+        if o["kind"] == "r":
+            o["clk"] = {o["sem"]: o["val"]}
+            continue
+        kn = known[q]
+        for j in sorted((j for j, w in o["deps"].items() if w), key=lambda j: -order.index(j) if False else -j):
+            p = ops[j]
+            if p["kind"] == "s":
+                raise ValueError("nothing waits for a send")
+            sem, val = (p["sem"], p["val"]) if p["kind"] != "c" else ("e" + p["q"], p["pos"])
+            if kn.get(sem, 0) < val:
+                QS[q].wait_ge(T.sem[sem], val)
+                for s2, v2 in p["clk"].items():
+                    if kn.get(s2, 0) < v2:
+                        kn[s2] = v2
+        ins = o["emit"]()
+        clk = dict(kn)
+        if o["kind"] == "c":
+            count[q] += 1
+            o["pos"] = count[q]
+            ins.then_inc(T.sem["e" + q], 1)
+            clk["e" + q] = count[q]
+        elif o["kind"] == "d":
+            if ins is not None:
+                ins.then_inc(T.sem[o["sem"]], 16)
+            clk[o["sem"]] = o["val"]
+        else:
+            nsend += 1
+        o["clk"] = clk
+    kn = known["Y"]
+    for q in ("V", "S", "T", "G"):
+        SY.wait_ge(T.sem["e" + q], count[q])
+    for o in ops:
+        if o["kind"] in ("d", "r"):
+            if kn.get(o["sem"], 0) < o["val"]:
+                SY.wait_ge(T.sem[o["sem"]], o["val"])
+                kn[o["sem"]] = o["val"]
+    g.wait_ge(T.sem.loc, neng * nsend)
+
+
+def _lead(e, c, T, g, V, S, TE, SY, add, vt, tt, sl, rs, col, rc, mm, ts, rid, pid, emask, neng, ops):
+    first, last = e == 0, e == LE - 1
+    n = 2 * e + c
+    B = lambda nm: T[nm + str(c)]
+    R = lambda nm, a=0, b=None: (nm + str(c), a, b if b is not None else SCRATCH[nm + str(c)][1][1])
+    P = lambda b: T["ps%d" % b]
+    PR = lambda b: ("ps%d" % b, 0, 512)
+    zb, hb = 512 * n, 256 * n
+    z = T.Z4[:, zb:zb + 128]
+    hi, lo = T.HL[:, hb:hb + 128], T.HL[:, hb + 128:hb + 256]
+    rz, rhl = ("Z4", zb, zb + 128), ("HL", hb, hb + 256)
+    if not first:
+        sh, sz = _lead_sends[(e - 1, c)]
+        add("R", 0, None, (), (rhl,), kind="r", sem="ah%d_%d" % (e, c), val=neng, lat=3.0, extra=(sh,))
+        add("R", 0, None, (), (rz,), kind="r", sem="az%d_%d" % (e, c), val=neng, lat=3.0, extra=(sz,))
+
+    def zrep():
+        s = T.sem["zr%d_%d" % (e, c)]
+        for j in range(1, 4):
+            SY.dma_start(T.Z4[:, zb + 128 * j:zb + 128 * j + 128], z).then_inc(s, 16)
+        return None
+    add("Y", 0.3, zrep, (rz,), (("Z4", zb + 128, zb + 512),), kind="d", sem="zr%d_%d" % (e, c), val=48, lat=2.2)
+
+    def fK(o):
+        mm(o, sl("ID64"), hi, True, False)
+        return mm(o, sl("ID"), lo, False, True)
+    Kp = P(7)[:, 0:128]
+    add("T", tt(128, 2), lambda: fK(Kp), (rhl, rs("ID64"), rs("ID")), (PR(7),))
+    add("V", vt(128), lambda: V.tensor_copy(B("K16")[:, :], Kp), (PR(7),), (R("K16"),))
+
+    def fU():
+        for r in range(16):
+            i = mm(P(7)[:, 128:136], T.WL[:, 128 * r:128 * r + 128], T.Z4[:, zb + r:zb + 128:16], r == 0, r == 15)
+        return i
+    add("T", tt(8, 16), fU, (rz, ("WL", 0, 2048)), (PR(7),))
+    add("V", vt(8), lambda: V.tensor_copy(B("ua")[:, :], P(7)[:, 128:136]), (PR(7),), (R("ua"),))
+    add("V", vt(8), lambda: ts(B("ub")[:, :], B("ua")[:, :], 63, None, A.bitwise_and), (R("ua"),), (R("ub"),))
+    add("V", vt(8), lambda: V.tensor_tensor(B("uc")[:, :], B("ub")[:, :], B("ub")[:, :], A.mult), (R("ub"),), (R("uc"),))
+    add("V", vt(8), lambda: ts(B("ud")[:, :], B("uc")[:, :], 5, 3, A.arith_shift_right, A.bitwise_and), (R("uc"),), (R("ud"),))
+    add("V", vt(8), lambda: V.tensor_tensor(B("ue")[:, :], B("ud")[:, :], T.I4[:, :], A.add), (R("ud"), ("I4", 0, 8)), (R("ue"),))
+    add("V", vt(8), lambda: V.tensor_copy(B("c16")[:, :], B("ue")[:, :]), (R("ue"),), (R("c16"),))
+    wa, wb = 512 * c, 512 * c + 512
+    add("S", vt(128, GAT), lambda: S.activation(B("Gs")[:, :], T.Gf[:, wa:wb].indirect(B("c16")[:, 0:8]), AF.Copy),
+        (R("c16"), ("Gf", wa, wb)), (R("Gs"),))
+    add("V", vt(128), lambda: V.tensor_tensor(B("p1")[:, :], B("Gs")[:, :], Kp, A.mult), (R("Gs"), PR(7)), (R("p1"),))
+
+    def fv():
+        mm(P(7)[:, 256:384], T.W37[:, :], z, True, False)
+        return mm(P(7)[:, 256:384], T.IDF[:, :], B("Gs")[:, :], False, True)
+    add("T", tt(128, 5), fv, (rz, ("W37", 0, 128), ("IDF", 0, 128), R("Gs")), (PR(7),))
+    add("V", vt(128), lambda: ts(B("pr")[:, :], B("p1")[:, :], 5, None, A.arith_shift_right), (R("p1"),), (R("pr"),))
+    add("V", vt(128), lambda: V.tensor_tensor(B("s1")[:, :], B("pr")[:, :], P(7)[:, 256:384], A.add), (R("pr"), PR(7)), (R("s1"),))
+    add("V", vt(128), lambda: ts(B("s2")[:, :], B("s1")[:, :], 4095, None, A.bitwise_and), (R("s1"),), (R("s2"),))
+    add("V", vt(128), lambda: V.tensor_copy(B("s16")[:, :], B("s2")[:, :]), (R("s2"),), (R("s16"),))
+    for hf in range(4):
+        def fx(hf=hf):
+            return S.activation(B("x")[:, 512 * hf:512 * hf + 512], T.X[:, :].indirect(B("K16")[:, 32 * hf:32 * hf + 32]), AF.Copy)
+        add("S", vt(512, GAT), fx, (R("K16"), ("X", 0, 4096)), (R("x", 512 * hf, 512 * hf + 512),))
+    add("S", vt(128, GAT), lambda: S.activation(B("Wo")[:, :], T.Wf[:, wa:wb].indirect(B("c16")[:, 0:8]), AF.Copy),
+        (R("c16"), ("Wf", wa, wb)), (R("Wo"),))
+    add("V", vt(128), lambda: V.tensor_tensor(B("dk")[:, :], B("Wo")[:, :], Kp, A.subtract), (R("Wo"), PR(7)), (R("dk"),))
+    for pc in range(4):
+        a, b = 512 * pc, 512 * pc + 512
+        yo = B("s16")[:, 32 * pc:32 * pc + 32]
+        if pc in YS:
+            bk = pc % 2
+
+            def fy(a=a, b=b, yo=yo):
+                return S.activation(B("d")[:, a:b], T.Y[:, :].indirect(yo), AF.Copy)
+            add("S", vt(512, GAT), fy, (R("s16"), ("Y", 0, 4096)), (R("d", a, b),))
+
+            def fd(a=a, b=b, bk=bk):
+                mm(P(bk)[:, 0:512], sl("NID"), B("x")[:, a:b], True, False)
+                return mm(P(bk)[:, 0:512], sl("ID"), B("d")[:, a:b], False, True)
+            add("T", tt(512, 2), fd, (R("x", a, b), R("d", a, b), rs("ID"), rs("NID")), (PR(bk),))
+            add("S", vt(512), lambda a=a, b=b, bk=bk: S.activation(B("d")[:, a:b], P(bk)[:, 0:512], AF.Abs), (PR(bk),), (R("d", a, b),))
+        else:
+            def fy(a=a, b=b, yo=yo):
+                return V.tensor_tensor(B("d")[:, a:b], T.Y[:, :].indirect(yo), B("x")[:, a:b], A.subtract)
+            add("V", vt(512, GAT), fy, (R("s16"), ("Y", 0, 4096), R("x", a, b)), (R("d", a, b),))
+
+            def fa(a=a, b=b):
+                return S.activation(B("d")[:, a:b], B("d")[:, a:b], AF.Abs)
+            add("S", vt(512), fa, (R("d", a, b),), (R("d", a, b),))
+        if pc % 2:
+            hf = pc // 2
+
+            def fD(hf=hf):
+                a, b = 1024 * hf, 1024 * hf + 1024
+                for k in range(16):
+                    i = mm(P(4)[:, 64 * hf:64 * hf + 64], T.L1[:, 128 * k:128 * k + 128], B("d")[:, a + k:b:16], k == 0, k == 15)
+                return i
+            add("T", tt(64, 16), fD, (R("d", 1024 * hf, 1024 * hf + 1024), ("L1", 0, 2048)), (PR(4),))
+    for bk in range(4):
+        pb = bk % 2
+
+        def fb(bk=bk, pb=pb):
+            mm(P(pb)[:, 0:512], sl("NID"), T.Z4[:, zb:zb + 512], True, False)
+            for j in range(4):
+                i = mm(P(pb)[:, 128 * j:128 * j + 128], sl("ID"), B("x")[:, 4 * bk + j:2048:16], False, j == 3)
+            return i
+        add("T", tt(512, 2), fb, (("Z4", zb, zb + 512), R("x"), rs("ID"), rs("NID")), (PR(pb),))
+        for j in range(2):
+            pr = 2 * bk + j
+
+            def fs(bk=pb, j=j, pr=pr):
+                return S.activation(B("sg")[:, 256 * pr:256 * pr + 256], P(bk)[:, 256 * j:256 * j + 256], AF.Sign, bias=0.5 - 16.0 * (7 - pr))
+            add("S", vt(256), fs, (PR(pb),), (R("sg", 256 * pr, 256 * pr + 256),))
+    for bk in range(4):
+        def fc(bk=bk):
+            for j in range(4):
+                k = 4 * bk + j
+                i = mm(P(5)[:, 0:128], T.L1[:, 128 * k:128 * k + 128], B("sg")[:, 128 * k:128 * k + 128], k == 0, False)
+            return i
+        add("T", tt(128, 4), fc, (R("sg", 512 * bk, 512 * bk + 512), ("L1", 0, 2048)), (PR(5),))
+    thr = 11 if first else 12
+    o, f, h = B("o")[:, :], B("f")[:, :], B("h")[:, :]
+    add("V", vt(128), lambda: ts(o, P(4)[:, 0:128], col(thr), 1024.0, A.is_ge, A.mult), (PR(4), rc(thr)), (R("o"),))
+    add("T", tt(128), lambda: mm(P(5)[:, 0:128], sl("IDm32"), o, False, True), (R("o"), rs("IDm32")), (PR(5),))
+    add("S", vt(128), lambda: S.activation(B("hd")[:, :], P(5)[:, 0:128], AF.Relu), (PR(5),), (R("hd"),))
+
+    def fE():
+        mm(P(4)[:, 128:256], sl("DE"), sl("ones"), True, False)
+        return mm(P(4)[:, 128:256], sl("SD"), o, False, True)
+    add("T", tt(128, 2), fE, (R("o"), rs("DE"), rs("SD"), rs("ones")), (PR(4),))
+    add("V", vt(128), lambda: V.tensor_tensor(B("eo")[:, :], o, P(4)[:, 128:256], A.mult), (R("o"), PR(4)), (R("eo"),))
+
+    def fF():
+        mm(P(5)[:, 128:256], sl("TGE"), B("hd")[:, :], True, False)
+        return mm(P(5)[:, 128:256], sl("IDh"), o, False, True)
+    add("T", tt(128, 2), fF, (R("o"), R("hd"), rs("TGE"), rs("IDh")), (PR(5),))
+    add("S", vt(128), lambda: S.activation(f, P(5)[:, 128:256], AF.Relu, bias=1.0, scale=-1.0, accum_out=B("Fs")[:, 0:1]),
+        (PR(5),), (R("f"), R("Fs")))
+    add("V", vt(128), lambda: V.tensor_tensor(h, P(5)[:, 128:256], o, A.is_gt), (PR(5), R("o")), (R("h"),))
+
+    def fX():
+        mm(P(4)[:, 384:512], sl("ID"), f, True, True)
+        mm(P(4)[:, 256:384], sl("DX"), sl("ones"), True, False)
+        mm(P(4)[:, 256:384], sl("SD"), o, False, False)
+        return mm(P(4)[:, 256:384], sl("NBD"), f, False, True)
+    add("T", tt(128, 4), fX, (R("o"), R("f"), rs("DX"), rs("SD"), rs("NBD"), rs("ones"), rs("ID")), (PR(4),))
+
+    def fK2():
+        return fK(P(6)[:, 256:384])
+    add("T", tt(128, 2), fK2, (rhl, rs("ID64"), rs("ID")), (PR(6),))
+    add("V", vt(128), lambda: V.tensor_tensor(B("dl")[:, :], B("dk")[:, :], P(4)[:, 384:512], A.mult), (R("dk"), PR(4)), (R("dl"),))
+    add("V", vt(128), lambda: V.tensor_tensor(B("val")[:, :], B("dl")[:, :], P(6)[:, 256:384], A.add), (R("dl"), PR(6)), (R("val"),))
+    add("S", vt(128), lambda: S.activation(B("h64")[:, :], B("val")[:, :], AF.Copy, bias=8224.5), (R("val"),), (R("h64"),))
+    add("V", vt(128), lambda: V.tensor_tensor(B("m")[:, :], h, P(4)[:, 256:384], A.mult), (R("h"), PR(4)), (R("m"),))
+
+    def fW(o_, dk, hs):
+        mm(o_, sl(dk), sl("ones"), True, False)
+        mm(o_, sl("NSLT"), o, False, False)
+        mm(o_, sl("ID16"), B("eo")[:, :], False, False)
+        return mm(o_, sl("ID64"), B("m")[:, :], False, False)
+    wr_ = (R("o"), R("eo"), R("m"), rs("ones"), rs("NSLT"), rs("ID16"), rs("ID64"), rs("DK"), rs("DKL"))
+    add("T", tt(128, 4), lambda: fW(P(5)[:, 256:384], "DK", None), wr_, (PR(5),))
+    add("T", tt(128, 4), lambda: fW(P(4)[:, 0:128], "DKL", None), wr_, (PR(4),))
+    add("T", tt(128), lambda: mm(P(5)[:, 256:384], sl("ID64t"), B("h64")[:, :], False, True), (R("h64"), rs("ID64t")), (PR(5),))
+    add("T", tt(128), lambda: mm(P(4)[:, 0:128], sl("NID"), B("h64")[:, :], False, True), (R("h64"), rs("NID")), (PR(4),))
+    add("V", vt(128), lambda: ts(B("WW")[:, 0:128], P(5)[:, 256:384], -129.0, None, A.add), (PR(5),), (R("WW", 0, 128),))
+    add("V", vt(128), lambda: V.tensor_tensor(B("WW")[:, 128:256], B("val")[:, :], P(4)[:, 0:128], A.add), (R("val"), PR(4)), (R("WW", 128, 256),))
+    if c == 1 and not last:
+        def fF2():
+            mm(P(6)[:, 384:385], T.ONE16[:, :], T.Fs0[:, 0:1], True, False)
+            return mm(P(6)[:, 384:385], T.ONE16[:, :], T.Fs1[:, 0:1], False, True)
+        add("T", tt(64, 8), fF2, (("Fs0", 0, 1), ("Fs1", 0, 1), ("ONE16", 0, 128)), (PR(6),))
+        add("V", vt(1), lambda: V.tensor_copy(T.Fi[:, 0:1], P(6)[:, 384:385]), (PR(6),), (("Fi", 0, 1),))
+        add("V", vt(1), lambda: ts(T.Fj[:, 0:1], T.Fi[:, 0:1], 511, None, A.bitwise_and), (("Fi", 0, 1),), (("Fj", 0, 1),))
+        add("V", vt(1), lambda: V.tensor_tensor(col(12), T.Fj[:, 0:1], col(11), A.add), (("Fj", 0, 1), rc(11)), (rc(12),))
+    for q in range(15):
+        def fq(q=q):
+            return ts(B("CL")[:, 256 * q:256 * q + 256], B("WW")[:, :], 64.0 * (q + 1), None, A.min)
+        add("V", vt(256, .5), fq, (R("WW"),), (R("CL", 256 * q, 256 * q + 256),))
+    add("T", tt(256), lambda: mm(P(6)[:, 0:256], T.PQ[:, 1920:2048], B("WW")[:, :], True, False), (R("WW"), ("PQ", 0, 2048)), (PR(6),))
+    for q0 in range(0, 15, 3):
+        def fp(q0=q0):
+            for q in range(q0, q0 + 3):
+                i = mm(P(6)[:, 0:256], T.PQ[:, 128 * q:128 * q + 128], B("CL")[:, 256 * q:256 * q + 256], False, q == 14)
+            return i
+        add("T", tt(256, 3), fp, (R("CL", 256 * q0, 256 * q0 + 768), ("PQ", 0, 2048)), (PR(6),))
+    add("S", vt(256), lambda: S.activation(T.HS[:, hb:hb + 256], P(6)[:, 0:256], AF.Identity, bias=col(5)), (PR(6), rc(5)), (("HS", hb, hb + 256),))
+    sh = None
+    if not last:
+        nb = 256 * (n + 2)
+
+        def sendh():
+            return g.remote_dma(out_ap=T.HL[:, nb:nb + 256], in_ap=T.HS[:, hb:hb + 256], remote_sem=T.sem["ah%d_%d" % (e + 1, c)],
+                                local_sem=T.sem.loc, pid=pid, routing_id=rid, dma_engine_mask=emask)
+        sh = add("G", 1.0, sendh, (("HS", hb, hb + 256),), (), kind="s")
+    else:
+        def fK3():
+            mm(P(7)[:, 0:128], sl("ID64"), T.HS[:, hb:hb + 128], True, False)
+            return mm(P(7)[:, 0:128], sl("ID"), T.HS[:, hb + 128:hb + 256], False, True)
+        add("T", tt(128, 2), fK3, (("HS", hb, hb + 256), rs("ID64"), rs("ID")), (PR(7),))
+        add("S", vt(128), lambda: S.activation(T.YK[:, 128 * c:128 * c + 128], P(7)[:, 0:128], AF.Copy), (PR(7),), (("YK", 128 * c, 128 * c + 128),))
+        add("Y", .1, lambda: SY.dma_start(T.yk[:, 128 * c:128 * c + 128], T.YK[:, 128 * c:128 * c + 128]), (("YK", 128 * c, 128 * c + 128),), (),
+            kind="d", sem="st%d" % c, val=16, lat=2.2)
+    add("V", vt(128, SCA), lambda: V.tensor_tensor(T.Wf[:, wa:wb].indirect(B("c16")[:, 0:8]), B("Wo")[:, :], B("dl")[:, :], A.subtract),
+        (R("Wo"), R("dl"), R("c16")), (("Wf", wa, wb),))
+    if last:
+        add("Y", .1, lambda: SY.dma_start(T.yw[:, wa:wb], T.Wf[:, wa:wb]), (("Wf", wa, wb),), (), kind="d", sem="st%d" % (2 + c), val=16, lat=2.5)
+    for bk in range(4):
+        pb = 2 + bk % 2
+
+        def fm(bk=bk, pb=pb):
+            for j in range(4):
+                k = 4 * bk + j
+                mm(P(pb)[:, 128 * j:128 * j + 128], sl("ID"), B("x")[:, k:2048:16], True, False)
+                i = mm(P(pb)[:, 128 * j:128 * j + 128], T.L2[:, 128 * k:128 * k + 128], h, False, True)
+            return i
+        add("T", tt(128, 8), fm, (R("h"), R("x"), ("L2", 0, 2048), rs("ID")), (PR(pb),))
+        for j in range(2):
+            def fM(bk=bk, j=j, pb=pb):
+                src = P(pb)[:, 256 * j:256 * j + 256]
+                if bk == 0 and j == 0:
+                    return ts(B("AC")[:, :], src, 256.0, None, A.max)
+                return V.tensor_tensor(B("AC")[:, :], B("AC")[:, :], src, A.max)
+            add("V", vt(256), fM, (PR(pb),) if bk == 0 and j == 0 else (R("AC"), PR(pb)), (R("AC"),))
+    add("V", vt(128, 2), lambda: V.tensor_tensor(B("mz")[:, :], B("AC")[:, 0:128], B("AC")[:, 128:256], A.max), (R("AC"),), (R("mz"),))
+    zs = 128 * n
+
+    def fz():
+        mm(P(2)[:, 0:128], sl("ID"), z, True, False)
+        return mm(P(2)[:, 0:128], sl("NID"), B("mz")[:, :], False, True)
+    add("T", tt(128, 2), fz, (rz, R("mz"), rs("ID"), rs("NID")), (PR(2),))
+    add("S", vt(128), lambda: S.activation(T.ZS[:, zs:zs + 128], P(2)[:, 0:128], AF.Abs, bias=256.0), (PR(2),), (("ZS", zs, zs + 128),))
+    if not last:
+        nz = 512 * (n + 2)
+
+        def sendz():
+            return g.remote_dma(out_ap=T.Z4[:, nz:nz + 128], in_ap=T.ZS[:, zs:zs + 128], remote_sem=T.sem["az%d_%d" % (e + 1, c)],
+                                local_sem=T.sem.loc, pid=pid, routing_id=rid, dma_engine_mask=emask)
+        sz = add("G", 1.0, sendz, (("ZS", zs, zs + 128),), (), kind="s")
+        _lead_sends[(e, c)] = (sh, sz)
+    else:
+        add("Y", .1, lambda: SY.dma_start(T.yz[:, 128 * c:128 * c + 128], T.ZS[:, zs:zs + 128]), (("ZS", zs, zs + 128),), (),
+            kind="d", sem="st%d" % (4 + c), val=16, lat=2.2)
+
+
+_lead_sends = {}

@@ -1,60 +1,54 @@
-import numpy as np
-from concourse.bass import DstId, RemoteDMATransfer
-from concourse.mybir import dt, AluOpType, AxisListType, ActivationFunctionType
+import math
+from concourse.mybir import AluOpType, AxisListType, ActivationFunctionType
 
 A = AluOpType
 AF = ActivationFunctionType
 LE = 6
-SLOTS = ["ones", "BD0", "BD", "ID", "ID64", "NID", "IDm32", "IDh", "TGE", "SLT", "SGT", "SD0", "SD", "NBD", "NSLT", "ID16",
-         "ID64t", "DE", "DX", "DK", "DKL"]
+V0 = 4192.0
+SLOTS = ["ones", "BD0", "BD", "ID", "NID", "ID2", "IDm16", "IDm256", "ID16k", "Cm192", "Cm96", "Cm4256", "TGE", "SLT", "SGT",
+         "SH", "SL", "TEo", "TFo", "THt", "THo", "CQ", "t0", "t1", "t2", "t3", "t4", "t5"]
 
 SCRATCH = {
     "X": ("sbuf", [128, 4096], "bfloat16"), "Y": ("sbuf", [128, 4096], "bfloat16"),
-    "Gf": ("sbuf", [128, 1024], "float32"), "Wf": ("sbuf", [128, 1024], "float32"),
+    "Gf": ("sbuf", [128, 1024], "float32"), "Wf": ("sbuf", [128, 1024], "float32"), "Wout": ("sbuf", [128, 1024], "float32"),
     "rti": ("sbuf", [128, 1024], "int32"), "wri": ("sbuf", [128, 1024], "int32"), "rki": ("sbuf", [128, 256], "int32"),
     "thi": ("sbuf", [128, 1], "int32"), "wtb": ("sbuf", [128, 1], "bfloat16"),
-    "Z4": ("sbuf", [128, 12 * 512], "bfloat16"), "HL": ("sbuf", [128, 12 * 256], "bfloat16"),
+    "ZL": ("sbuf", [128, 12 * 128], "bfloat16"), "HL": ("sbuf", [128, 12 * 256], "bfloat16"),
     "HS": ("sbuf", [128, 12 * 256], "bfloat16"), "ZS": ("sbuf", [128, 12 * 128], "bfloat16"),
     "TB": ("sbuf", [128, 128 * len(SLOTS)], "bfloat16"),
-    "IDF": ("sbuf", [128, 128], "float32"), "ONE16": ("sbuf", [128, 128], "float32"),
-    "L1": ("sbuf", [128, 2048], "bfloat16"), "L2": ("sbuf", [128, 2048], "bfloat16"),
-    "PQ": ("sbuf", [128, 2048], "bfloat16"), "WL": ("sbuf", [128, 2048], "bfloat16"),
+    "ONE16": ("sbuf", [128, 128], "float32"),
+    "Z1": ("sbuf", [128, 144], "bfloat16"), "WZ": ("sbuf", [128, 144], "bfloat16"),
+    "L2": ("sbuf", [128, 2048], "bfloat16"), "PQ": ("sbuf", [128, 1024], "bfloat16"),
     "W37": ("sbuf", [128, 128], "float16"),
-    "COL": ("sbuf", [128, 16], "float32"), "kk": ("sbuf", [128, 16], "float32"), "RK": ("sbuf", [128, 16], "float32"),
-    "rowi": ("sbuf", [128, 2], "int32"), "r15": ("sbuf", [128, 2], "int32"),
+    "COL": ("sbuf", [128, 32], "float32"), "kk": ("sbuf", [128, 16], "float32"), "RK": ("sbuf", [128, 16], "float32"),
+    "rowi": ("sbuf", [128, 4], "int32"),
     "I4a": ("sbuf", [128, 8], "int32"), "I4": ("sbuf", [128, 8], "int32"),
+    "Fs": ("sbuf", [128, 4], "float32"), "Ff": ("sbuf", [128, 1], "float32"),
     "Fi": ("sbuf", [128, 1], "int32"), "Fj": ("sbuf", [128, 1], "int32"),
     "YK": ("sbuf", [128, 256], "float32"), "hI": ("sbuf", [128, 256], "int32"), "lI": ("sbuf", [128, 256], "int32"),
+    "Z2": ("sbuf", [128, 144], "bfloat16"), "CT": ("sbuf", [128, 256], "bfloat16"),
 }
 for _c in range(2):
     for _n, _w, _d in (("K16", 128, "uint16"), ("x", 2048, "bfloat16"), ("d", 2048, "bfloat16"), ("sg", 2048, "bfloat16"),
                        ("ua", 8, "int32"), ("ub", 8, "int32"), ("uc", 8, "int32"), ("ud", 8, "int32"), ("ue", 8, "int32"),
-                       ("c16", 8, "uint16"), ("Gs", 128, "float32"), ("Wo", 128, "float32"), ("dk", 128, "float32"),
-                       ("dl", 128, "float32"), ("val", 128, "float32"), ("p1", 128, "int32"), ("pr", 128, "int32"),
-                       ("s1", 128, "int32"), ("s2", 128, "int32"), ("s16", 128, "uint16"), ("o", 128, "bfloat16"),
-                       ("hd", 128, "bfloat16"), ("eo", 128, "bfloat16"), ("f", 128, "bfloat16"), ("h", 128, "bfloat16"),
-                       ("m", 128, "bfloat16"), ("h64", 128, "bfloat16"), ("WW", 256, "float16"),
-                       ("CL", 15 * 256, "float16"), ("AC", 256, "float16"), ("mz", 128, "float16"), ("Fs", 1, "float32")):
+                       ("c16", 8, "uint16"), ("Gs", 128, "float32"), ("Wo", 128, "float32"), ("Wp", 128, "float32"),
+                       ("dk", 128, "float32"), ("dl", 128, "float32"), ("val", 128, "float32"), ("p1", 128, "int32"),
+                       ("pr", 128, "int32"), ("s1", 128, "int32"), ("s2", 128, "int32"), ("s16", 128, "uint16"),
+                       ("un", 128, "bfloat16"), ("cs", 128, "bfloat16"), ("hd", 128, "bfloat16"), ("ta", 128, "bfloat16"),
+                       ("EE", 384, "bfloat16"), ("WW", 256, "bfloat16"), ("CL", 8 * 256, "bfloat16"), ("tq", 256, "bfloat16"),
+                       ("AC", 256, "float16"), ("mz", 128, "float16")):
         SCRATCH[_n + str(_c)] = ("sbuf", [128, _w], _d)
 for _b in range(8):
     SCRATCH["ps%d" % _b] = ("psum", [128, 512], "float32")
 
-SEMAPHORES = ["eV", "eS", "eT", "eG", "loc"] + ["ld%d" % _i for _i in range(20)] + ["st%d" % _i for _i in range(8)]
-for _e in range(LE):
+SEMAPHORES = ["eV", "eS", "eT", "eG", "loc"] + ["ld%d" % _i for _i in range(12)] + ["st%d" % _i for _i in range(6)]
+for _e in range(1, LE):
     for _c in range(2):
-        SEMAPHORES += ["zr%d_%d" % (_e, _c), "ah%d_%d" % (_e, _c), "az%d_%d" % (_e, _c)]
+        SEMAPHORES += ["ah%d_%d" % (_e, _c), "az%d_%d" % (_e, _c)]
 
-CY = 0.83e-3 * 1.25
-TC = 0.42e-3 * 1.25
-GAT = 1.55
-SCA = 3.8
-YS = ()
-NOISE, SEED, WIN, BON = 0.0, 0, 0.02, 0.0
-_OFF = [
-    [15, 31, -2, -25, 55, 35, 8, 160, 63, 53, 15, 11, 25, 37, -30, 33, -3, 8, 48, 22, 15, 7, 8, 30, -5, -6, 11, 52, 2, 83, -6, 11, -5, 40, 8, -23, 61, 98, 2, 36, 32, 67, 21, 54, 23, 37, 62, 43, 47, 44, -12, -25, 18, 67, -4, 64, 35, 31, -69, 33, 9, 51, -23, 46, -6, 24, 10, 77, 36, -46, -65, 60, 31, 47, -6, 19, 2, 11, 23, 23, -11, 9, -34, -43, -11, -13, -20, 25, 21, 65, 4, 31, 1, 52, -15, 51, -57, 30, -74, -30, 44, 28, 22, 10, -43, -3, -24, 33, 14, 65, 18, 0, -13, 4],
-    [-42, -73, 42, 3, 40, 4, -27, 28, 27, -103, -24, 68, 5, 34, 66, -27, -22, -38, 24, -14, -14, -24, -21, -40, -40, 47, -2, 35, 23, -30, -84, -68, -82, -70, -72, -72, 35, -51, -108, -26, -28, -25, -65, -80, -5, -54, -111, -32, -11, -69, -6, -24, -20, 36, -80, -14, -111, 33, 50, 68, 2, 45, 26, 24, 92, 84, 105, -5, 38, -4, 16, 17, 14, 23, 6, 19, 43, 4, 9, 4, -1, 103, 6, 30, -3, -1, 23, 46, 13, -2, -28, -73, 0, -79, -50, 11, -48, -12, -13, 8, 7, 5, -16, -5, 67, -46, -49, -5, 11, 30, -48, 82, -67, -41, -64]]
-OFFS = {(_c, _i): float(_v) for _c in range(2) for _i, _v in enumerate(_OFF[_c])}
-HOP = 0.08
+PAR = {"CY": 0.83e-3 * 1.05, "TC": 0.42e-3 * 1.05, "GAT": 1.55, "SCA": 3.8, "HOP": 0.1, "REM": 3.2, "WIN": 0.02, "XV": (3,),
+       "PASS": 6, "T": 20, "S": 10, "BW": 0.2}
+_ORDER = {}
 
 
 def rank_program(g, core, T, topo):
@@ -64,251 +58,381 @@ def rank_program(g, core, T, topo):
     cores = list(T.cores)
     dst = cores[(rank + 1) % len(cores)]
     rid, pid, _s = topo.addr(dst)
-    engines = topo.engines(core, dst)
     emask = topo.mask(core, dst)
-    neng = len(engines)
-
+    neng = len(topo.engines(core, dst))
     V, S, TE, SY = g.vector, g.scalar, g.tensor, g.sync
     QS = {"V": V, "S": S, "T": TE, "G": g, "Y": SY}
-    ops, acc = [], {}
-    cur = [-1, -1, 0]
+    CY, TC = PAR["CY"], PAR["TC"]
+    ops, acc, cur = [], {}, [-1]
+
+    def ap(o):
+        if not isinstance(o, tuple):
+            return o
+        a = T[o[0]][:, o[1]:o[2]:o[3]] if o[3] != 1 else T[o[0]][:, o[1]:o[2]]
+        return a.indirect(ap(o[4])) if len(o) > 4 else a
+
+    def width(o):
+        return 16 * width(o[4]) if len(o) > 4 else len(range(o[1], o[2], o[3]))
 
     def add(q, dur, emit, R=(), W=(), kind="c", sem=None, val=0, lat=0.0, extra=()):
         i = len(ops)
-        deps = {}
-        for j in extra:
-            deps[j] = False
+        deps = {j: False for j in extra}
+        R = [o for o in R if isinstance(o, tuple)]
+        R += [o[4] for o in list(R) + list(W) if len(o) > 4]
         for isw, regs in ((False, R), (True, W)):
-            for buf, lo, hi in regs:
-                lst = acc.setdefault(buf, [])
+            for o in regs:
+                buf, lo, hi = o[0], o[1], o[2]
                 ps = buf[:2] == "ps"
                 keep = []
-                for a in lst:
+                for a in acc.get(buf, []):
                     j, l, h, aw = a
                     if j == i:
                         keep.append(a)
                         continue
-                    over = ps or (l < hi and lo < h)
+                    over = l < hi and lo < h
                     same = ops[j]["q"] == q and ops[j]["kind"] == "c" and kind == "c"
-                    if over:
-                        if ps:
-                            deps[j] = deps.get(j, False) or not same
-                        elif isw or aw:
-                            deps[j] = deps.get(j, False) or (aw if same else True)
-                    if ps and same:
-                        continue
-                    if isw and (not ps) and l >= lo and h <= hi:
-                        continue
+                    if ps:
+                        deps[j] = deps.get(j, False) or not same or (over and (aw or isw) and q != "T")
+                        if not same or q == "T" or (isw and l >= lo and h <= hi):
+                            continue
+                    else:
+                        if over and (isw or aw):
+                            deps[j] = True
+                        if isw and l >= lo and h <= hi:
+                            continue
                     keep.append(a)
                 keep.append((i, lo, hi, isw))
                 acc[buf] = keep
-        ops.append({"q": q, "dur": dur, "emit": emit, "deps": deps, "kind": kind, "sem": sem, "val": val, "lat": lat,
-                    "key": (cur[0], cur[1], i - cur[2])})
+        ops.append({"q": q, "dur": dur, "emit": emit, "deps": deps, "kind": kind, "sem": sem, "val": val, "lat": lat, "grp": cur[0]})
         return i
 
-    def vt(n, rate=1.0):
-        return 0.03 + max(64, n * rate) * CY
+    def two(o):
+        return SCRATCH[o[0]][2] in ("bfloat16", "float16", "uint16")
 
-    def tt(n, cnt=1, f=1):
-        return 0.02 + cnt * max(64, n) * TC * f
+    def cyc(out, ins, rate):
+        if len(out) > 4:
+            return 0.05 + width(out) * PAR["SCA"] * CY
+        if len(ins[0]) > 4:
+            return 0.06 + width(out) * PAR["GAT"] * CY
+        return 0.03 + max(64, width(out) * rate) * CY
+
+    def ts(out, in0, s1, op0, s2=None, op1=None):
+        def f():
+            if op1 is None:
+                return V.tensor_scalar(ap(out), ap(in0), ap(s1), None, op0)
+            return V.tensor_scalar(ap(out), ap(in0), ap(s1), ap(s2), op0, op1)
+        return add("V", cyc(out, (in0,), .5 if two(out) and two(in0) else 1), f, (in0, s1, s2), (out,))
+
+    def tt(out, a, b, op):
+        r = 1 if "ps" in (a[0][:2], b[0][:2]) else 2
+        return add("V", cyc(out, (a,), r), lambda: V.tensor_tensor(ap(out), ap(a), ap(b), op), (a, b), (out,))
+
+    def cp(out, a):
+        return add("V", cyc(out, (a,), .5 if two(out) and two(a) else 1), lambda: V.tensor_copy(ap(out), ap(a)), (a,), (out,))
+
+    def fill(out, v):
+        return add("V", cyc(out, (out,), .5 if two(out) else 1), lambda: V.memset(ap(out), v), (), (out,))
+
+    def act(out, a, fn, bias=0.0, scale=1.0, accum=None):
+        def f():
+            if accum is None:
+                return S.activation(ap(out), ap(a), fn, bias=ap(bias), scale=ap(scale))
+            return S.activation(ap(out), ap(a), fn, bias=ap(bias), scale=ap(scale), accum_out=ap(accum))
+        return add("S", cyc(out, (a,), 1), f, (a, bias, scale), (out,) if accum is None else (out, accum))
+
+    def mms(lst):
+        def f():
+            for o, l, r, a, b in lst:
+                i = TE.matmul(ap(o), ap(l), ap(r), a, b)
+            return i
+        dur = sum(max(64, width(r)) * TC * (1 if two(r) else 4) for o, l, r, a, b in lst)
+        return add("T", dur, f, [x for m in lst for x in m[1:3]], [m[0] for m in lst])
+
+    def mm(out, *terms):
+        return mms([(out, l, r, j == 0, j == len(terms) - 1) for j, (l, r) in enumerate(terms)])
 
     def sl(n):
         s = SLOTS.index(n)
-        return T.TB[:, 128 * s:128 * s + 128]
-
-    def rs(n):
-        s = SLOTS.index(n)
-        return ("TB", 128 * s, 128 * s + 128)
+        return ("TB", 128 * s, 128 * s + 128, 1)
 
     def col(i):
-        return T.COL[:, i:i + 1]
+        return ("COL", i, i + 1, 1)
 
-    def rc(i):
-        return ("COL", i, i + 1)
+    def whole(n):
+        return (n, 0, SCRATCH[n][1][1], 1)
 
-    def mm(o, l, r, a, b):
-        return TE.matmul(o, l, r, a, b)
+    clock = [0, 2.0]
 
-    def ts(out, in0, s1, s2, op0, op1=None):
-        if op1 is None:
-            return V.tensor_scalar(out, in0, s1, None, op0)
-        return V.tensor_scalar(out, in0, s1, s2, op0, op1)
+    def load(q, reg, src):
+        s = "ld%d" % clock[0]
+        clock[0] += 1
+        clock[1] += width(reg) * (2 if two(reg) else 4) * 128e-6 / PAR["BW"]
+        QS[q].dma_start(ap(reg), src).then_inc(T.sem[s], 16)
+        add("R", 0, None, (), (reg,), kind="r", sem=s, val=16, lat=clock[1])
 
-    nld = [0]
+    load("S", whole("wtb"), T.wt[:, :])
+    load("S", ("ZL", 0, 256, 1), T.z0[:, :])
+    load("Y", whole("rki"), T.rk[:, :])
+    load("Y", ("rti", 0, 512, 1), T.rt[:, 0:512])
+    load("Y", whole("X"), T.gx[:, :])
+    load("Y", ("Y", 160, 4096, 1), T.sy[:, 0:3936])
+    load("S", ("Y", 0, 160, 1), T.sy[:, 3936:4096])
+    load("S", whole("thi"), T.th[:, :])
+    load("Y", ("rti", 512, 1024, 1), T.rt[:, 512:1024])
+    load("Y", ("wri", 0, 512, 1), T.wr[:, 0:512])
+    load("Y", ("wri", 512, 1024, 1), T.wr[:, 512:1024])
 
-    def load(q, out, in_, reg, dur, lat):
-        s = "ld%d" % nld[0]
-        nld[0] += 1
-        eng = QS[q]
-        add(q, dur, lambda: eng.dma_start(out, in_), (), (reg,), kind="d", sem=s, val=16, lat=lat)
+    def sel(o, i, pat, op, base, cm):
+        add("G", .4, lambda: g.affine_select(ap(sl(o)), ap(sl(i)), pat, op, 0.0, base, cm), (sl(i),), (sl(o),))
 
-    load("Y", T.rki[:, :], T.rk[:, :], ("rki", 0, 256), 0.1, 2.2)
-    load("S", T.Z4[:, 0:128], T.z0[:, 0:128], ("Z4", 0, 128), 0.1, 2.2)
-    load("S", T.wtb[:, :], T.wt[:, :], ("wtb", 0, 1), 0.1, 2.2)
-    load("Y", T.rti[:, 0:512], T.rt[:, 0:512], ("rti", 0, 512), 0.1, 3.5)
-    load("S", T.X[:, :], T.gx[:, :], ("X", 0, 4096), 0.1, 6.5)
-    load("S", T.Z4[:, 512:640], T.z0[:, 128:256], ("Z4", 512, 640), 0.1, 6.5)
-    load("Y", T.Y[:, :], T.sy[:, :], ("Y", 0, 4096), 0.1, 9.5)
-    load("Y", T.thi[:, :], T.th[:, :], ("thi", 0, 1), 0.1, 9.5)
-    load("Y", T.wri[:, 0:512], T.wr[:, 0:512], ("wri", 0, 512), 0.1, 10.5)
-    load("Y", T.rti[:, 512:1024], T.rt[:, 512:1024], ("rti", 512, 1024), 0.1, 11.5)
-    load("Y", T.wri[:, 512:1024], T.wr[:, 512:1024], ("wri", 512, 1024), 0.1, 12.5)
-
-    add("V", vt(128, .5), lambda: V.memset(sl("ones"), 1.0), (), (rs("ones"),))
-    add("G", .4, lambda: g.iota(T.rowi[:, 0:1], [[0, 1]], 0, 1), (), (("rowi", 0, 1),))
-    add("G", .4, lambda: g.affine_select(sl("BD0"), sl("ones"), [[-16, 8], [0, 16]], A.is_ge, 0.0, 0, 1), (rs("ones"),), (rs("BD0"),))
-    add("G", .4, lambda: g.affine_select(sl("BD"), sl("BD0"), [[16, 8], [0, 16]], A.is_ge, 0.0, 15, -1), (rs("BD0"),), (rs("BD"),))
-    add("G", .4, lambda: g.affine_select(sl("ID"), sl("ones"), [[-1, 128]], A.is_equal, 0.0, 0, 1), (rs("ones"),), (rs("ID"),))
-    add("G", .2, lambda: g.iota(T.I4a[:, :], [[64, 8]], 0, 0), (), (("I4a", 0, 8),))
-    add("G", .2, lambda: g.iota(T.kk[:, :], [[1, 16]], 0, 0, allow_small_or_imprecise_dtypes=True), (), (("kk", 0, 16),))
-    add("G", .4, lambda: g.affine_select(sl("TGE"), sl("BD"), [[-1, 128]], A.is_ge, 0.0, 0, 1), (rs("BD"),), (rs("TGE"),))
-    add("V", vt(1), lambda: ts(T.r15[:, 0:1], T.rowi[:, 0:1], 15, None, A.bitwise_and), (("rowi", 0, 1),), (("r15", 0, 1),))
-    add("V", vt(1), lambda: V.tensor_copy(col(0), T.r15[:, 0:1]), (("r15", 0, 1),), (rc(0),))
+    fill(sl("ones"), 1.0)
+    add("G", .2, lambda: g.iota(T.rowi[:, 0:1], [[0, 1]], 0, 1), (), (("rowi", 0, 1, 1),))
+    sel("ID", "ones", [[-1, 128]], A.is_equal, 0, 1)
+    sel("BD0", "ones", [[-16, 8], [0, 16]], A.is_ge, 0, 1)
+    sel("BD", "BD0", [[16, 8], [0, 16]], A.is_ge, 15, -1)
+    add("G", .2, lambda: g.iota(T.I4a[:, :], [[64, 8]], 0, 0), (), (whole("I4a"),))
+    add("G", .2, lambda: g.iota(T.kk[:, :], [[1, 16]], 0, 0, allow_small_or_imprecise_dtypes=True), (), (whole("kk"),))
+    sel("TGE", "BD", [[-1, 128]], A.is_ge, 0, 1)
+    sel("SLT", "BD", [[1, 128]], A.is_ge, -1, -1)
+    sel("SGT", "BD", [[-1, 128]], A.is_ge, -1, 1)
+    sel("SH", "ones", [[1, 128]], A.is_equal, -1, -1)
+    sel("SL", "ones", [[-1, 128]], A.is_equal, -1, 1)
+    ts(("rowi", 1, 2, 1), ("rowi", 0, 1, 1), 15, A.bitwise_and)
+    ts(("rowi", 2, 3, 1), ("rowi", 0, 1, 1), 1, A.bitwise_and)
+    cp(col(0), ("rowi", 1, 2, 1))
 
     def lin(o, i, a, b):
-        add("V", vt(1), lambda: ts(col(o), col(i), float(a), float(b), A.mult, A.add), (rc(i),), (rc(o),))
-    lin(10, 0, 4, 0)
-    add("V", vt(8), lambda: ts(T.I4[:, :], T.I4a[:, :], col(10), None, A.add), (("I4a", 0, 8), rc(10)), (("I4", 0, 8),))
+        ts(col(o), col(i), float(a), A.mult, float(b), A.add)
 
     def scl(o, i, a):
-        add("S", vt(128), lambda: S.activation(sl(o), sl(i), AF.Copy, scale=float(a)), (rs(i),), (rs(o),))
-    scl("ID64", "ID", 64)
-    add("V", vt(2048, .5), lambda: V.memset(T.L1[:, :], 0.0), (), (("L1", 0, 2048),))
-
-    def cpy(buf, base, off, src):
-        a = 128 * SLOTS.index(src)
-        add("S", vt(8), lambda: S.activation(T[buf][:, base + off:base + 128:16], T.TB[:, a + off:a + 128:16], AF.Copy),
-            (rs(src),), ((buf, base + off, base + off + 113),))
+        act(sl(o), sl(i), AF.Copy, scale=a)
+    lin(10, 0, 4, 0)
+    ts(whole("I4"), whole("I4a"), col(10), A.add)
+    fill(whole("Z1"), 0.0)
+    bd = sl("BD")
+    bd8 = ("TB", bd[1], bd[2], 16)
+    cp(("Z1", 15, 143, 16), bd8)
+    ts(whole("WZ"), whole("Z1"), whole("wtb"), A.mult)
+    scl("Cm4256", "ID", -4256.0)
+    ts(col(7), whole("wtb"), 37.0, A.mult)
+    ts(col(8), col(7), 2048.0, A.is_gt, -4096.0, A.mult)
+    tt(col(9), col(7), col(8), A.add)
+    ts(whole("W37"), bd, col(9), A.mult)
+    ts(whole("hI"), whole("rki"), 4064, A.bitwise_and)
+    ts(whole("lI"), whole("rki"), 31, A.bitwise_and)
+    for c in range(2):
+        ts(("HL", 256 * c, 256 * c + 128, 1), ("hI", 128 * c, 128 * c + 128, 1), 4096.0, A.add)
+        ts(("HL", 256 * c + 128, 256 * c + 256, 1), ("lI", 128 * c, 128 * c + 128, 1), 192.0, A.add)
+    for c in range(2):
+        ts(("Gf", 512 * c, 512 * c + 512, 1), ("rti", 512 * c, 512 * c + 512, 1), -32.0, A.add)
+        ts(("Wf", 512 * c, 512 * c + 512, 1), ("wri", 512 * c, 512 * c + 512, 1), V0, A.add)
+    ts(col(11), whole("thi"), -1.0, A.mult, 0.5, A.add)
+    for n, a in (("NID", -1), ("ID2", 2), ("IDm16", -16), ("IDm256", -256), ("ID16k", 16384), ("Cm192", -192), ("Cm96", -96)):
+        scl(n, "ID", float(a))
+    for n, t, a, tri, b in (("TEo", "t0", 128, "SGT", -3.5), ("TFo", "t1", -256, "SLT", -3.5), ("THt", "t2", 256, "SGT", 7.0),
+                            ("THo", "t3", 128, "SGT", 3.5)):
+        scl(t, tri, b)
+        scl(n, "ID", float(a))
+        tt(sl(n), sl(n), sl(t), A.add)
+    ln2 = math.log(2.0)
+    lin(1, 0, 3.5 * ln2, (105 - 52.5 - 57 - 128) * ln2)
+    lin(2, 0, 3.5 * ln2, (-56 - 256) * ln2)
+    lin(3, 0, -3.5 * ln2, (52.5 - 57 - 128) * ln2)
+    ts(col(13), ("rowi", 2, 3, 1), -1.0, A.mult, 1.0, A.add)
+    cp(col(20), ("rowi", 2, 3, 1))
+    lin(14, 0, 2 ** 20, -15 * 2 ** 20)
+    ts(col(14), col(14), col(20), A.mult)
+    ts(col(15), col(0), 14.0, A.is_lt, col(20), A.mult)
+    lin(16, 0, -64, -64)
+    ts(col(15), col(15), col(16), A.mult)
+    ts(col(16), col(13), 4128.0, A.mult)
+    scl("CQ", "ID", col(16))
+    scl("t4", "SH", col(15))
+    scl("t5", "SL", col(14))
+    tt(sl("CQ"), sl("CQ"), sl("t4"), A.add)
+    tt(sl("CQ"), sl("CQ"), sl("t5"), A.add)
+    fill(("CT", 0, 128, 1), 1.0)
+    ts(("CT", 128, 256, 1), sl("ones"), col(13), A.add)
+    lin(17, 0, 8191.5, .5 - 8192 * 15)
+    for o, top, low in ((4, -15.75, 6144.0), (5, 64 - .9765625, 189.0)):
+        ts(col(18 + o - 4), col(17), top - low, A.add)
+        ts(col(o), col(18 + o - 4), col(20), A.mult, low, A.add)
+    ts(col(6), col(20), 2.0 ** 23 + 1, A.mult, -1.0, A.add)
+    fill(whole("Z2"), 0.0)
+    cp(("Z2", 15, 143, 16), bd8)
+    ts(("Z2", 16, 144, 16), bd8, 2.0 ** -30, A.mult)
+    fill(whole("ONE16"), -16.0)
+    ts(whole("RK"), whole("kk"), col(0), A.is_equal, 256.0, A.mult)
     for k in range(16):
-        cpy("L1", 128 * k, k, "BD")
-    add("V", vt(2048, .5), lambda: ts(T.WL[:, :], T.L1[:, :], T.wtb[:, 0:1], None, A.mult), (("L1", 0, 2048), ("wtb", 0, 1)), (("WL", 0, 2048),))
-    add("V", vt(1), lambda: ts(col(7), T.wtb[:, 0:1], 37.0, None, A.mult), (("wtb", 0, 1),), (rc(7),))
-    add("V", vt(1), lambda: ts(col(8), col(7), 2048.0, -4096.0, A.is_gt, A.mult), (rc(7),), (rc(8),))
-    add("V", vt(1), lambda: V.tensor_tensor(col(9), col(7), col(8), A.add), (rc(7), rc(8)), (rc(9),))
-    add("V", vt(128, .5), lambda: ts(T.W37[:, :], sl("BD"), col(9), None, A.mult), (rs("BD"), rc(9)), (("W37", 0, 128),))
-    add("V", vt(128), lambda: V.tensor_copy(T.IDF[:, :], sl("ID")), (rs("ID"),), (("IDF", 0, 128),))
+        o = ("L2", 128 * k, 128 * k + 128, 1)
+        if k % 2:
+            act(o, bd, AF.Copy, scale=("RK", k, k + 1, 1))
+        else:
+            ts(o, bd, ("RK", k, k + 1, 1), A.mult)
+    for a in range(8):
+        ts(("PQ", 128 * a, 128 * a + 128, 1), ("Z2", 15 - 2 * a, 143 - 2 * a, 1), 2.0 ** (56 - 14 * a), A.mult)
 
-    def hl0(c):
-        a, b = 128 * c, 128 * c + 128
-        add("V", vt(128), lambda: ts(T.hI[:, a:b], T.rki[:, a:b], 6, None, A.arith_shift_right), (("rki", 0, 256),), (("hI", a, b),))
-        add("V", vt(128), lambda: ts(T.lI[:, a:b], T.rki[:, a:b], 63, None, A.bitwise_and), (("rki", 0, 256),), (("lI", a, b),))
-        add("V", vt(128), lambda: V.tensor_copy(T.HL[:, 256 * c:256 * c + 128], T.hI[:, a:b]), (("hI", a, b),), (("HL", 256 * c, 256 * c + 128),))
-        add("V", vt(128), lambda: V.tensor_copy(T.HL[:, 256 * c + 128:256 * c + 256], T.lI[:, a:b]), (("lI", a, b),), (("HL", 256 * c + 128, 256 * c + 256),))
-    hl0(0)
-    hl0(1)
+    def row(buf, k):
+        return (buf, 15 - k, 143 - k, 1)
 
-    def conv(dst_, src, c):
-        a, b = 512 * c, 512 * c + 512
-        add("V", vt(512), lambda: V.tensor_copy(T[dst_][:, a:b], T[src][:, a:b]), ((src, a, b),), ((dst_, a, b),))
-    conv("Gf", "rti", 0)
-    conv("Wf", "wri", 0)
-    conv("Gf", "rti", 1)
-    conv("Wf", "wri", 1)
-    add("V", vt(1), lambda: V.tensor_copy(col(11), T.thi[:, 0:1]), (("thi", 0, 1),), (rc(11),))
-    lin(1, 0, -1, 15)
-    lin(2, 0, -2, 15)
-    lin(3, 0, 64, 0)
-    lin(4, 0, 64, 8256)
-    lin(5, 0, 64, -960)
-    scl("NID", "ID", -1)
-    scl("IDm32", "ID", -1 / 32)
-    scl("IDh", "ID", 0.5)
-    scl("ID16", "ID", 1 / 16)
-    scl("ID64t", "ID", 1 / 64)
-    scl("NBD", "BD", -1)
-    add("G", .4, lambda: g.affine_select(sl("SLT"), sl("BD"), [[1, 128]], A.is_ge, 0.0, -1, -1), (rs("BD"),), (rs("SLT"),))
-    add("G", .4, lambda: g.affine_select(sl("SGT"), sl("BD"), [[-1, 128]], A.is_ge, 0.0, -1, 1), (rs("BD"),), (rs("SGT"),))
-    add("V", vt(128, 2), lambda: V.tensor_tensor(sl("SD0"), sl("SLT"), sl("SGT"), A.subtract), (rs("SLT"), rs("SGT")), (rs("SD0"),))
-    scl("SD", "SD0", 1 / 1024)
-    scl("NSLT", "SLT", -1 / 16)
-    for nm, ci in (("DE", 1), ("DX", 2), ("DK", 3), ("DKL", 4)):
-        def dg(nm=nm, ci=ci):
-            add("S", vt(128), lambda: S.activation(sl(nm), sl("ID"), AF.Copy, scale=col(ci)), (rs("ID"), rc(ci)), (rs(nm),))
-        dg()
-    add("V", vt(128), lambda: V.memset(T.ONE16[:, :], 16.0), (), (("ONE16", 0, 128),))
-    add("V", vt(16), lambda: ts(T.RK[:, :], T.kk[:, :], col(0), 256.0, A.is_equal, A.mult), (("kk", 0, 16), rc(0)), (("RK", 0, 16),))
-    for k in range(16):
-        def l2(k=k):
-            add("S", vt(128), lambda: S.activation(T.L2[:, 128 * k:128 * k + 128], sl("BD"), AF.Copy, scale=T.RK[:, k:k + 1]),
-                (rs("BD"), ("RK", 0, 16)), (("L2", 128 * k, 128 * k + 128),))
-        l2()
-    add("V", vt(2048, .5), lambda: V.memset(T.PQ[:, :], 0.0), (), (("PQ", 0, 2048),))
-    for k in range(16):
-        cpy("PQ", 128 * k, k, "BD")
-        if k < 15:
-            cpy("PQ", 128 * k, k + 1, "NBD")
+    sends = {}
+
+    def lead(e, c):
+        first, last = e == 0, e == LE - 1
+        n = 2 * e + c
+
+        def B(nm, a=0, b=None, st=1):
+            return (nm + str(c), a, SCRATCH[nm + str(c)][1][1] if b is None else b, st)
+
+        def P(b, j, w=128, st=1):
+            return ("ps%d" % b, 128 * j, 128 * j + w, st)
+        pa, pb = 4 + 2 * c, 5 + 2 * c
+        z = ("ZL", 128 * n, 128 * n + 128, 1)
+        hi, lo = ("HL", 256 * n, 256 * n + 128, 1), ("HL", 256 * n + 128, 256 * n + 256, 1)
+        if not first:
+            sh, sz = sends[(e - 1, c)]
+            add("R", 0, None, (), (("HL", hi[1], lo[2], 1),), kind="r", sem="ah%d_%d" % (e, c), val=neng, lat=PAR["REM"], extra=(sh,))
+            add("R", 0, None, (), (z,), kind="r", sem="az%d_%d" % (e, c), val=neng, lat=PAR["REM"], extra=(sz,))
+        kt = ((sl("ID"), hi), (sl("ID"), lo))
+        Kp, up = P(pa, 0), P(pb, 0, 8)
+        mm(Kp, (sl("Cm4256"), sl("ones")), *kt)
+        ts(B("K16"), Kp, -32.0, A.add)
+        mm(up, *[(row("WZ", r), ("ZL", z[1] + r, z[2], 16)) for r in range(16)])
+        cp(B("ua"), up)
+        ts(B("ub"), B("ua"), 63, A.bitwise_and)
+        tt(B("uc"), B("ub"), B("ub"), A.mult)
+        ts(B("ud"), B("uc"), 5, A.arith_shift_right, 3, A.bitwise_and)
+        tt(B("ue"), B("ud"), whole("I4"), A.add)
+        cp(B("c16"), B("ue"))
+        wa, wb = 512 * c, 512 * c + 512
+        act(B("Gs"), ("Gf", wa, wb, 1, B("c16")), AF.Copy)
+        mm(P(pb, 1), (whole("W37"), z), *kt)
+        mm(P(pb, 2), (sl("Cm96"), sl("ones")), *kt)
+        tt(B("p1"), B("Gs"), Kp, A.mult)
+        ts(B("pr"), B("p1"), 5, A.arith_shift_right)
+        tt(B("s1"), B("pr"), P(pb, 1), A.add)
+        ts(B("s2"), B("s1"), 4095, A.bitwise_and)
+        cp(B("s16"), B("s2"))
+        for j in range(4):
+            o, w = B("x", 512 * j, 512 * j + 512), ("X", 0, 4096, 1, B("K16", 32 * j, 32 * j + 32))
+            if j in PAR["XV"]:
+                cp(o, w)
+            else:
+                act(o, w, AF.Copy)
+        act(B("Wo"), ("Wf", wa, wb, 1, B("c16")), AF.Copy)
+        tt(B("dk"), B("Wo"), P(pb, 2), A.subtract)
+        if last:
+            act(("Wout", wa, wb, 1), ("Wf", wa, wb, 1), AF.Copy, bias=-V0)
+            act(B("Wp"), B("Wo"), AF.Copy, bias=-V0)
+        for j in range(4):
+            o = B("d", 512 * j, 512 * j + 512)
+            tt(o, ("Y", 0, 4096, 1, B("s16", 32 * j, 32 * j + 32)), B("x", 512 * j, 512 * j + 512), A.subtract)
+            act(o, o, AF.Abs)
+            if j % 2:
+                a = 512 * j - 512
+                mm(("ps%d" % pb, 384 + a // 16, 448 + a // 16, 1), *[(row("Z1", k), B("d", a + k, a + 1024, 16)) for k in range(16)])
+        for j in range(4):
+            for k in range(4 * j, 4 * j + 4, 2):
+                mms([m for k2 in (k, k + 1) for m in ((P(j % 2, k2 % 4), sl("NID"), z, True, False),
+                                                      (P(j % 2, k2 % 4), sl("ID"), B("x", k2, 2048, 16), False, True))])
+            for k in range(4 * j, 4 * j + 4, 2):
+                act(B("sg", 128 * k, 128 * k + 256), P(j % 2, k % 4, 256), AF.Sign, bias=0.5 - 16.0 * (7 - k // 2))
+            mms([(("ps%d" % pa, 128 + k, 256, 16), B("sg", 128 * k, 128 * k + 128), bd8, True, True) for k in range(4 * j, 4 * j + 4)])
+        act(B("cs"), P(pa, 1), AF.Sign, bias=-1.0)
+        un, ta = B("un"), B("ta")
+        act(un, P(pb, 3), AF.Sign, bias=col(11 if first else 12), accum=("Fs", 2 * c, 2 * c + 1, 1))
+        mm(P(pa, 2), (B("cs"), sl("ID")), (sl("NID"), un))
+        act(B("hd"), P(pa, 2), AF.Relu, bias=-1.0)
+        mm(P(pb, 0), (sl("TEo"), un))
+        act(B("EE", 0, 128), P(pb, 0), AF.Exp, bias=col(1), scale=ln2)
+        mm(P(pa, 3), (sl("IDm16"), un), (sl("TGE"), B("hd")))
+        act(ta, P(pa, 3), AF.Sign, bias=-16.0, accum=("Fs", 2 * c + 1, 2 * c + 2, 1))
+        mm(P(pa, 0), (sl("TFo"), un), (sl("IDm256"), ta))
+        mm(P(pa, 1), (sl("THo"), un), (sl("THt"), ta))
+        mm(P(pb, 1), (sl("Cm192"), sl("ones")), (sl("ID2"), hi), (sl("ID2"), lo), (sl("ID16k"), un), (sl("ID16k"), ta))
+        mm(P(pb, 2), (sl("NID"), un), (sl("NID"), ta))
+        act(B("EE", 128, 256), P(pa, 0), AF.Exp, bias=col(2), scale=ln2)
+        act(B("EE", 256, 384), P(pa, 1), AF.Exp, bias=col(3), scale=ln2)
+        tt(B("val"), B("Wo"), P(pb, 1), A.max)
+        mm(P(pa, 2), *[(sl("ID"), B("EE", 128 * j, 128 * j + 128)) for j in range(3)])
+        tt(P(pa, 3), B("val"), P(pa, 2), A.mult)
+        ts(B("WW", 0, 128), P(pa, 3), 0.98, A.mult)
+        tt(B("WW", 128, 256), P(pa, 3), B("WW", 0, 128), A.subtract)
+        tt(B("dl"), B("dk"), P(pb, 2), A.mult)
+        if c == 1 and not last:
+            fp = ("ps%d" % pb, 0, 4, 1)
+            mm(fp, (whole("ONE16"), whole("Fs")))
+            add("V", .1, lambda: V.tensor_reduce(ap(whole("Ff")), ap(fp), AxisListType.X, A.add), (fp,), (whole("Ff"),))
+            cp(whole("Fi"), whole("Ff"))
+            ts(whole("Fj"), whole("Fi"), 511, A.bitwise_and)
+            ts(col(12), whole("Fj"), -1.0, A.mult, col(11), A.add)
+        R1 = P(pa, 0, 256)
+        for a in range(8):
+            u = 2.0 ** (14 * a - 56)
+            ts(B("CL", 256 * a, 256 * a + 256), B("WW"), 64 * u, A.max, u * 2 ** 20, A.min)
+            if a % 2:
+                mms(([(R1, sl("CQ"), whole("CT"), True, False)] if a == 1 else []) +
+                    [(R1, ("PQ", 128 * b, 128 * b + 128, 1), B("CL", 256 * b, 256 * b + 256), False, b == 7) for b in (a - 1, a)])
+        act(B("tq", 0, 128), P(pa, 0), AF.Identity, bias=col(4), scale=col(6))
+        act(B("tq", 128, 256), P(pa, 1), AF.Identity, bias=col(5), scale=col(6))
+        nh, nl = ("HS", hi[1], hi[2], 1), ("HS", lo[1], lo[2], 1)
+        tt(("HS", hi[1], lo[2], 1), B("tq"), R1, A.add)
+
+        def send(src, to, sem):
+            return add("G", 0.6, lambda: g.remote_dma(out_ap=ap(to), in_ap=ap(src), remote_sem=T.sem[sem], local_sem=T.sem.loc,
+                                                      pid=pid, routing_id=rid, dma_engine_mask=emask), (src,), (), kind="s")
+
+        def store(out, src, s):
+            add("Y", .1, lambda: SY.dma_start(out, ap(src)), (src,), (), kind="d", sem="st%d" % s, val=16, lat=2.3)
+        if not last:
+            sh = send(("HS", hi[1], lo[2], 1), ("HL", hi[1] + 512, lo[2] + 512, 1), "ah%d_%d" % (e + 1, c))
+        else:
+            mm(P(pa, 2), (sl("ID"), nh), (sl("ID"), nl))
+            act(("YK", 128 * c, 128 * c + 128, 1), P(pa, 2), AF.Copy, bias=-96 - V0)
+            store(T.yk[:, 128 * c:128 * c + 128], ("YK", 128 * c, 128 * c + 128, 1), c)
+        if not last:
+            tt(("Wf", wa, wb, 1, B("c16")), B("Wo"), B("dl"), A.subtract)
+        else:
+            tt(("Wout", wa, wb, 1, B("c16")), B("Wp"), B("dl"), A.subtract)
+            store(T.yw[:, wa:wb], ("Wout", wa, wb, 1), 2 + c)
+        for j in range(4):
+            b = 2 + j % 2
+            for k in range(4 * j, 4 * j + 4, 2):
+                mms([m for k2 in (k, k + 1) for m in ((P(b, k2 % 4), sl("ID"), B("x", k2, 2048, 16), True, False),
+                                                      (P(b, k2 % 4), ("L2", 128 * k2, 128 * k2 + 128, 1), ta, False, True))])
+            for h in range(2):
+                if j == 0 and h == 0:
+                    ts(B("AC"), P(b, 0, 256), 256.0, A.max)
+                else:
+                    tt(B("AC"), B("AC"), P(b, 2 * h, 256), A.max)
+        tt(B("mz"), B("AC", 0, 128), B("AC", 128, 256), A.max)
+        mm(P(pb, 3), (sl("ID"), z), (sl("NID"), B("mz")))
+        nz = ("ZS", z[1], z[2], 1)
+        act(nz, P(pb, 3), AF.Abs, bias=256.0)
+        if not last:
+            sends[(e, c)] = (sh, send(nz, ("ZL", z[1] + 256, z[2] + 256, 1), "az%d_%d" % (e + 1, c)))
+        else:
+            store(T.yz[:, 128 * c:128 * c + 128], nz, 4 + c)
 
     for e in range(LE):
         for c in range(2):
-            cur[0], cur[1], cur[2] = e, c, len(ops) + (0 if e else -2)
-            _lead(e, c, T, g, V, S, TE, SY, add, vt, tt, sl, rs, col, rc, mm, ts, rid, pid, emask, neng, ops)
+            cur[0] = 2 * e + c
+            lead(e, c)
 
-    n = len(ops)
-    succ = [[] for _ in range(n)]
-    cnt = [0] * n
-    for i, o in enumerate(ops):
-        for j in o["deps"]:
-            succ[j].append(i)
-        cnt[i] = len(o["deps"])
-    tail = [0.0] * n
-    for i in range(n - 1, -1, -1):
-        o = ops[i]
-        tail[i] = o["dur"] + o["lat"] + max([tail[k] + HOP for k in succ[i]] + [0.0])
-    rng = np.random.RandomState(SEED)
-    for i in range(n):
-        tail[i] = tail[i] + NOISE * float(rng.rand()) + (OFFS.get(ops[i]["key"][1:], 0.0) if ops[i]["key"][0] >= 0 else 0.0)
-    free = {}
-    ready = [0.0] * n
-    cand = {}
-    for i in range(n):
-        if cnt[i] == 0:
-            cand.setdefault(ops[i]["q"], []).append(i)
-    order = []
-    while True:
-        best = None
-        for q, lst in cand.items():
-            if not lst:
-                continue
-            fq = free.get(q, 0.0)
-            st = min(max(fq, ready[i]) for i in lst)
-            pick = max((i for i in lst if max(fq, ready[i]) <= st + WIN), key=lambda i: (tail[i], -i))
-            if best is None or st < best[0]:
-                best = (st, q, pick)
-        if best is None:
-            break
-        _st, q, i = best
-        cand[q].remove(i)
-        start = max(free.get(q, 0.0), ready[i])
-        if ops[i]["kind"] == "r":
-            end = start
-        else:
-            end = start + ops[i]["dur"]
-            free[q] = end
-        end += ops[i]["lat"]
-        order.append(i)
-        for k in succ[i]:
-            inorder = ops[k]["q"] == q and not ops[k]["deps"][i]
-            ready[k] = max(ready[k], end if inorder else end + HOP)
-            cnt[k] -= 1
-            if cnt[k] == 0:
-                cand.setdefault(ops[k]["q"], []).append(k)
-    if len(order) != n:
-        raise ValueError("cycle")
-
+    if "o" not in _ORDER:
+        _ORDER["o"] = schedule(ops)
     count = {"V": 0, "S": 0, "T": 0, "G": 0}
-    known = {q: {} for q in ("V", "S", "T", "G", "Y")}
+    known = {q: {} for q in QS}
     nsend = 0
-    for i in order:
+    for i in _ORDER["o"]:
         o = ops[i]
         q = o["q"]
         if o["kind"] == "r":
             o["clk"] = {o["sem"]: o["val"]}
             continue
         kn = known[q]
-        for j in sorted((j for j, w in o["deps"].items() if w), key=lambda j: -order.index(j) if False else -j):
+        for j in sorted((j for j, w in o["deps"].items() if w), reverse=True):
             p = ops[j]
-            if p["kind"] == "s":
-                raise ValueError("nothing waits for a send")
             sem, val = (p["sem"], p["val"]) if p["kind"] != "c" else ("e" + p["q"], p["pos"])
             if kn.get(sem, 0) < val:
                 QS[q].wait_ge(T.sem[sem], val)
@@ -323,8 +447,7 @@ def rank_program(g, core, T, topo):
             ins.then_inc(T.sem["e" + q], 1)
             clk["e" + q] = count[q]
         elif o["kind"] == "d":
-            if ins is not None:
-                ins.then_inc(T.sem[o["sem"]], 16)
+            ins.then_inc(T.sem[o["sem"]], 16)
             clk[o["sem"]] = o["val"]
         else:
             nsend += 1
@@ -333,251 +456,65 @@ def rank_program(g, core, T, topo):
     for q in ("V", "S", "T", "G"):
         SY.wait_ge(T.sem["e" + q], count[q])
     for o in ops:
-        if o["kind"] in ("d", "r"):
-            if kn.get(o["sem"], 0) < o["val"]:
-                SY.wait_ge(T.sem[o["sem"]], o["val"])
-                kn[o["sem"]] = o["val"]
+        if o["kind"] in ("d", "r") and kn.get(o["sem"], 0) < o["val"]:
+            SY.wait_ge(T.sem[o["sem"]], o["val"])
+            kn[o["sem"]] = o["val"]
     g.wait_ge(T.sem.loc, neng * nsend)
 
 
-def _lead(e, c, T, g, V, S, TE, SY, add, vt, tt, sl, rs, col, rc, mm, ts, rid, pid, emask, neng, ops):
-    first, last = e == 0, e == LE - 1
-    n = 2 * e + c
-    B = lambda nm: T[nm + str(c)]
-    R = lambda nm, a=0, b=None: (nm + str(c), a, b if b is not None else SCRATCH[nm + str(c)][1][1])
-    P = lambda b: T["ps%d" % b]
-    PR = lambda b: ("ps%d" % b, 0, 512)
-    zb, hb = 512 * n, 256 * n
-    z = T.Z4[:, zb:zb + 128]
-    hi, lo = T.HL[:, hb:hb + 128], T.HL[:, hb + 128:hb + 256]
-    rz, rhl = ("Z4", zb, zb + 128), ("HL", hb, hb + 256)
-    if not first:
-        sh, sz = _lead_sends[(e - 1, c)]
-        add("R", 0, None, (), (rhl,), kind="r", sem="ah%d_%d" % (e, c), val=neng, lat=3.0, extra=(sh,))
-        add("R", 0, None, (), (rz,), kind="r", sem="az%d_%d" % (e, c), val=neng, lat=3.0, extra=(sz,))
+def schedule(ops):
+    n, HOP = len(ops), PAR["HOP"]
+    pred = [[(j, HOP if w or ops[j]["q"] != o["q"] else 0.0) for j, w in o["deps"].items()] for o in ops]
+    succ = [[] for _ in range(n)]
+    for i in range(n):
+        for j, h in pred[i]:
+            succ[j].append((i, h))
 
-    def zrep():
-        s = T.sem["zr%d_%d" % (e, c)]
-        for j in range(1, 4):
-            SY.dma_start(T.Z4[:, zb + 128 * j:zb + 128 * j + 128], z).then_inc(s, 16)
-        return None
-    add("Y", 0.3, zrep, (rz,), (("Z4", zb + 128, zb + 512),), kind="d", sem="zr%d_%d" % (e, c), val=48, lat=2.2)
+    def run(nxt, prv, prio, back):
+        cnt = [len(p) for p in prv]
+        ready, free, cand, start, order = [0.0] * n, {}, {}, [0.0] * n, []
+        for i in range(n):
+            if cnt[i] == 0:
+                ready[i] = ops[i]["lat"] if back else 0.0
+                cand.setdefault(ops[i]["q"], []).append(i)
+        end_all = 0.0
+        while len(order) < n:
+            best = None
+            for q, lst in cand.items():
+                if lst:
+                    st = max(free.get(q, 0.0), min(ready[i] for i in lst))
+                    if best is None or st < best[0]:
+                        best = (st, q)
+            st, q = best
+            i = max((i for i in cand[q] if ready[i] <= st + PAR["WIN"]), key=lambda i: (prio[i], -i))
+            cand[q].remove(i)
+            start[i] = max(free.get(q, 0.0), ready[i])
+            end = start[i] + ops[i]["dur"]
+            if q != "R":
+                free[q] = end
+            if not back:
+                end += ops[i]["lat"]
+            end_all = max(end_all, end)
+            order.append(i)
+            for k, h in nxt[i]:
+                ready[k] = max(ready[k], end + h + (ops[k]["lat"] if back else 0.0))
+                cnt[k] -= 1
+                if cnt[k] == 0:
+                    cand.setdefault(ops[k]["q"], []).append(k)
+        return end_all, order, [start[i] + ops[i]["dur"] for i in range(n)]
 
-    def fK(o):
-        mm(o, sl("ID64"), hi, True, False)
-        return mm(o, sl("ID"), lo, False, True)
-    Kp = P(7)[:, 0:128]
-    add("T", tt(128, 2), lambda: fK(Kp), (rhl, rs("ID64"), rs("ID")), (PR(7),))
-    add("V", vt(128), lambda: V.tensor_copy(B("K16")[:, :], Kp), (PR(7),), (R("K16"),))
-
-    def fU():
-        for r in range(16):
-            i = mm(P(7)[:, 128:136], T.WL[:, 128 * r:128 * r + 128], T.Z4[:, zb + r:zb + 128:16], r == 0, r == 15)
-        return i
-    add("T", tt(8, 16), fU, (rz, ("WL", 0, 2048)), (PR(7),))
-    add("V", vt(8), lambda: V.tensor_copy(B("ua")[:, :], P(7)[:, 128:136]), (PR(7),), (R("ua"),))
-    add("V", vt(8), lambda: ts(B("ub")[:, :], B("ua")[:, :], 63, None, A.bitwise_and), (R("ua"),), (R("ub"),))
-    add("V", vt(8), lambda: V.tensor_tensor(B("uc")[:, :], B("ub")[:, :], B("ub")[:, :], A.mult), (R("ub"),), (R("uc"),))
-    add("V", vt(8), lambda: ts(B("ud")[:, :], B("uc")[:, :], 5, 3, A.arith_shift_right, A.bitwise_and), (R("uc"),), (R("ud"),))
-    add("V", vt(8), lambda: V.tensor_tensor(B("ue")[:, :], B("ud")[:, :], T.I4[:, :], A.add), (R("ud"), ("I4", 0, 8)), (R("ue"),))
-    add("V", vt(8), lambda: V.tensor_copy(B("c16")[:, :], B("ue")[:, :]), (R("ue"),), (R("c16"),))
-    wa, wb = 512 * c, 512 * c + 512
-    add("S", vt(128, GAT), lambda: S.activation(B("Gs")[:, :], T.Gf[:, wa:wb].indirect(B("c16")[:, 0:8]), AF.Copy),
-        (R("c16"), ("Gf", wa, wb)), (R("Gs"),))
-    add("V", vt(128), lambda: V.tensor_tensor(B("p1")[:, :], B("Gs")[:, :], Kp, A.mult), (R("Gs"), PR(7)), (R("p1"),))
-
-    def fv():
-        mm(P(7)[:, 256:384], T.W37[:, :], z, True, False)
-        return mm(P(7)[:, 256:384], T.IDF[:, :], B("Gs")[:, :], False, True)
-    add("T", tt(128, 5), fv, (rz, ("W37", 0, 128), ("IDF", 0, 128), R("Gs")), (PR(7),))
-    add("V", vt(128), lambda: ts(B("pr")[:, :], B("p1")[:, :], 5, None, A.arith_shift_right), (R("p1"),), (R("pr"),))
-    add("V", vt(128), lambda: V.tensor_tensor(B("s1")[:, :], B("pr")[:, :], P(7)[:, 256:384], A.add), (R("pr"), PR(7)), (R("s1"),))
-    add("V", vt(128), lambda: ts(B("s2")[:, :], B("s1")[:, :], 4095, None, A.bitwise_and), (R("s1"),), (R("s2"),))
-    add("V", vt(128), lambda: V.tensor_copy(B("s16")[:, :], B("s2")[:, :]), (R("s2"),), (R("s16"),))
-    for hf in range(4):
-        def fx(hf=hf):
-            return S.activation(B("x")[:, 512 * hf:512 * hf + 512], T.X[:, :].indirect(B("K16")[:, 32 * hf:32 * hf + 32]), AF.Copy)
-        add("S", vt(512, GAT), fx, (R("K16"), ("X", 0, 4096)), (R("x", 512 * hf, 512 * hf + 512),))
-    add("S", vt(128, GAT), lambda: S.activation(B("Wo")[:, :], T.Wf[:, wa:wb].indirect(B("c16")[:, 0:8]), AF.Copy),
-        (R("c16"), ("Wf", wa, wb)), (R("Wo"),))
-    add("V", vt(128), lambda: V.tensor_tensor(B("dk")[:, :], B("Wo")[:, :], Kp, A.subtract), (R("Wo"), PR(7)), (R("dk"),))
-    for pc in range(4):
-        a, b = 512 * pc, 512 * pc + 512
-        yo = B("s16")[:, 32 * pc:32 * pc + 32]
-        if pc in YS:
-            bk = pc % 2
-
-            def fy(a=a, b=b, yo=yo):
-                return S.activation(B("d")[:, a:b], T.Y[:, :].indirect(yo), AF.Copy)
-            add("S", vt(512, GAT), fy, (R("s16"), ("Y", 0, 4096)), (R("d", a, b),))
-
-            def fd(a=a, b=b, bk=bk):
-                mm(P(bk)[:, 0:512], sl("NID"), B("x")[:, a:b], True, False)
-                return mm(P(bk)[:, 0:512], sl("ID"), B("d")[:, a:b], False, True)
-            add("T", tt(512, 2), fd, (R("x", a, b), R("d", a, b), rs("ID"), rs("NID")), (PR(bk),))
-            add("S", vt(512), lambda a=a, b=b, bk=bk: S.activation(B("d")[:, a:b], P(bk)[:, 0:512], AF.Abs), (PR(bk),), (R("d", a, b),))
+    loc, prio = [0.0] * n, [0.0] * n
+    for i in range(n - 1, -1, -1):
+        gp, d = ops[i]["grp"], ops[i]["dur"] + ops[i]["lat"]
+        loc[i] = d + max([loc[k] + h for k, h in succ[i] if ops[k]["grp"] == gp] + [0.0])
+        if gp >= 0:
+            prio[i] = loc[i] - (gp // 2) * PAR["T"] - (gp % 2) * PAR["S"]
         else:
-            def fy(a=a, b=b, yo=yo):
-                return V.tensor_tensor(B("d")[:, a:b], T.Y[:, :].indirect(yo), B("x")[:, a:b], A.subtract)
-            add("V", vt(512, GAT), fy, (R("s16"), ("Y", 0, 4096), R("x", a, b)), (R("d", a, b),))
-
-            def fa(a=a, b=b):
-                return S.activation(B("d")[:, a:b], B("d")[:, a:b], AF.Abs)
-            add("S", vt(512), fa, (R("d", a, b),), (R("d", a, b),))
-        if pc % 2:
-            hf = pc // 2
-
-            def fD(hf=hf):
-                a, b = 1024 * hf, 1024 * hf + 1024
-                for k in range(16):
-                    i = mm(P(4)[:, 64 * hf:64 * hf + 64], T.L1[:, 128 * k:128 * k + 128], B("d")[:, a + k:b:16], k == 0, k == 15)
-                return i
-            add("T", tt(64, 16), fD, (R("d", 1024 * hf, 1024 * hf + 1024), ("L1", 0, 2048)), (PR(4),))
-    for bk in range(4):
-        pb = bk % 2
-
-        def fb(bk=bk, pb=pb):
-            mm(P(pb)[:, 0:512], sl("NID"), T.Z4[:, zb:zb + 512], True, False)
-            for j in range(4):
-                i = mm(P(pb)[:, 128 * j:128 * j + 128], sl("ID"), B("x")[:, 4 * bk + j:2048:16], False, j == 3)
-            return i
-        add("T", tt(512, 2), fb, (("Z4", zb, zb + 512), R("x"), rs("ID"), rs("NID")), (PR(pb),))
-        for j in range(2):
-            pr = 2 * bk + j
-
-            def fs(bk=pb, j=j, pr=pr):
-                return S.activation(B("sg")[:, 256 * pr:256 * pr + 256], P(bk)[:, 256 * j:256 * j + 256], AF.Sign, bias=0.5 - 16.0 * (7 - pr))
-            add("S", vt(256), fs, (PR(pb),), (R("sg", 256 * pr, 256 * pr + 256),))
-    for bk in range(4):
-        def fc(bk=bk):
-            for j in range(4):
-                k = 4 * bk + j
-                i = mm(P(5)[:, 0:128], T.L1[:, 128 * k:128 * k + 128], B("sg")[:, 128 * k:128 * k + 128], k == 0, False)
-            return i
-        add("T", tt(128, 4), fc, (R("sg", 512 * bk, 512 * bk + 512), ("L1", 0, 2048)), (PR(5),))
-    thr = 11 if first else 12
-    o, f, h = B("o")[:, :], B("f")[:, :], B("h")[:, :]
-    add("V", vt(128), lambda: ts(o, P(4)[:, 0:128], col(thr), 1024.0, A.is_ge, A.mult), (PR(4), rc(thr)), (R("o"),))
-    add("T", tt(128), lambda: mm(P(5)[:, 0:128], sl("IDm32"), o, False, True), (R("o"), rs("IDm32")), (PR(5),))
-    add("S", vt(128), lambda: S.activation(B("hd")[:, :], P(5)[:, 0:128], AF.Relu), (PR(5),), (R("hd"),))
-
-    def fE():
-        mm(P(4)[:, 128:256], sl("DE"), sl("ones"), True, False)
-        return mm(P(4)[:, 128:256], sl("SD"), o, False, True)
-    add("T", tt(128, 2), fE, (R("o"), rs("DE"), rs("SD"), rs("ones")), (PR(4),))
-    add("V", vt(128), lambda: V.tensor_tensor(B("eo")[:, :], o, P(4)[:, 128:256], A.mult), (R("o"), PR(4)), (R("eo"),))
-
-    def fF():
-        mm(P(5)[:, 128:256], sl("TGE"), B("hd")[:, :], True, False)
-        return mm(P(5)[:, 128:256], sl("IDh"), o, False, True)
-    add("T", tt(128, 2), fF, (R("o"), R("hd"), rs("TGE"), rs("IDh")), (PR(5),))
-    add("S", vt(128), lambda: S.activation(f, P(5)[:, 128:256], AF.Relu, bias=1.0, scale=-1.0, accum_out=B("Fs")[:, 0:1]),
-        (PR(5),), (R("f"), R("Fs")))
-    add("V", vt(128), lambda: V.tensor_tensor(h, P(5)[:, 128:256], o, A.is_gt), (PR(5), R("o")), (R("h"),))
-
-    def fX():
-        mm(P(4)[:, 384:512], sl("ID"), f, True, True)
-        mm(P(4)[:, 256:384], sl("DX"), sl("ones"), True, False)
-        mm(P(4)[:, 256:384], sl("SD"), o, False, False)
-        return mm(P(4)[:, 256:384], sl("NBD"), f, False, True)
-    add("T", tt(128, 4), fX, (R("o"), R("f"), rs("DX"), rs("SD"), rs("NBD"), rs("ones"), rs("ID")), (PR(4),))
-
-    def fK2():
-        return fK(P(6)[:, 256:384])
-    add("T", tt(128, 2), fK2, (rhl, rs("ID64"), rs("ID")), (PR(6),))
-    add("V", vt(128), lambda: V.tensor_tensor(B("dl")[:, :], B("dk")[:, :], P(4)[:, 384:512], A.mult), (R("dk"), PR(4)), (R("dl"),))
-    add("V", vt(128), lambda: V.tensor_tensor(B("val")[:, :], B("dl")[:, :], P(6)[:, 256:384], A.add), (R("dl"), PR(6)), (R("val"),))
-    add("S", vt(128), lambda: S.activation(B("h64")[:, :], B("val")[:, :], AF.Copy, bias=8224.5), (R("val"),), (R("h64"),))
-    add("V", vt(128), lambda: V.tensor_tensor(B("m")[:, :], h, P(4)[:, 256:384], A.mult), (R("h"), PR(4)), (R("m"),))
-
-    def fW(o_, dk, hs):
-        mm(o_, sl(dk), sl("ones"), True, False)
-        mm(o_, sl("NSLT"), o, False, False)
-        mm(o_, sl("ID16"), B("eo")[:, :], False, False)
-        return mm(o_, sl("ID64"), B("m")[:, :], False, False)
-    wr_ = (R("o"), R("eo"), R("m"), rs("ones"), rs("NSLT"), rs("ID16"), rs("ID64"), rs("DK"), rs("DKL"))
-    add("T", tt(128, 4), lambda: fW(P(5)[:, 256:384], "DK", None), wr_, (PR(5),))
-    add("T", tt(128, 4), lambda: fW(P(4)[:, 0:128], "DKL", None), wr_, (PR(4),))
-    add("T", tt(128), lambda: mm(P(5)[:, 256:384], sl("ID64t"), B("h64")[:, :], False, True), (R("h64"), rs("ID64t")), (PR(5),))
-    add("T", tt(128), lambda: mm(P(4)[:, 0:128], sl("NID"), B("h64")[:, :], False, True), (R("h64"), rs("NID")), (PR(4),))
-    add("V", vt(128), lambda: ts(B("WW")[:, 0:128], P(5)[:, 256:384], -129.0, None, A.add), (PR(5),), (R("WW", 0, 128),))
-    add("V", vt(128), lambda: V.tensor_tensor(B("WW")[:, 128:256], B("val")[:, :], P(4)[:, 0:128], A.add), (R("val"), PR(4)), (R("WW", 128, 256),))
-    if c == 1 and not last:
-        def fF2():
-            mm(P(6)[:, 384:385], T.ONE16[:, :], T.Fs0[:, 0:1], True, False)
-            return mm(P(6)[:, 384:385], T.ONE16[:, :], T.Fs1[:, 0:1], False, True)
-        add("T", tt(64, 8), fF2, (("Fs0", 0, 1), ("Fs1", 0, 1), ("ONE16", 0, 128)), (PR(6),))
-        add("V", vt(1), lambda: V.tensor_copy(T.Fi[:, 0:1], P(6)[:, 384:385]), (PR(6),), (("Fi", 0, 1),))
-        add("V", vt(1), lambda: ts(T.Fj[:, 0:1], T.Fi[:, 0:1], 511, None, A.bitwise_and), (("Fi", 0, 1),), (("Fj", 0, 1),))
-        add("V", vt(1), lambda: V.tensor_tensor(col(12), T.Fj[:, 0:1], col(11), A.add), (("Fj", 0, 1), rc(11)), (rc(12),))
-    for q in range(15):
-        def fq(q=q):
-            return ts(B("CL")[:, 256 * q:256 * q + 256], B("WW")[:, :], 64.0 * (q + 1), None, A.min)
-        add("V", vt(256, .5), fq, (R("WW"),), (R("CL", 256 * q, 256 * q + 256),))
-    add("T", tt(256), lambda: mm(P(6)[:, 0:256], T.PQ[:, 1920:2048], B("WW")[:, :], True, False), (R("WW"), ("PQ", 0, 2048)), (PR(6),))
-    for q0 in range(0, 15, 3):
-        def fp(q0=q0):
-            for q in range(q0, q0 + 3):
-                i = mm(P(6)[:, 0:256], T.PQ[:, 128 * q:128 * q + 128], B("CL")[:, 256 * q:256 * q + 256], False, q == 14)
-            return i
-        add("T", tt(256, 3), fp, (R("CL", 256 * q0, 256 * q0 + 768), ("PQ", 0, 2048)), (PR(6),))
-    add("S", vt(256), lambda: S.activation(T.HS[:, hb:hb + 256], P(6)[:, 0:256], AF.Identity, bias=col(5)), (PR(6), rc(5)), (("HS", hb, hb + 256),))
-    sh = None
-    if not last:
-        nb = 256 * (n + 2)
-
-        def sendh():
-            return g.remote_dma(out_ap=T.HL[:, nb:nb + 256], in_ap=T.HS[:, hb:hb + 256], remote_sem=T.sem["ah%d_%d" % (e + 1, c)],
-                                local_sem=T.sem.loc, pid=pid, routing_id=rid, dma_engine_mask=emask)
-        sh = add("G", 1.0, sendh, (("HS", hb, hb + 256),), (), kind="s")
-    else:
-        def fK3():
-            mm(P(7)[:, 0:128], sl("ID64"), T.HS[:, hb:hb + 128], True, False)
-            return mm(P(7)[:, 0:128], sl("ID"), T.HS[:, hb + 128:hb + 256], False, True)
-        add("T", tt(128, 2), fK3, (("HS", hb, hb + 256), rs("ID64"), rs("ID")), (PR(7),))
-        add("S", vt(128), lambda: S.activation(T.YK[:, 128 * c:128 * c + 128], P(7)[:, 0:128], AF.Copy), (PR(7),), (("YK", 128 * c, 128 * c + 128),))
-        add("Y", .1, lambda: SY.dma_start(T.yk[:, 128 * c:128 * c + 128], T.YK[:, 128 * c:128 * c + 128]), (("YK", 128 * c, 128 * c + 128),), (),
-            kind="d", sem="st%d" % c, val=16, lat=2.2)
-    add("V", vt(128, SCA), lambda: V.tensor_tensor(T.Wf[:, wa:wb].indirect(B("c16")[:, 0:8]), B("Wo")[:, :], B("dl")[:, :], A.subtract),
-        (R("Wo"), R("dl"), R("c16")), (("Wf", wa, wb),))
-    if last:
-        add("Y", .1, lambda: SY.dma_start(T.yw[:, wa:wb], T.Wf[:, wa:wb]), (("Wf", wa, wb),), (), kind="d", sem="st%d" % (2 + c), val=16, lat=2.5)
-    for bk in range(4):
-        pb = 2 + bk % 2
-
-        def fm(bk=bk, pb=pb):
-            for j in range(4):
-                k = 4 * bk + j
-                mm(P(pb)[:, 128 * j:128 * j + 128], sl("ID"), B("x")[:, k:2048:16], True, False)
-                i = mm(P(pb)[:, 128 * j:128 * j + 128], T.L2[:, 128 * k:128 * k + 128], h, False, True)
-            return i
-        add("T", tt(128, 8), fm, (R("h"), R("x"), ("L2", 0, 2048), rs("ID")), (PR(pb),))
-        for j in range(2):
-            def fM(bk=bk, j=j, pb=pb):
-                src = P(pb)[:, 256 * j:256 * j + 256]
-                if bk == 0 and j == 0:
-                    return ts(B("AC")[:, :], src, 256.0, None, A.max)
-                return V.tensor_tensor(B("AC")[:, :], B("AC")[:, :], src, A.max)
-            add("V", vt(256), fM, (PR(pb),) if bk == 0 and j == 0 else (R("AC"), PR(pb)), (R("AC"),))
-    add("V", vt(128, 2), lambda: V.tensor_tensor(B("mz")[:, :], B("AC")[:, 0:128], B("AC")[:, 128:256], A.max), (R("AC"),), (R("mz"),))
-    zs = 128 * n
-
-    def fz():
-        mm(P(2)[:, 0:128], sl("ID"), z, True, False)
-        return mm(P(2)[:, 0:128], sl("NID"), B("mz")[:, :], False, True)
-    add("T", tt(128, 2), fz, (rz, R("mz"), rs("ID"), rs("NID")), (PR(2),))
-    add("S", vt(128), lambda: S.activation(T.ZS[:, zs:zs + 128], P(2)[:, 0:128], AF.Abs, bias=256.0), (PR(2),), (("ZS", zs, zs + 128),))
-    if not last:
-        nz = 512 * (n + 2)
-
-        def sendz():
-            return g.remote_dma(out_ap=T.Z4[:, nz:nz + 128], in_ap=T.ZS[:, zs:zs + 128], remote_sem=T.sem["az%d_%d" % (e + 1, c)],
-                                local_sem=T.sem.loc, pid=pid, routing_id=rid, dma_engine_mask=emask)
-        sz = add("G", 1.0, sendz, (("ZS", zs, zs + 128),), (), kind="s")
-        _lead_sends[(e, c)] = (sh, sz)
-    else:
-        add("Y", .1, lambda: SY.dma_start(T.yz[:, 128 * c:128 * c + 128], T.ZS[:, zs:zs + 128]), (("ZS", zs, zs + 128),), (),
-            kind="d", sem="st%d" % (4 + c), val=16, lat=2.2)
-
-
-_lead_sends = {}
+            prio[i] = d + max([prio[k] + h for k, h in succ[i]] + [-99.0])
+    best = cur = run(succ, pred, prio, False)
+    for _ in range(PAR["PASS"]):
+        cur = run(succ, pred, run(pred, succ, cur[2], True)[2], False)
+        if cur[0] < best[0]:
+            best = cur
+    _ORDER["est"] = best[0]
+    return best[1]

@@ -3,51 +3,51 @@ from concourse.mybir import AluOpType, AxisListType, ActivationFunctionType
 
 A = AluOpType
 AF = ActivationFunctionType
-LE = 6
+LE, NC, R = 6, 4, 64
 V0 = 4192.0
-SLOTS = ["ones", "BD0", "BD", "ID", "NID", "ID2", "IDm16", "IDm256", "ID16k", "Cm192", "Cm96", "Cm4256", "TGE", "SLT", "SGT",
-         "SH", "SL", "TEo", "TFo", "THt", "THo", "CQ", "t0", "t1", "t2", "t3", "t4", "t5"]
+BIG = 16192.0
+SLOTS = ["ones", "BD0", "BD", "ID", "NID", "ID2", "ID64", "ID98", "IDm16", "IDm256", "IDbig", "Cval", "Cnew", "TGE", "SLT", "SGT",
+         "SH", "SL", "TEo", "TFo", "THt", "THo", "CQ", "DF", "DO", "t0", "t1", "t2", "t3", "t4", "t5"]
 
 SCRATCH = {
     "X": ("sbuf", [128, 4096], "bfloat16"), "Y": ("sbuf", [128, 4096], "bfloat16"),
-    "Gf": ("sbuf", [128, 1024], "float32"), "Wf": ("sbuf", [128, 1024], "float32"), "Wout": ("sbuf", [128, 1024], "float32"),
+    "Gf": ("sbuf", [128, 1024], "float32"), "Wf": ("sbuf", [128, 1024], "float32"),
     "rti": ("sbuf", [128, 1024], "int32"), "wri": ("sbuf", [128, 1024], "int32"), "rki": ("sbuf", [128, 256], "int32"),
     "thi": ("sbuf", [128, 1], "int32"), "wtb": ("sbuf", [128, 1], "bfloat16"),
-    "ZL": ("sbuf", [128, 12 * 128], "bfloat16"), "HL": ("sbuf", [128, 12 * 256], "bfloat16"),
-    "HS": ("sbuf", [128, 12 * 256], "bfloat16"), "ZS": ("sbuf", [128, 12 * 128], "bfloat16"),
-    "TB": ("sbuf", [128, 128 * len(SLOTS)], "bfloat16"),
-    "ONE16": ("sbuf", [128, 128], "float32"),
-    "Z1": ("sbuf", [128, 144], "bfloat16"), "WZ": ("sbuf", [128, 144], "bfloat16"),
-    "L2": ("sbuf", [128, 2048], "bfloat16"), "PQ": ("sbuf", [128, 1024], "bfloat16"),
-    "W37": ("sbuf", [128, 128], "float16"),
-    "COL": ("sbuf", [128, 32], "float32"), "kk": ("sbuf", [128, 16], "float32"), "RK": ("sbuf", [128, 16], "float32"),
-    "rowi": ("sbuf", [128, 4], "int32"),
-    "I4a": ("sbuf", [128, 8], "int32"), "I4": ("sbuf", [128, 8], "int32"),
-    "Fs": ("sbuf", [128, 4], "float32"), "Ff": ("sbuf", [128, 1], "float32"),
+    "HL": ("sbuf", [128, LE * 768], "bfloat16"), "HS": ("sbuf", [128, LE * 768], "bfloat16"),
+    "TB": ("sbuf", [128, 128 * len(SLOTS)], "bfloat16"), "ONE16": ("sbuf", [128, 128], "float32"),
+    "Z1": ("sbuf", [128, 144], "bfloat16"), "Z2": ("sbuf", [128, 144], "bfloat16"), "WZ": ("sbuf", [128, 144], "bfloat16"),
+    "L2": ("sbuf", [128, 2048], "bfloat16"), "PQ": ("sbuf", [128, 1024], "bfloat16"), "CT": ("sbuf", [128, 128], "bfloat16"),
+    "W37": ("sbuf", [128, 128], "float16"), "COL": ("sbuf", [128, 24], "float32"), "rowi": ("sbuf", [128, 4], "int32"),
+    "I4a": ("sbuf", [128, 4], "int32"), "I4": ("sbuf", [128, 4], "int32"), "Fs": ("sbuf", [128, 8], "float32"), "Ff": ("sbuf", [128, 1], "float32"),
     "Fi": ("sbuf", [128, 1], "int32"), "Fj": ("sbuf", [128, 1], "int32"),
     "YK": ("sbuf", [128, 256], "float32"), "hI": ("sbuf", [128, 256], "int32"), "lI": ("sbuf", [128, 256], "int32"),
-    "Z2": ("sbuf", [128, 144], "bfloat16"), "CT": ("sbuf", [128, 256], "bfloat16"),
 }
-for _c in range(2):
-    for _n, _w, _d in (("K16", 128, "uint16"), ("x", 2048, "bfloat16"), ("d", 2048, "bfloat16"), ("sg", 2048, "bfloat16"),
-                       ("ua", 8, "int32"), ("ub", 8, "int32"), ("uc", 8, "int32"), ("ud", 8, "int32"), ("ue", 8, "int32"),
-                       ("c16", 8, "uint16"), ("Gs", 128, "float32"), ("Wo", 128, "float32"), ("Wp", 128, "float32"),
-                       ("dk", 128, "float32"), ("dl", 128, "float32"), ("val", 128, "float32"), ("p1", 128, "int32"),
-                       ("pr", 128, "int32"), ("s1", 128, "int32"), ("s2", 128, "int32"), ("s16", 128, "uint16"),
-                       ("un", 128, "bfloat16"), ("cs", 128, "bfloat16"), ("hd", 128, "bfloat16"), ("ta", 128, "bfloat16"),
-                       ("EE", 384, "bfloat16"), ("WW", 256, "bfloat16"), ("CL", 8 * 256, "bfloat16"), ("tq", 256, "bfloat16"),
-                       ("AC", 256, "float16"), ("mz", 128, "float16")):
-        SCRATCH[_n + str(_c)] = ("sbuf", [128, _w], _d)
+PER_RACK = {"K16": (1, "uint16"), "s16": (1, "uint16"), "x": (16, "bfloat16"), "d": (16, "bfloat16"), "sg": (16, "bfloat16"),
+            "Kf": (1, "float32"), "Wo": (1, "float32"), "Tc": (1, "float32"), "gw": (1, "float32"), "nw": (1, "float32"),
+            "val": (1, "float32"), "p1": (1, "int32"), "la": (1, "int32"), "lb": (1, "int32"), "s1": (1, "int32"), "s2": (1, "int32"),
+            "un": (1, "bfloat16"), "hd": (1, "bfloat16"), "ta": (1, "bfloat16"), "cs": (2, "bfloat16"), "EE": (3, "bfloat16"),
+            "WW": (2, "bfloat16"), "CL": (16, "bfloat16"), "tq": (2, "bfloat16"), "AC": (4, "float16"), "mz": (1, "float16")}
+for _n, (_w, _d) in PER_RACK.items():
+    SCRATCH[_n] = ("sbuf", [128, 256 * _w], _d)
+for _n in ("ua", "ub", "uc", "ud", "c16"):
+    SCRATCH[_n] = ("sbuf", [128, 16], "uint16" if _n == "c16" else "int32")
 for _b in range(8):
     SCRATCH["ps%d" % _b] = ("psum", [128, 512], "float32")
+TABLES = ("TB", "Z1", "WZ", "L2", "PQ", "W37", "CT", "X", "Y", "Gf", "ONE16", "I4")
 
-SEMAPHORES = ["eV", "eS", "eT", "eG", "loc"] + ["ld%d" % _i for _i in range(12)] + ["st%d" % _i for _i in range(6)]
+SEMAPHORES = ["eV", "eS", "eT", "eG", "loc"] + ["ld%d" % _i for _i in range(18)] + ["st%d" % _i for _i in range(3 * NC)]
 for _e in range(1, LE):
-    for _c in range(2):
+    for _c in range(NC):
         SEMAPHORES += ["ah%d_%d" % (_e, _c), "az%d_%d" % (_e, _c)]
 
-PAR = {"CY": 0.83e-3 * 1.05, "TC": 0.42e-3 * 1.05, "GAT": 1.55, "SCA": 3.8, "HOP": 0.1, "REM": 3.2, "WIN": 0.02, "XV": (3,),
-       "PASS": 6, "T": 20, "S": 10, "BW": 0.2}
+PLACE = {"u": (None, 0), "K": (None, 1), "lin": (None, 2), "yx": (None, 0), "cnt": (1, 6), "D": (None, 4), "hd": (None, 7), "F": (None, 6), "ex": (None, 0),
+         "E": (None, 5), "E98": (None, 6), "V": (None, 0), "pair": (None, 6), "yk": (None, 0),
+         "val": (None, 3), "new": (None, 4), "A": (None, 7), "m": (2, 4), "z": (3, 6)}
+
+PAR = {"CY": 0.83e-3, "TC": 0.42e-3, "GAT": 1.3, "SCA": 2.8, "GO": 0.06, "OV": 0.005, "HOP": 0.26, "HOPS": 0.2, "ISS": 0.4, "REM": 3.5,
+       "BW": 0.26, "T": 20, "S": (2, 3, 4, 5, 6), "LOOK": (0, .3), "PASS": 5, "XP": (32, 32), "YP": (32, 32), "XV": (), "EP": 2,
+       "CP": 1, "TV": 0, "YS": (), "TS": 1, "C4": 0, "LB": 0, "MIX": 0.1, "GS": 1.15, "VF": 0, "MG": 2, "KF": 1, "E4": 1, "ONE": (), "FAR": 0.3}
 _ORDER = {}
 
 
@@ -62,27 +62,33 @@ def rank_program(g, core, T, topo):
     neng = len(topo.engines(core, dst))
     V, S, TE, SY = g.vector, g.scalar, g.tensor, g.sync
     QS = {"V": V, "S": S, "T": TE, "G": g, "Y": SY}
-    CY, TC = PAR["CY"], PAR["TC"]
+    CY = PAR["CY"]
     ops, acc, cur = [], {}, [-1]
 
     def ap(o):
         if not isinstance(o, tuple):
             return o
-        a = T[o[0]][:, o[1]:o[2]:o[3]] if o[3] != 1 else T[o[0]][:, o[1]:o[2]]
+        st, n = o[3] if isinstance(o[3], tuple) else (o[3], 128)
+        a = T[o[0]][0:n, o[1]:o[2]:st] if st != 1 else T[o[0]][0:n, o[1]:o[2]]
         return a.indirect(ap(o[4])) if len(o) > 4 else a
 
     def width(o):
-        return 16 * width(o[4]) if len(o) > 4 else len(range(o[1], o[2], o[3]))
+        return 16 * width(o[4]) if len(o) > 4 else len(range(o[1], o[2], o[3][0] if isinstance(o[3], tuple) else o[3]))
 
-    def add(q, dur, emit, R=(), W=(), kind="c", sem=None, val=0, lat=0.0, extra=()):
+    def sub(o, a, b, st=1):
+        return (o[0], o[1] + a, o[1] + b, st)
+
+    def add(q, dur, emit, reads=(), writes=(), kind="c", sem=None, val=0, lat=0.0, extra=()):
         i = len(ops)
         deps = {j: False for j in extra}
-        R = [o for o in R if isinstance(o, tuple)]
-        R += [o[4] for o in list(R) + list(W) if len(o) > 4]
-        for isw, regs in ((False, R), (True, W)):
+        reads = [o for o in reads if isinstance(o, tuple)]
+        reads += [o[4] for o in list(reads) + list(writes) if len(o) > 4]
+        for isw, regs in ((False, reads), (True, writes)):
             for o in regs:
                 buf, lo, hi = o[0], o[1], o[2]
-                ps = buf[:2] == "ps"
+                if cur[0] >= 0 and buf in TABLES:
+                    deps.update((a[0], True) for a in acc[buf] if a[3] and a[1] < hi and lo < a[2])
+                    continue
                 keep = []
                 for a in acc.get(buf, []):
                     j, l, h, aw = a
@@ -91,7 +97,7 @@ def rank_program(g, core, T, topo):
                         continue
                     over = l < hi and lo < h
                     same = ops[j]["q"] == q and ops[j]["kind"] == "c" and kind == "c"
-                    if ps:
+                    if buf[:2] == "ps":
                         deps[j] = deps.get(j, False) or not same or (over and (aw or isw) and q != "T")
                         if not same or q == "T" or (isw and l >= lo and h <= hi):
                             continue
@@ -103,53 +109,52 @@ def rank_program(g, core, T, topo):
                     keep.append(a)
                 keep.append((i, lo, hi, isw))
                 acc[buf] = keep
-        ops.append({"q": q, "dur": dur, "emit": emit, "deps": deps, "kind": kind, "sem": sem, "val": val, "lat": lat, "grp": cur[0]})
+        slow = 1.5 * dur * (PAR["GS"] if any(len(o) > 4 for o in list(reads) + list(writes)) else 1.0)
+        ops.append({"q": q, "fast": dur, "slow": slow, "dur": dur + PAR["MIX"] * (slow - dur), "emit": emit, "deps": deps, "kind": kind, "sem": sem, "val": val, "lat": lat, "grp": cur[0]})
         return i
 
     def two(o):
         return SCRATCH[o[0]][2] in ("bfloat16", "float16", "uint16")
 
-    def cyc(out, ins, rate):
-        if len(out) > 4:
-            return 0.05 + width(out) * PAR["SCA"] * CY
-        if len(ins[0]) > 4:
-            return 0.06 + width(out) * PAR["GAT"] * CY
-        return 0.03 + max(64, width(out) * rate) * CY
+    def cyc(out, a, rate):
+        if len(out) > 4 or len(a) > 4:
+            return PAR["GO"] + width(out) * PAR["SCA" if len(out) > 4 else "GAT"] * CY
+        return PAR["OV"] + max(64, width(out) * rate) * CY
 
     def ts(out, in0, s1, op0, s2=None, op1=None):
         def f():
             if op1 is None:
                 return V.tensor_scalar(ap(out), ap(in0), ap(s1), None, op0)
             return V.tensor_scalar(ap(out), ap(in0), ap(s1), ap(s2), op0, op1)
-        return add("V", cyc(out, (in0,), .5 if two(out) and two(in0) else 1), f, (in0, s1, s2), (out,))
+        return add("V", cyc(out, in0, .5 if two(out) and two(in0) else 1), f, (in0, s1, s2), (out,))
 
     def tt(out, a, b, op):
         r = 1 if "ps" in (a[0][:2], b[0][:2]) else 2
-        return add("V", cyc(out, (a,), r), lambda: V.tensor_tensor(ap(out), ap(a), ap(b), op), (a, b), (out,))
+        return add("V", cyc(out, a, r), lambda: V.tensor_tensor(ap(out), ap(a), ap(b), op), (a, b), (out,))
 
     def cp(out, a):
-        return add("V", cyc(out, (a,), .5 if two(out) and two(a) else 1), lambda: V.tensor_copy(ap(out), ap(a)), (a,), (out,))
+        return add("V", cyc(out, a, .5 if two(out) and two(a) else 1), lambda: V.tensor_copy(ap(out), ap(a)), (a,), (out,))
 
     def fill(out, v):
-        return add("V", cyc(out, (out,), .5 if two(out) else 1), lambda: V.memset(ap(out), v), (), (out,))
+        return add("V", cyc(out, out, .5 if two(out) else 1), lambda: V.memset(ap(out), v), (), (out,))
 
     def act(out, a, fn, bias=0.0, scale=1.0, accum=None):
         def f():
             if accum is None:
                 return S.activation(ap(out), ap(a), fn, bias=ap(bias), scale=ap(scale))
             return S.activation(ap(out), ap(a), fn, bias=ap(bias), scale=ap(scale), accum_out=ap(accum))
-        return add("S", cyc(out, (a,), 1), f, (a, bias, scale), (out,) if accum is None else (out, accum))
+        return add("S", cyc(out, a, 1), f, (a, bias, scale), (out,) if accum is None else (out, accum))
 
     def mms(lst):
         def f():
             for o, l, r, a, b in lst:
                 i = TE.matmul(ap(o), ap(l), ap(r), a, b)
             return i
-        dur = sum(max(64, width(r)) * TC * (1 if two(r) else 4) for o, l, r, a, b in lst)
+        dur = sum(max(64, width(r)) * PAR["TC"] * (1 if two(r) else 4) for o, l, r, a, b in lst)
         return add("T", dur, f, [x for m in lst for x in m[1:3]], [m[0] for m in lst])
 
-    def mm(out, *terms):
-        return mms([(out, l, r, j == 0, j == len(terms) - 1) for j, (l, r) in enumerate(terms)])
+    def grp(out, *terms):
+        return [(out, l, r, j == 0, j == len(terms) - 1) for j, (l, r) in enumerate(terms)]
 
     def sl(n):
         s = SLOTS.index(n)
@@ -171,27 +176,32 @@ def rank_program(g, core, T, topo):
         add("R", 0, None, (), (reg,), kind="r", sem=s, val=16, lat=clock[1])
 
     load("S", whole("wtb"), T.wt[:, :])
-    load("S", ("ZL", 0, 256, 1), T.z0[:, :])
+    for c in range(NC):
+        load("S", ("HL", 3 * R * c + 2 * R, 3 * R * c + 3 * R, 1), T.z0[:, R * c:R * c + R])
     load("Y", whole("rki"), T.rk[:, :])
-    load("Y", ("rti", 0, 512, 1), T.rt[:, 0:512])
     load("Y", whole("X"), T.gx[:, :])
-    load("Y", ("Y", 160, 4096, 1), T.sy[:, 0:3936])
-    load("S", ("Y", 0, 160, 1), T.sy[:, 3936:4096])
+    load("Y", ("rti", 0, 4 * R, 1), T.rt[:, 0:4 * R])
+    load("Y", ("Y", 320, 4096, 1), T.sy[:, 0:3776])
+    load("S", ("Y", 0, 320, 1), T.sy[:, 3776:4096])
     load("S", whole("thi"), T.th[:, :])
-    load("Y", ("rti", 512, 1024, 1), T.rt[:, 512:1024])
-    load("Y", ("wri", 0, 512, 1), T.wr[:, 0:512])
-    load("Y", ("wri", 512, 1024, 1), T.wr[:, 512:1024])
+    for a in range(0, 1024, 4 * R):
+        if a:
+            load("Y", ("rti", a, a + 4 * R, 1), T.rt[:, a:a + 4 * R])
+        load("Y", ("wri", a, a + 4 * R, 1), T.wr[:, a:a + 4 * R])
 
     def sel(o, i, pat, op, base, cm):
         add("G", .4, lambda: g.affine_select(ap(sl(o)), ap(sl(i)), pat, op, 0.0, base, cm), (sl(i),), (sl(o),))
 
+    def lin(o, i, a, b):
+        ts(col(o), col(i), float(a), A.mult, float(b), A.add)
+
+    def scl(o, i, a):
+        act(sl(o), sl(i), AF.Copy, scale=a)
     fill(sl("ones"), 1.0)
     add("G", .2, lambda: g.iota(T.rowi[:, 0:1], [[0, 1]], 0, 1), (), (("rowi", 0, 1, 1),))
     sel("ID", "ones", [[-1, 128]], A.is_equal, 0, 1)
     sel("BD0", "ones", [[-16, 8], [0, 16]], A.is_ge, 0, 1)
     sel("BD", "BD0", [[16, 8], [0, 16]], A.is_ge, 15, -1)
-    add("G", .2, lambda: g.iota(T.I4a[:, :], [[64, 8]], 0, 0), (), (whole("I4a"),))
-    add("G", .2, lambda: g.iota(T.kk[:, :], [[1, 16]], 0, 0, allow_small_or_imprecise_dtypes=True), (), (whole("kk"),))
     sel("TGE", "BD", [[-1, 128]], A.is_ge, 0, 1)
     sel("SLT", "BD", [[1, 128]], A.is_ge, -1, -1)
     sel("SGT", "BD", [[-1, 128]], A.is_ge, -1, 1)
@@ -200,258 +210,312 @@ def rank_program(g, core, T, topo):
     ts(("rowi", 1, 2, 1), ("rowi", 0, 1, 1), 15, A.bitwise_and)
     ts(("rowi", 2, 3, 1), ("rowi", 0, 1, 1), 1, A.bitwise_and)
     cp(col(0), ("rowi", 1, 2, 1))
-
-    def lin(o, i, a, b):
-        ts(col(o), col(i), float(a), A.mult, float(b), A.add)
-
-    def scl(o, i, a):
-        act(sl(o), sl(i), AF.Copy, scale=a)
-    lin(10, 0, 4, 0)
-    ts(whole("I4"), whole("I4a"), col(10), A.add)
-    fill(whole("Z1"), 0.0)
+    cp(col(1), ("rowi", 2, 3, 1))
+    lin(2, 1, -1, 1)
+    lin(3, 0, 4, 0)
+    add("G", .2, lambda: g.iota(T.I4a[:, :], [[64, R // 16]], 0, 0), (), (whole("I4a"),))
+    ts(whole("I4"), whole("I4a"), col(3), A.add)
     bd = sl("BD")
-    bd8 = ("TB", bd[1], bd[2], 16)
+    bd8 = sub(bd, 0, 128, 16)
+    fill(whole("Z1"), 0.0)
     cp(("Z1", 15, 143, 16), bd8)
     ts(whole("WZ"), whole("Z1"), whole("wtb"), A.mult)
-    scl("Cm4256", "ID", -4256.0)
     ts(col(7), whole("wtb"), 37.0, A.mult)
     ts(col(8), col(7), 2048.0, A.is_gt, -4096.0, A.mult)
     tt(col(9), col(7), col(8), A.add)
-    ts(whole("W37"), bd, col(9), A.mult)
+    ts(whole("W37"), bd, col(9), A.mult, 16.0 if PAR["LB"] else 1.0, A.mult)
     ts(whole("hI"), whole("rki"), 4064, A.bitwise_and)
     ts(whole("lI"), whole("rki"), 31, A.bitwise_and)
-    for c in range(2):
-        ts(("HL", 256 * c, 256 * c + 128, 1), ("hI", 128 * c, 128 * c + 128, 1), 4096.0, A.add)
-        ts(("HL", 256 * c + 128, 256 * c + 256, 1), ("lI", 128 * c, 128 * c + 128, 1), 192.0, A.add)
-    for c in range(2):
-        ts(("Gf", 512 * c, 512 * c + 512, 1), ("rti", 512 * c, 512 * c + 512, 1), -32.0, A.add)
-        ts(("Wf", 512 * c, 512 * c + 512, 1), ("wri", 512 * c, 512 * c + 512, 1), V0, A.add)
+    for c in range(NC):
+        ts(("HL", 3 * R * c, 3 * R * c + R, 1), ("hI", R * c, R * c + R, 1), 4096.0, A.add)
+        ts(("HL", 3 * R * c + R, 3 * R * c + 2 * R, 1), ("lI", R * c, R * c + R, 1), 192.0, A.add)
+    for a in range(0, 1024, 4 * R):
+        ts(("Gf", a, a + 4 * R, 1), ("rti", a, a + 4 * R, 1), -64.0, A.add)
+        cp(("Wf", a, a + 4 * R, 1), ("wri", a, a + 4 * R, 1))
     ts(col(11), whole("thi"), -1.0, A.mult, 0.5, A.add)
-    for n, a in (("NID", -1), ("ID2", 2), ("IDm16", -16), ("IDm256", -256), ("ID16k", 16384), ("Cm192", -192), ("Cm96", -96)):
+    for n, a in (("ID64", 64), ("NID", -1), ("ID2", 2), ("ID98", 251 / 256), ("IDm16", -16), ("IDm256", -256), ("IDbig", BIG),
+                 ("Cval", -192), ("Cnew", BIG - 96 - V0)):
         scl(n, "ID", float(a))
-    for n, t, a, tri, b in (("TEo", "t0", 128, "SGT", -3.5), ("TFo", "t1", -256, "SLT", -3.5), ("THt", "t2", 256, "SGT", 7.0),
-                            ("THo", "t3", 128, "SGT", 3.5)):
+    for n, t, a, tri, b in (("TEo", "t0", 124, "SGT", -3.5), ("TFo", "t1", -256, "SLT", -3.5), ("THt", "t2", 143, "SGT", 7.0),
+                            ("THo", "t3", 71.5, "SGT", 3.5)):
         scl(t, tri, b)
         scl(n, "ID", float(a))
         tt(sl(n), sl(n), sl(t), A.add)
-    ln2 = math.log(2.0)
-    lin(1, 0, 3.5 * ln2, (105 - 52.5 - 57 - 128) * ln2)
-    lin(2, 0, 3.5 * ln2, (-56 - 256) * ln2)
-    lin(3, 0, -3.5 * ln2, (52.5 - 57 - 128) * ln2)
-    ts(col(13), ("rowi", 2, 3, 1), -1.0, A.mult, 1.0, A.add)
-    cp(col(20), ("rowi", 2, 3, 1))
-    lin(14, 0, 2 ** 20, -15 * 2 ** 20)
-    ts(col(14), col(14), col(20), A.mult)
-    ts(col(15), col(0), 14.0, A.is_lt, col(20), A.mult)
+    lin(10, 0, 7, -236)
+    scl("DF", "ID", col(10))
+    lin(23, 0, 7, -52.5)
+    scl("DO", "ID", col(23))
+    lin(22, 0, -3.5 * math.log(2.0), -76 * math.log(2.0))
+    lin(13, 0, 2 ** 20, -15 * 2 ** 20)
+    ts(col(14), col(13), col(1), A.mult)
+    ts(col(15), col(0), 14.0, A.is_lt, col(1), A.mult)
     lin(16, 0, -64, -64)
-    ts(col(15), col(15), col(16), A.mult)
-    ts(col(16), col(13), 4128.0, A.mult)
-    scl("CQ", "ID", col(16))
-    scl("t4", "SH", col(15))
+    ts(col(17), col(15), col(16), A.mult)
+    ts(col(18), col(2), 4128.0, A.mult)
+    scl("CQ", "ID", col(18))
+    scl("t4", "SH", col(17))
     scl("t5", "SL", col(14))
+    tt(sl("t4"), sl("t4"), sl("t5"), A.add)
     tt(sl("CQ"), sl("CQ"), sl("t4"), A.add)
-    tt(sl("CQ"), sl("CQ"), sl("t5"), A.add)
-    fill(("CT", 0, 128, 1), 1.0)
-    ts(("CT", 128, 256, 1), sl("ones"), col(13), A.add)
-    lin(17, 0, 8191.5, .5 - 8192 * 15)
-    for o, top, low in ((4, -15.75, 6144.0), (5, 64 - .9765625, 189.0)):
-        ts(col(18 + o - 4), col(17), top - low, A.add)
-        ts(col(o), col(18 + o - 4), col(20), A.mult, low, A.add)
-    ts(col(6), col(20), 2.0 ** 23 + 1, A.mult, -1.0, A.add)
+    fill(("CT", 0, R, 1), 1.0)
+    ts(("CT", R, 2 * R, 1), sub(sl("ones"), 0, R), col(2), A.add)
+    lin(19, 0, 8191.5, .5 - 8192 * 15)
+    for o, t, top, low in ((4, 20, -15.75, 6144.0), (5, 21, 64 - .9765625, 189.0)):
+        ts(col(t), col(19), top - low, A.add)
+        ts(col(o), col(t), col(1), A.mult, low, A.add)
+    ts(col(6), col(1), 2.0 ** 23 + 1, A.mult, -1.0, A.add)
     fill(whole("Z2"), 0.0)
     cp(("Z2", 15, 143, 16), bd8)
     ts(("Z2", 16, 144, 16), bd8, 2.0 ** -30, A.mult)
-    fill(whole("ONE16"), -16.0)
-    ts(whole("RK"), whole("kk"), col(0), A.is_equal, 256.0, A.mult)
-    for k in range(16):
-        o = ("L2", 128 * k, 128 * k + 128, 1)
-        if k % 2:
-            act(o, bd, AF.Copy, scale=("RK", k, k + 1, 1))
-        else:
-            ts(o, bd, ("RK", k, k + 1, 1), A.mult)
     for a in range(8):
         ts(("PQ", 128 * a, 128 * a + 128, 1), ("Z2", 15 - 2 * a, 143 - 2 * a, 1), 2.0 ** (56 - 14 * a), A.mult)
+    fill(whole("ONE16"), -16.0)
+    fill(whole("L2"), 256.0)
+    add("G", 3.8, lambda: g.affine_select(T.L2[:, :], T.L2[:, :], [[-1, 16], [-16, 8], [0, 16]], A.is_equal, 0.0, 0, 1),
+        (whole("L2"),), (whole("L2"),))
+    ln2 = math.log(2.0)
 
     def row(buf, k):
         return (buf, 15 - k, 143 - k, 1)
+
+    def cut(ws):
+        return [(sum(ws[:j]), sum(ws[:j + 1])) for j in range(len(ws))]
 
     sends = {}
 
     def lead(e, c):
         first, last = e == 0, e == LE - 1
-        n = 2 * e + c
+        r0, wa, wb = R * c, 4 * R * c, 4 * R * c + 4 * R
 
         def B(nm, a=0, b=None, st=1):
-            return (nm + str(c), a, SCRATCH[nm + str(c)][1][1] if b is None else b, st)
+            w = PER_RACK[nm][0] * R if nm in PER_RACK else R // 16
+            return (nm, w * c + a, w * c + (w if b is None else b), st)
 
-        def P(b, j, w=128, st=1):
-            return ("ps%d" % b, 128 * j, 128 * j + w, st)
-        pa, pb = 4 + 2 * c, 5 + 2 * c
-        z = ("ZL", 128 * n, 128 * n + 128, 1)
-        hi, lo = ("HL", 256 * n, 256 * n + 128, 1), ("HL", 256 * n + 128, 256 * n + 256, 1)
+        def P(b, j, n=1):
+            return ("ps%d" % b, R * j, R * (j + n), 1)
+
+        def Q(nm, j=0, n=1):
+            b, s = PLACE[nm]
+            return P(4 + c if b is None else b, s + j, n)
+
+        def send(src, sem):
+            to = ("HL", src[1] + 768, src[2] + 768, 1)
+            sends[sem] = add("G", PAR["ISS"], lambda: g.remote_dma(
+                out_ap=ap(to), in_ap=ap(src), remote_sem=T.sem[sem], local_sem=T.sem.loc, pid=pid, routing_id=rid,
+                dma_engine_mask=emask), (src,), (), kind="s")
+
+        def store(out, src, s):
+            add("Y", .1, lambda: SY.dma_start(out, ap(src)), (src,), (), kind="d", sem="st%d" % (3 * c + s), val=16, lat=2.3)
+        land = ("HL", 768 * e + 3 * r0, 768 * e + 3 * r0 + 3 * R, 1)
+        hl, hi, lo, z = sub(land, 0, 2 * R), sub(land, 0, R), sub(land, R, 2 * R), sub(land, 2 * R, 3 * R)
+        ones = sub(sl("ones"), 0, R)
         if not first:
-            sh, sz = sends[(e - 1, c)]
-            add("R", 0, None, (), (("HL", hi[1], lo[2], 1),), kind="r", sem="ah%d_%d" % (e, c), val=neng, lat=PAR["REM"], extra=(sh,))
-            add("R", 0, None, (), (z,), kind="r", sem="az%d_%d" % (e, c), val=neng, lat=PAR["REM"], extra=(sz,))
-        kt = ((sl("ID"), hi), (sl("ID"), lo))
-        Kp, up = P(pa, 0), P(pb, 0, 8)
-        mm(Kp, (sl("Cm4256"), sl("ones")), *kt)
-        ts(B("K16"), Kp, -32.0, A.add)
-        mm(up, *[(row("WZ", r), ("ZL", z[1] + r, z[2], 16)) for r in range(16)])
+            for o, s in ((land, "az%d_%d" % (e, c)),) if c in PAR["ONE"] else ((hl, "ah%d_%d" % (e, c)), (z, "az%d_%d" % (e, c))):
+                add("R", 0, None, (), (o,), kind="r", sem=s, val=neng, lat=PAR["REM"], extra=(sends[s],))
+        thr = col(11 if first else 12)
+        if PAR["KF"]:
+            mms(grp(Q("K"), (sl("ID"), hi), (sl("ID"), lo)))
+            ts(B("K16"), Q("K"), -96 - V0, A.add)
+            act(B("Kf"), Q("K"), AF.Copy, bias=-64 - V0)
+        up = sub(Q("u"), 0, R // 16)
+        mms(grp(up, *[(row("WZ", r), sub(z, r, R, 16)) for r in range(16)]))
         cp(B("ua"), up)
         ts(B("ub"), B("ua"), 63, A.bitwise_and)
         tt(B("uc"), B("ub"), B("ub"), A.mult)
         ts(B("ud"), B("uc"), 5, A.arith_shift_right, 3, A.bitwise_and)
-        tt(B("ue"), B("ud"), whole("I4"), A.add)
-        cp(B("c16"), B("ue"))
-        wa, wb = 512 * c, 512 * c + 512
-        act(B("Gs"), ("Gf", wa, wb, 1, B("c16")), AF.Copy)
-        mm(P(pb, 1), (whole("W37"), z), *kt)
-        mm(P(pb, 2), (sl("Cm96"), sl("ones")), *kt)
-        tt(B("p1"), B("Gs"), Kp, A.mult)
-        ts(B("pr"), B("p1"), 5, A.arith_shift_right)
-        tt(B("s1"), B("pr"), P(pb, 1), A.add)
-        ts(B("s2"), B("s1"), 4095, A.bitwise_and)
+        if PAR["C4"]:
+            for a in range(R // 16):
+                ts(B("c16", a, a + 1), B("ud", a, a + 1), col(3), A.add, 64.0 * a, A.add)
+        else:
+            tt(B("ub"), B("ud"), whole("I4"), A.add)
+            cp(B("c16"), B("ub"))
+        mms(([] if PAR["KF"] else grp(Q("K"), (sl("ID"), hi), (sl("ID"), lo))) +
+            (grp(Q("lin"), (whole("W37"), z), (whole("W37"), z), (sl("ID64"), hi), (sl("ID64"), lo)) if PAR["LB"] else
+             grp(Q("lin"), (whole("W37"), z), (sl("ID2"), hi), (sl("ID2"), lo))))
+        if not PAR["KF"]:
+            ts(B("K16"), Q("K"), -96 - V0, A.add)
+        if PAR["LB"]:
+            cp(B("la"), Q("lin"))
+        if not PAR["KF"]:
+            act(B("Kf"), Q("K"), AF.Copy, bias=-64 - V0)
+        if PAR["LB"]:
+            ts(B("lb"), B("la"), 131071, A.bitwise_and)
+        tt(B("p1"), ("Gf", wa, wb, 1, B("c16")), B("Kf"), A.mult)
+        if PAR["LB"]:
+            tt(B("s1"), B("p1"), B("lb"), A.add)
+        else:
+            ts(B("lb"), B("p1"), 5, A.arith_shift_right)
+            tt(B("s1"), B("lb"), Q("lin"), A.add)
+        if PAR["LB"]:
+            ts(B("s2"), B("s1"), 5, A.arith_shift_right, 4095, A.bitwise_and)
+        else:
+            ts(B("s2"), B("s1"), 4095, A.bitwise_and)
         cp(B("s16"), B("s2"))
-        for j in range(4):
-            o, w = B("x", 512 * j, 512 * j + 512), ("X", 0, 4096, 1, B("K16", 32 * j, 32 * j + 32))
+        for j, (a, b) in enumerate(cut(PAR["XP"])):
+            o, w = B("x", 16 * a, 16 * b), ("X", 0, 4096, 1, B("K16", a, b))
             if j in PAR["XV"]:
                 cp(o, w)
             else:
                 act(o, w, AF.Copy)
-        act(B("Wo"), ("Wf", wa, wb, 1, B("c16")), AF.Copy)
-        tt(B("dk"), B("Wo"), P(pb, 2), A.subtract)
-        if last:
-            act(("Wout", wa, wb, 1), ("Wf", wa, wb, 1), AF.Copy, bias=-V0)
-            act(B("Wp"), B("Wo"), AF.Copy, bias=-V0)
-        for j in range(4):
-            o = B("d", 512 * j, 512 * j + 512)
-            tt(o, ("Y", 0, 4096, 1, B("s16", 32 * j, 32 * j + 32)), B("x", 512 * j, 512 * j + 512), A.subtract)
-            act(o, o, AF.Abs)
+        act(B("Wo"), ("Wf", wa, wb, 1, B("c16")), AF.Copy, bias=V0)
+        for j, (a, b) in enumerate(cut(PAR["YP"])):
+            o, w, x = B("d", 16 * a, 16 * b), ("Y", 0, 4096, 1, B("s16", a, b)), B("x", 16 * a, 16 * b)
+            if (j, c) in PAR["YS"]:
+                act(o, w, AF.Copy)
+                mms(grp(Q("yx", 0, (b - a) // 4), (sl("NID"), x), (sl("ID"), o)))
+                act(o, Q("yx", 0, (b - a) // 4), AF.Abs)
+            else:
+                tt(o, w, x, A.subtract)
+                act(o, o, AF.Abs)
+        for j in range(4 if PAR["E4"] else 0):
+            for k in range(4 * j, 4 * j + 4, 2):
+                mms([m for k2 in (k, k + 1) for m in grp(P(j % 2, k2 % 4), (sl("NID"), z), (sl("ID"), B("x", k2, 16 * R, 16)))])
+            for k in range(4 * j, 4 * j + 4, 2):
+                act(B("sg", R * k, R * k + 2 * R), P(j % 2, k % 4, 2), AF.Sign, bias=0.5 - 16.0 * (7 - k // 2))
             if j % 2:
-                a = 512 * j - 512
-                mm(("ps%d" % pb, 384 + a // 16, 448 + a // 16, 1), *[(row("Z1", k), B("d", a + k, a + 1024, 16)) for k in range(16)])
-        for j in range(4):
-            for k in range(4 * j, 4 * j + 4, 2):
-                mms([m for k2 in (k, k + 1) for m in ((P(j % 2, k2 % 4), sl("NID"), z, True, False),
-                                                      (P(j % 2, k2 % 4), sl("ID"), B("x", k2, 2048, 16), False, True))])
-            for k in range(4 * j, 4 * j + 4, 2):
-                act(B("sg", 128 * k, 128 * k + 256), P(j % 2, k % 4, 256), AF.Sign, bias=0.5 - 16.0 * (7 - k // 2))
-            mms([(("ps%d" % pa, 128 + k, 256, 16), B("sg", 128 * k, 128 * k + 128), bd8, True, True) for k in range(4 * j, 4 * j + 4)])
-        act(B("cs"), P(pa, 1), AF.Sign, bias=-1.0)
+                mms([(sub(Q("cnt"), k, 128, (16, R)), B("sg", R * k, R * k + R), bd8, True, True) for k in range(4 * j - 4, 4 * j + 4)])
+        cs = sub(B("cs"), 0, 128, (1, R))
+        act(cs, sub(Q("cnt"), 0, 128, (1, R)), AF.Sign, bias=-1.0)
         un, ta = B("un"), B("ta")
-        act(un, P(pb, 3), AF.Sign, bias=col(11 if first else 12), accum=("Fs", 2 * c, 2 * c + 1, 1))
-        mm(P(pa, 2), (B("cs"), sl("ID")), (sl("NID"), un))
-        act(B("hd"), P(pa, 2), AF.Relu, bias=-1.0)
-        mm(P(pb, 0), (sl("TEo"), un))
-        act(B("EE", 0, 128), P(pb, 0), AF.Exp, bias=col(1), scale=ln2)
-        mm(P(pa, 3), (sl("IDm16"), un), (sl("TGE"), B("hd")))
-        act(ta, P(pa, 3), AF.Sign, bias=-16.0, accum=("Fs", 2 * c + 1, 2 * c + 2, 1))
-        mm(P(pa, 0), (sl("TFo"), un), (sl("IDm256"), ta))
-        mm(P(pa, 1), (sl("THo"), un), (sl("THt"), ta))
-        mm(P(pb, 1), (sl("Cm192"), sl("ones")), (sl("ID2"), hi), (sl("ID2"), lo), (sl("ID16k"), un), (sl("ID16k"), ta))
-        mm(P(pb, 2), (sl("NID"), un), (sl("NID"), ta))
-        act(B("EE", 128, 256), P(pa, 0), AF.Exp, bias=col(2), scale=ln2)
-        act(B("EE", 256, 384), P(pa, 1), AF.Exp, bias=col(3), scale=ln2)
-        tt(B("val"), B("Wo"), P(pb, 1), A.max)
-        mm(P(pa, 2), *[(sl("ID"), B("EE", 128 * j, 128 * j + 128)) for j in range(3)])
-        tt(P(pa, 3), B("val"), P(pa, 2), A.mult)
-        ts(B("WW", 0, 128), P(pa, 3), 0.98, A.mult)
-        tt(B("WW", 128, 256), P(pa, 3), B("WW", 0, 128), A.subtract)
-        tt(B("dl"), B("dk"), P(pb, 2), A.mult)
-        if c == 1 and not last:
-            fp = ("ps%d" % pb, 0, 4, 1)
-            mm(fp, (whole("ONE16"), whole("Fs")))
-            add("V", .1, lambda: V.tensor_reduce(ap(whole("Ff")), ap(fp), AxisListType.X, A.add), (fp,), (whole("Ff"),))
-            cp(whole("Fi"), whole("Ff"))
+        mms(grp(Q("D"), *[(row("Z1", k), B("d", k, 16 * R, 16)) for k in range(16)]))
+        act(un, Q("D"), AF.Sign, bias=thr, accum=("Fs", c, c + 1, 1))
+        mms(grp(Q("hd"), (cs, sub(sl("ID"), 0, R, (1, R))), (sl("NID"), un)))
+        act(B("hd"), Q("hd"), AF.Relu, bias=-1.0)
+        mms(grp(Q("F"), (sl("IDm16"), un), (sl("TGE"), B("hd"))))
+        act(ta, Q("F"), AF.Sign, bias=-16.0, accum=("Fs", NC + c, NC + c + 1, 1))
+        mms(grp(Q("ex", 0), (sl("DF"), ones), (sl("TFo"), un), (sl("IDm256"), ta)) + grp(Q("ex", 1), (sl("THo"), un), (sl("THt"), ta)) +
+            grp(Q("ex", 2), (sl("DO"), ones), (sl("TEo"), un)))
+        mms(grp(Q("val"), (sl("Cval"), ones), (sl("ID2"), hi), (sl("ID2"), lo), (sl("IDbig"), un), (sl("IDbig"), ta)) +
+            grp(Q("new"), (sl("Cnew"), ones), (sl("ID"), hi), (sl("ID"), lo), (sl("IDbig"), un), (sl("IDbig"), ta)))
+        count = c == NC - 1 and not last
+        if count:
+            part, fa = ("Fs", 0, 2 * NC - 1, 1), sub(Q("A"), 0, 1)
+            add("V", .06, lambda: V.tensor_reduce(ap(whole("Ff")), ap(part), AxisListType.X, A.add), (part,), (whole("Ff"),))
+            mms(grp(fa, (whole("ONE16"), whole("Ff")), (whole("ONE16"), ("Fs", 2 * NC - 1, 2 * NC, 1))))
+        if PAR["VF"]:
+            tt(B("val"), B("Wo"), Q("val"), A.max)
+        act(B("EE"), Q("ex", 0, 3), AF.Exp, bias=col(22), scale=ln2)
+        mms(grp(Q("E"), *[(sl("ID"), B("EE", R * j, R * j + R)) for j in range(3)]) +
+            grp(Q("E98"), *[(sl("ID98"), B("EE", R * j, R * j + R)) for j in range(3)]))
+        if not PAR["VF"]:
+            tt(B("val"), B("Wo"), Q("val"), A.max)
+        if count:
+            cp(whole("Fi"), fa)
             ts(whole("Fj"), whole("Fi"), 511, A.bitwise_and)
             ts(col(12), whole("Fj"), -1.0, A.mult, col(11), A.add)
-        R1 = P(pa, 0, 256)
+        tt(B("nw"), B("Wo"), Q("new"), A.min)
+        tt(B("WW", 0, R), B("val"), Q("E98"), A.mult)
+        tt(Q("V"), B("val"), Q("E"), A.mult)
+        tt(B("WW", R, 2 * R), Q("V"), B("WW", 0, R), A.subtract)
+        pair = Q("pair", 0, 2)
         for a in range(8):
             u = 2.0 ** (14 * a - 56)
-            ts(B("CL", 256 * a, 256 * a + 256), B("WW"), 64 * u, A.max, u * 2 ** 20, A.min)
+            ts(B("CL", 2 * R * a, 2 * R * a + 2 * R), B("WW"), 64 * u, A.max, u * 2 ** 20, A.min)
             if a % 2:
-                mms(([(R1, sl("CQ"), whole("CT"), True, False)] if a == 1 else []) +
-                    [(R1, ("PQ", 128 * b, 128 * b + 128, 1), B("CL", 256 * b, 256 * b + 256), False, b == 7) for b in (a - 1, a)])
-        act(B("tq", 0, 128), P(pa, 0), AF.Identity, bias=col(4), scale=col(6))
-        act(B("tq", 128, 256), P(pa, 1), AF.Identity, bias=col(5), scale=col(6))
-        nh, nl = ("HS", hi[1], hi[2], 1), ("HS", lo[1], lo[2], 1)
-        tt(("HS", hi[1], lo[2], 1), B("tq"), R1, A.add)
-
-        def send(src, to, sem):
-            return add("G", 0.6, lambda: g.remote_dma(out_ap=ap(to), in_ap=ap(src), remote_sem=T.sem[sem], local_sem=T.sem.loc,
-                                                      pid=pid, routing_id=rid, dma_engine_mask=emask), (src,), (), kind="s")
-
-        def store(out, src, s):
-            add("Y", .1, lambda: SY.dma_start(out, ap(src)), (src,), (), kind="d", sem="st%d" % s, val=16, lat=2.3)
-        if not last:
-            sh = send(("HS", hi[1], lo[2], 1), ("HL", hi[1] + 512, lo[2] + 512, 1), "ah%d_%d" % (e + 1, c))
-        else:
-            mm(P(pa, 2), (sl("ID"), nh), (sl("ID"), nl))
-            act(("YK", 128 * c, 128 * c + 128, 1), P(pa, 2), AF.Copy, bias=-96 - V0)
-            store(T.yk[:, 128 * c:128 * c + 128], ("YK", 128 * c, 128 * c + 128, 1), c)
-        if not last:
-            tt(("Wf", wa, wb, 1, B("c16")), B("Wo"), B("dl"), A.subtract)
-        else:
-            tt(("Wout", wa, wb, 1, B("c16")), B("Wp"), B("dl"), A.subtract)
-            store(T.yw[:, wa:wb], ("Wout", wa, wb, 1), 2 + c)
+                mms(([(pair, sl("CQ"), whole("CT"), True, False)] if a == 1 else []) +
+                    [(pair, ("PQ", 128 * b, 128 * b + 128, 1), B("CL", 2 * R * b, 2 * R * b + 2 * R), False, b == 7) for b in (a - 1, a)])
+        for j in range(2):
+            if PAR["TV"]:
+                ts(B("tq", R * j, R * j + R), Q("pair", j), col(6), A.mult, col(4 + j), A.add)
+            else:
+                act(B("tq", R * j, R * j + R), Q("pair", j), AF.Identity, bias=col(4 + j), scale=col(6))
+        hs, nz = ("HS",) + hl[1:], ("HS",) + z[1:]
+        tt(hs, B("tq"), pair, A.add)
+        if not last and c not in PAR["ONE"]:
+            send(hs, "ah%d_%d" % (e + 1, c))
+        elif last:
+            mms(grp(Q("yk"), (sl("ID"), sub(hs, 0, R)), (sl("ID"), sub(hs, R, 2 * R))))
+            act(("YK", r0, r0 + R, 1), Q("yk"), AF.Copy, bias=-96 - V0)
+            store(T.yk[:, r0:r0 + R], ("YK", r0, r0 + R, 1), 0)
+        act(B("gw"), ta, AF.Abs, scale=V0)
+        tt(("Wf", wa, wb, 1, B("c16")), B("nw"), B("gw"), A.subtract)
+        if last:
+            store(T.yw[:, wa:wb], ("Wf", wa, wb, 1), 1)
         for j in range(4):
             b = 2 + j % 2
-            for k in range(4 * j, 4 * j + 4, 2):
-                mms([m for k2 in (k, k + 1) for m in ((P(b, k2 % 4), sl("ID"), B("x", k2, 2048, 16), True, False),
-                                                      (P(b, k2 % 4), ("L2", 128 * k2, 128 * k2 + 128, 1), ta, False, True))])
-            for h in range(2):
-                if j == 0 and h == 0:
-                    ts(B("AC"), P(b, 0, 256), 256.0, A.max)
-                else:
-                    tt(B("AC"), B("AC"), P(b, 2 * h, 256), A.max)
-        tt(B("mz"), B("AC", 0, 128), B("AC", 128, 256), A.max)
-        mm(P(pb, 3), (sl("ID"), z), (sl("NID"), B("mz")))
-        nz = ("ZS", z[1], z[2], 1)
-        act(nz, P(pb, 3), AF.Abs, bias=256.0)
-        if not last:
-            sends[(e, c)] = (sh, send(nz, ("ZL", z[1] + 256, z[2] + 256, 1), "az%d_%d" % (e + 1, c)))
+            for k0 in (4 * j, 4 * j + 2):
+                mms([m for k in (k0, k0 + 1) for m in grp(P(b, k % 4), (sl("ID"), B("x", k, 16 * R, 16)),
+                                                          (("L2", 128 * k, 128 * k + 128, 1), ta))])
+            if PAR["MG"] == 2:
+                for h in range(2):
+                    if j == 0 and h == 0:
+                        ts(B("AC", 0, 2 * R), P(b, 0, 2), 256.0, A.max)
+                    else:
+                        tt(B("AC", 0, 2 * R), B("AC", 0, 2 * R), P(b, 2 * h, 2), A.max)
+            elif j == 0:
+                ts(B("AC"), P(b, 0, 4), 256.0, A.max)
+            elif j < 3:
+                tt(B("AC"), B("AC"), P(b, 0, 4), A.max)
+        if PAR["MG"] == 2:
+            tt(B("mz"), B("AC", 0, R), B("AC", R, 2 * R), A.max)
+        elif PAR["MG"]:
+            tt(Q("m", 0, 2), B("AC", 0, 2 * R), P(3, 0, 2), A.max)
+            tt(B("AC", 2 * R, 4 * R), B("AC", 2 * R, 4 * R), P(3, 2, 2), A.max)
+            tt(Q("m"), B("AC", 2 * R, 3 * R), Q("m"), A.max)
+            tt(B("AC", 3 * R, 4 * R), B("AC", 3 * R, 4 * R), Q("m", 1), A.max)
+            tt(B("mz"), B("AC", 3 * R, 4 * R), Q("m"), A.max)
         else:
-            store(T.yz[:, 128 * c:128 * c + 128], nz, 4 + c)
+            tt(P(3, 0, 2), B("AC", 0, 2 * R), P(3, 0, 2), A.max)
+            tt(B("AC", 2 * R, 4 * R), B("AC", 2 * R, 4 * R), P(3, 2, 2), A.max)
+            tt(B("AC", 0, 2 * R), B("AC", 2 * R, 4 * R), P(3, 0, 2), A.max)
+            tt(B("mz"), B("AC", 0, R), B("AC", R, 2 * R), A.max)
+        mms(grp(Q("z"), (sl("ID"), z), (sl("NID"), B("mz"))))
+        act(nz, Q("z"), AF.Abs, bias=256.0)
+        if not last:
+            send(("HS",) + land[1:] if c in PAR["ONE"] else nz, "az%d_%d" % (e + 1, c))
+        else:
+            store(T.yz[:, r0:r0 + R], nz, 2)
 
     for e in range(LE):
-        for c in range(2):
-            cur[0] = 2 * e + c
+        for c in range(NC):
+            cur[0] = NC * e + c
             lead(e, c)
 
     if "o" not in _ORDER:
         _ORDER["o"] = schedule(ops)
-    count = {"V": 0, "S": 0, "T": 0, "G": 0}
+    place = {"V": 0, "S": 0, "T": 0, "G": 0}
     known = {q: {} for q in QS}
-    nsend = 0
     for i in _ORDER["o"]:
         o = ops[i]
         q = o["q"]
         if o["kind"] == "r":
             o["clk"] = {o["sem"]: o["val"]}
             continue
-        kn = known[q]
-        for j in sorted((j for j, w in o["deps"].items() if w), reverse=True):
+        kn, o["wait"] = known[q], {}
+        for j in sorted((j for j, w in o["deps"].items() if w), key=lambda j: -ops[j].get("pos", 1 << 30)):
             p = ops[j]
             sem, val = (p["sem"], p["val"]) if p["kind"] != "c" else ("e" + p["q"], p["pos"])
             if kn.get(sem, 0) < val:
-                QS[q].wait_ge(T.sem[sem], val)
+                o["wait"][sem] = p
+                p["seen"] = True
                 for s2, v2 in p["clk"].items():
                     if kn.get(s2, 0) < v2:
                         kn[s2] = v2
-        ins = o["emit"]()
-        clk = dict(kn)
+        o["clk"] = dict(kn)
         if o["kind"] == "c":
-            count[q] += 1
-            o["pos"] = count[q]
-            ins.then_inc(T.sem["e" + q], 1)
-            clk["e" + q] = count[q]
+            place[q] += 1
+            o["pos"] = o["clk"]["e" + q] = place[q]
+        elif o["kind"] == "d":
+            o["clk"][o["sem"]] = o["val"]
+    count = {"V": 0, "S": 0, "T": 0, "G": 0}
+    nsend = 0
+    for i in _ORDER["o"]:
+        o = ops[i]
+        q = o["q"]
+        if o["kind"] == "r":
+            continue
+        for sem, p in o["wait"].items():
+            QS[q].wait_ge(T.sem[sem], p["val"])
+        ins = o["emit"]()
+        if o["kind"] == "c":
+            if "seen" in o or o["pos"] == place[q]:
+                count[q] += 1
+                o["val"] = count[q]
+                ins.then_inc(T.sem["e" + q], 1)
         elif o["kind"] == "d":
             ins.then_inc(T.sem[o["sem"]], 16)
-            clk[o["sem"]] = o["val"]
         else:
             nsend += 1
-        o["clk"] = clk
     kn = known["Y"]
     for q in ("V", "S", "T", "G"):
         SY.wait_ge(T.sem["e" + q], count[q])
@@ -463,33 +527,32 @@ def rank_program(g, core, T, topo):
 
 
 def schedule(ops):
-    n, HOP = len(ops), PAR["HOP"]
-    pred = [[(j, HOP if w or ops[j]["q"] != o["q"] else 0.0) for j, w in o["deps"].items()] for o in ops]
+    n = len(ops)
+    pred = [[(j, PAR["HOP"] if ops[j]["q"] != o["q"] else PAR["HOPS"] if w else 0.0) for j, w in o["deps"].items()] for o in ops]
     succ = [[] for _ in range(n)]
     for i in range(n):
         for j, h in pred[i]:
             succ[j].append((i, h))
 
-    def run(nxt, prv, prio, back):
+    def run(nxt, prv, prio, back, look=0.0):
         cnt = [len(p) for p in prv]
-        ready, free, cand, start, order = [0.0] * n, {}, {}, [0.0] * n, []
+        ready, free, cand, fin, order = [0.0] * n, {}, {}, [0.0] * n, []
         for i in range(n):
             if cnt[i] == 0:
                 ready[i] = ops[i]["lat"] if back else 0.0
                 cand.setdefault(ops[i]["q"], []).append(i)
         end_all = 0.0
         while len(order) < n:
-            best = None
-            for q, lst in cand.items():
-                if lst:
-                    st = max(free.get(q, 0.0), min(ready[i] for i in lst))
-                    if best is None or st < best[0]:
-                        best = (st, q)
-            st, q = best
-            i = max((i for i in cand[q] if ready[i] <= st + PAR["WIN"]), key=lambda i: (prio[i], -i))
+            st, q = min((max(free.get(q, 0.0), min(ready[i] for i in lst)), q) for q, lst in cand.items() if lst)
+            i = max((i for i in cand[q] if ready[i] <= st + 0.02), key=lambda i: (prio[i], -i))
+            soon = [j for j in cand[q] if st < ready[j] < st + ops[i]["dur"] and prio[j] > prio[i]]
+            if soon and look:
+                j = max(soon, key=lambda j: (prio[j], -j))
+                if max(ready[j] + prio[j], ready[j] + ops[j]["dur"] + prio[i]) < st + ops[i]["dur"] + prio[j] - look:
+                    fit = [k for k in cand[q] if ready[k] <= st and st + ops[k]["dur"] <= ready[j] + look]
+                    i = max(fit, key=lambda k: (prio[k], -k)) if fit else j
             cand[q].remove(i)
-            start[i] = max(free.get(q, 0.0), ready[i])
-            end = start[i] + ops[i]["dur"]
+            end = fin[i] = max(free.get(q, 0.0), ready[i]) + ops[i]["dur"]
             if q != "R":
                 free[q] = end
             if not back:
@@ -501,20 +564,35 @@ def schedule(ops):
                 cnt[k] -= 1
                 if cnt[k] == 0:
                     cand.setdefault(ops[k]["q"], []).append(k)
-        return end_all, order, [start[i] + ops[i]["dur"] for i in range(n)]
+        return end_all, order, fin
 
-    loc, prio = [0.0] * n, [0.0] * n
-    for i in range(n - 1, -1, -1):
-        gp, d = ops[i]["grp"], ops[i]["dur"] + ops[i]["lat"]
-        loc[i] = d + max([loc[k] + h for k, h in succ[i] if ops[k]["grp"] == gp] + [0.0])
-        if gp >= 0:
-            prio[i] = loc[i] - (gp // 2) * PAR["T"] - (gp % 2) * PAR["S"]
-        else:
-            prio[i] = d + max([prio[k] + h for k, h in succ[i]] + [-99.0])
-    best = cur = run(succ, pred, prio, False)
-    for _ in range(PAR["PASS"]):
-        cur = run(succ, pred, run(pred, succ, cur[2], True)[2], False)
-        if cur[0] < best[0]:
-            best = cur
-    _ORDER["est"] = best[0]
+    def replay(order, speed, far=1.0):
+        free, end = {}, [0.0] * n
+        for i in order:
+            o = ops[i]
+            t = max([end[j] + h for j, h in pred[i]] + [free.get(o["q"], 0.0)]) + o[speed]
+            if o["q"] != "R":
+                free[o["q"]] = t
+            end[i] = t + o["lat"] * (far if o["grp"] >= 0 else 1.0)
+        return max(end)
+
+    best = None
+    for skew in PAR["S"]:
+        loc, prio = [0.0] * n, [0.0] * n
+        for i in range(n - 1, -1, -1):
+            gp, d = ops[i]["grp"], ops[i]["dur"] + ops[i]["lat"]
+            loc[i] = d + max([loc[k] + h for k, h in succ[i] if ops[k]["grp"] == gp] + [0.0])
+            if gp >= 0:
+                prio[i] = loc[i] - (gp // NC) * PAR["T"] - (gp % NC) * skew
+            else:
+                prio[i] = d + max([prio[k] + h for k, h in succ[i]] + [-99.0])
+        for look in PAR["LOOK"]:
+            cur = run(succ, pred, prio, False)
+            for _ in range(PAR["PASS"]):
+                cur = run(succ, pred, run(pred, succ, cur[2], True, look)[2], False, look)
+                score = replay(cur[1], "fast") + replay(cur[1], "slow") / 1.5 + PAR["FAR"] * replay(cur[1], "fast", 1.8)
+                if best is None or score < best[0]:
+                    best = (score, cur[1], cur[0])
+    _ORDER["est"] = best[2]
+    _ORDER["ops"] = ops
     return best[1]

import math
from concourse.mybir import AluOpType, AxisListType, ActivationFunctionType

A = AluOpType
AF = ActivationFunctionType
LE, NC, R = 6, 4, 64
V0 = 4192.0
BIG = 16192.0
SLOTS = ["ones", "BD0", "BD", "ID", "NID", "ID2", "ID64", "ID98", "IDm16", "IDm256", "IDbig", "Cval", "Cnew", "TGE", "SLT", "SGT",
         "SH", "SL", "TEo", "TFo", "THt", "THo", "CQ", "DF", "DO", "t0", "t1", "t2", "t3", "t4", "t5"]

SCRATCH = {
    "X": ("sbuf", [128, 4096], "bfloat16"), "Y": ("sbuf", [128, 4096], "bfloat16"),
    "Gf": ("sbuf", [128, 1024], "float32"), "Wf": ("sbuf", [128, 1024], "float32"),
    "rti": ("sbuf", [128, 1024], "int32"), "wri": ("sbuf", [128, 1024], "int32"), "rki": ("sbuf", [128, 256], "int32"),
    "thi": ("sbuf", [128, 1], "int32"), "wtb": ("sbuf", [128, 1], "bfloat16"),
    "HL": ("sbuf", [128, LE * 768], "bfloat16"), "HS": ("sbuf", [128, LE * 768], "bfloat16"),
    "TB": ("sbuf", [128, 128 * len(SLOTS)], "bfloat16"), "ONE16": ("sbuf", [128, 128], "float32"),
    "Z1": ("sbuf", [128, 144], "bfloat16"), "Z2": ("sbuf", [128, 144], "bfloat16"), "WZ": ("sbuf", [128, 144], "bfloat16"),
    "L2": ("sbuf", [128, 2048], "bfloat16"), "PQ": ("sbuf", [128, 1024], "bfloat16"), "CT": ("sbuf", [128, 128], "bfloat16"),
    "W37": ("sbuf", [128, 128], "float16"), "COL": ("sbuf", [128, 24], "float32"), "rowi": ("sbuf", [128, 4], "int32"),
    "I4a": ("sbuf", [128, 4], "int32"), "I4": ("sbuf", [128, 4], "int32"), "Fs": ("sbuf", [128, 8], "float32"), "Ff": ("sbuf", [128, 1], "float32"),
    "Fi": ("sbuf", [128, 1], "int32"), "Fj": ("sbuf", [128, 1], "int32"),
    "YK": ("sbuf", [128, 256], "float32"), "hI": ("sbuf", [128, 256], "int32"), "lI": ("sbuf", [128, 256], "int32"),
}
PER_RACK = {"K16": (1, "uint16"), "s16": (1, "uint16"), "x": (16, "bfloat16"), "d": (16, "bfloat16"), "sg": (16, "bfloat16"),
            "Kf": (1, "float32"), "Wo": (1, "float32"), "Tc": (1, "float32"), "gw": (1, "float32"), "nw": (1, "float32"),
            "val": (1, "float32"), "p1": (1, "int32"), "la": (1, "int32"), "lb": (1, "int32"), "s1": (1, "int32"), "s2": (1, "int32"),
            "un": (1, "bfloat16"), "hd": (1, "bfloat16"), "ta": (1, "bfloat16"), "cs": (2, "bfloat16"), "EE": (3, "bfloat16"),
            "WW": (2, "bfloat16"), "CL": (16, "bfloat16"), "tq": (2, "bfloat16"), "AC": (4, "float16"), "mz": (1, "float16")}
for _n, (_w, _d) in PER_RACK.items():
    SCRATCH[_n] = ("sbuf", [128, 256 * _w], _d)
for _n in ("ua", "ub", "uc", "ud", "c16"):
    SCRATCH[_n] = ("sbuf", [128, 16], "uint16" if _n == "c16" else "int32")
for _b in range(8):
    SCRATCH["ps%d" % _b] = ("psum", [128, 512], "float32")
TABLES = ("TB", "Z1", "WZ", "L2", "PQ", "W37", "CT", "X", "Y", "Gf", "ONE16", "I4")

SEMAPHORES = ["eV", "eS", "eT", "eG", "loc"] + ["ld%d" % _i for _i in range(18)] + ["st%d" % _i for _i in range(3 * NC)]
for _e in range(1, LE):
    for _c in range(NC):
        SEMAPHORES += ["ah%d_%d" % (_e, _c), "az%d_%d" % (_e, _c)]

PLACE = {"u": (None, 0), "K": (None, 1), "lin": (None, 2), "yx": (None, 0), "cnt": (1, 6), "D": (None, 4), "hd": (None, 7), "F": (None, 6), "ex": (None, 0),
         "E": (None, 5), "E98": (None, 6), "V": (None, 0), "pair": (None, 6), "yk": (None, 0),
         "val": (None, 3), "new": (None, 4), "A": (None, 7), "m": (2, 4), "z": (3, 6)}

PAR = {"CY": 0.83e-3, "TC": 0.42e-3, "GAT": 1.3, "SCA": 2.8, "GO": 0.06, "OV": 0.005, "HOP": 0.26, "HOPS": 0.2, "ISS": 0.4, "REM": 3.5,
       "BW": 0.26, "T": 20, "S": (2, 3, 4, 5, 6), "LOOK": (0, .3), "PASS": 5, "XP": (32, 32), "YP": (32, 32), "XV": (), "EP": 2,
       "CP": 1, "TV": 0, "YS": (), "TS": 1, "C4": 0, "LB": 0, "MIX": 0.1, "GS": 1.15, "VF": 0, "MG": 2, "KF": 1, "E4": 1, "ONE": (), "FAR": 0.3}
_ORDER = {}


def rank_program(g, core, T, topo):
    rank = T.rank_of(core)
    if rank is None:
        return
    cores = list(T.cores)
    dst = cores[(rank + 1) % len(cores)]
    rid, pid, _s = topo.addr(dst)
    emask = topo.mask(core, dst)
    neng = len(topo.engines(core, dst))
    V, S, TE, SY = g.vector, g.scalar, g.tensor, g.sync
    QS = {"V": V, "S": S, "T": TE, "G": g, "Y": SY}
    CY = PAR["CY"]
    ops, acc, cur = [], {}, [-1]

    def ap(o):
        if not isinstance(o, tuple):
            return o
        st, n = o[3] if isinstance(o[3], tuple) else (o[3], 128)
        a = T[o[0]][0:n, o[1]:o[2]:st] if st != 1 else T[o[0]][0:n, o[1]:o[2]]
        return a.indirect(ap(o[4])) if len(o) > 4 else a

    def width(o):
        return 16 * width(o[4]) if len(o) > 4 else len(range(o[1], o[2], o[3][0] if isinstance(o[3], tuple) else o[3]))

    def sub(o, a, b, st=1):
        return (o[0], o[1] + a, o[1] + b, st)

    def add(q, dur, emit, reads=(), writes=(), kind="c", sem=None, val=0, lat=0.0, extra=()):
        i = len(ops)
        deps = {j: False for j in extra}
        reads = [o for o in reads if isinstance(o, tuple)]
        reads += [o[4] for o in list(reads) + list(writes) if len(o) > 4]
        for isw, regs in ((False, reads), (True, writes)):
            for o in regs:
                buf, lo, hi = o[0], o[1], o[2]
                if cur[0] >= 0 and buf in TABLES:
                    deps.update((a[0], True) for a in acc[buf] if a[3] and a[1] < hi and lo < a[2])
                    continue
                keep = []
                for a in acc.get(buf, []):
                    j, l, h, aw = a
                    if j == i:
                        keep.append(a)
                        continue
                    over = l < hi and lo < h
                    same = ops[j]["q"] == q and ops[j]["kind"] == "c" and kind == "c"
                    if buf[:2] == "ps":
                        deps[j] = deps.get(j, False) or not same or (over and (aw or isw) and q != "T")
                        if not same or q == "T" or (isw and l >= lo and h <= hi):
                            continue
                    else:
                        if over and (isw or aw):
                            deps[j] = True
                        if isw and l >= lo and h <= hi:
                            continue
                    keep.append(a)
                keep.append((i, lo, hi, isw))
                acc[buf] = keep
        slow = 1.5 * dur * (PAR["GS"] if any(len(o) > 4 for o in list(reads) + list(writes)) else 1.0)
        ops.append({"q": q, "fast": dur, "slow": slow, "dur": dur + PAR["MIX"] * (slow - dur), "emit": emit, "deps": deps, "kind": kind, "sem": sem, "val": val, "lat": lat, "grp": cur[0]})
        return i

    def two(o):
        return SCRATCH[o[0]][2] in ("bfloat16", "float16", "uint16")

    def cyc(out, a, rate):
        if len(out) > 4 or len(a) > 4:
            return PAR["GO"] + width(out) * PAR["SCA" if len(out) > 4 else "GAT"] * CY
        return PAR["OV"] + max(64, width(out) * rate) * CY

    def ts(out, in0, s1, op0, s2=None, op1=None):
        def f():
            if op1 is None:
                return V.tensor_scalar(ap(out), ap(in0), ap(s1), None, op0)
            return V.tensor_scalar(ap(out), ap(in0), ap(s1), ap(s2), op0, op1)
        return add("V", cyc(out, in0, .5 if two(out) and two(in0) else 1), f, (in0, s1, s2), (out,))

    def tt(out, a, b, op):
        r = 1 if "ps" in (a[0][:2], b[0][:2]) else 2
        return add("V", cyc(out, a, r), lambda: V.tensor_tensor(ap(out), ap(a), ap(b), op), (a, b), (out,))

    def cp(out, a):
        return add("V", cyc(out, a, .5 if two(out) and two(a) else 1), lambda: V.tensor_copy(ap(out), ap(a)), (a,), (out,))

    def fill(out, v):
        return add("V", cyc(out, out, .5 if two(out) else 1), lambda: V.memset(ap(out), v), (), (out,))

    def act(out, a, fn, bias=0.0, scale=1.0, accum=None):
        def f():
            if accum is None:
                return S.activation(ap(out), ap(a), fn, bias=ap(bias), scale=ap(scale))
            return S.activation(ap(out), ap(a), fn, bias=ap(bias), scale=ap(scale), accum_out=ap(accum))
        return add("S", cyc(out, a, 1), f, (a, bias, scale), (out,) if accum is None else (out, accum))

    def mms(lst):
        def f():
            for o, l, r, a, b in lst:
                i = TE.matmul(ap(o), ap(l), ap(r), a, b)
            return i
        dur = sum(max(64, width(r)) * PAR["TC"] * (1 if two(r) else 4) for o, l, r, a, b in lst)
        return add("T", dur, f, [x for m in lst for x in m[1:3]], [m[0] for m in lst])

    def grp(out, *terms):
        return [(out, l, r, j == 0, j == len(terms) - 1) for j, (l, r) in enumerate(terms)]

    def sl(n):
        s = SLOTS.index(n)
        return ("TB", 128 * s, 128 * s + 128, 1)

    def col(i):
        return ("COL", i, i + 1, 1)

    def whole(n):
        return (n, 0, SCRATCH[n][1][1], 1)

    clock = [0, 2.0]

    def load(q, reg, src):
        s = "ld%d" % clock[0]
        clock[0] += 1
        clock[1] += width(reg) * (2 if two(reg) else 4) * 128e-6 / PAR["BW"]
        QS[q].dma_start(ap(reg), src).then_inc(T.sem[s], 16)
        add("R", 0, None, (), (reg,), kind="r", sem=s, val=16, lat=clock[1])

    load("S", whole("wtb"), T.wt[:, :])
    for c in range(NC):
        load("S", ("HL", 3 * R * c + 2 * R, 3 * R * c + 3 * R, 1), T.z0[:, R * c:R * c + R])
    load("Y", whole("rki"), T.rk[:, :])
    load("Y", whole("X"), T.gx[:, :])
    load("Y", ("rti", 0, 4 * R, 1), T.rt[:, 0:4 * R])
    load("Y", ("Y", 320, 4096, 1), T.sy[:, 0:3776])
    load("S", ("Y", 0, 320, 1), T.sy[:, 3776:4096])
    load("S", whole("thi"), T.th[:, :])
    for a in range(0, 1024, 4 * R):
        if a:
            load("Y", ("rti", a, a + 4 * R, 1), T.rt[:, a:a + 4 * R])
        load("Y", ("wri", a, a + 4 * R, 1), T.wr[:, a:a + 4 * R])

    def sel(o, i, pat, op, base, cm):
        add("G", .4, lambda: g.affine_select(ap(sl(o)), ap(sl(i)), pat, op, 0.0, base, cm), (sl(i),), (sl(o),))

    def lin(o, i, a, b):
        ts(col(o), col(i), float(a), A.mult, float(b), A.add)

    def scl(o, i, a):
        act(sl(o), sl(i), AF.Copy, scale=a)
    fill(sl("ones"), 1.0)
    add("G", .2, lambda: g.iota(T.rowi[:, 0:1], [[0, 1]], 0, 1), (), (("rowi", 0, 1, 1),))
    sel("ID", "ones", [[-1, 128]], A.is_equal, 0, 1)
    sel("BD0", "ones", [[-16, 8], [0, 16]], A.is_ge, 0, 1)
    sel("BD", "BD0", [[16, 8], [0, 16]], A.is_ge, 15, -1)
    sel("TGE", "BD", [[-1, 128]], A.is_ge, 0, 1)
    sel("SLT", "BD", [[1, 128]], A.is_ge, -1, -1)
    sel("SGT", "BD", [[-1, 128]], A.is_ge, -1, 1)
    sel("SH", "ones", [[1, 128]], A.is_equal, -1, -1)
    sel("SL", "ones", [[-1, 128]], A.is_equal, -1, 1)
    ts(("rowi", 1, 2, 1), ("rowi", 0, 1, 1), 15, A.bitwise_and)
    ts(("rowi", 2, 3, 1), ("rowi", 0, 1, 1), 1, A.bitwise_and)
    cp(col(0), ("rowi", 1, 2, 1))
    cp(col(1), ("rowi", 2, 3, 1))
    lin(2, 1, -1, 1)
    lin(3, 0, 4, 0)
    add("G", .2, lambda: g.iota(T.I4a[:, :], [[64, R // 16]], 0, 0), (), (whole("I4a"),))
    ts(whole("I4"), whole("I4a"), col(3), A.add)
    bd = sl("BD")
    bd8 = sub(bd, 0, 128, 16)
    fill(whole("Z1"), 0.0)
    cp(("Z1", 15, 143, 16), bd8)
    ts(whole("WZ"), whole("Z1"), whole("wtb"), A.mult)
    ts(col(7), whole("wtb"), 37.0, A.mult)
    ts(col(8), col(7), 2048.0, A.is_gt, -4096.0, A.mult)
    tt(col(9), col(7), col(8), A.add)
    ts(whole("W37"), bd, col(9), A.mult, 16.0 if PAR["LB"] else 1.0, A.mult)
    ts(whole("hI"), whole("rki"), 4064, A.bitwise_and)
    ts(whole("lI"), whole("rki"), 31, A.bitwise_and)
    for c in range(NC):
        ts(("HL", 3 * R * c, 3 * R * c + R, 1), ("hI", R * c, R * c + R, 1), 4096.0, A.add)
        ts(("HL", 3 * R * c + R, 3 * R * c + 2 * R, 1), ("lI", R * c, R * c + R, 1), 192.0, A.add)
    for a in range(0, 1024, 4 * R):
        ts(("Gf", a, a + 4 * R, 1), ("rti", a, a + 4 * R, 1), -64.0, A.add)
        cp(("Wf", a, a + 4 * R, 1), ("wri", a, a + 4 * R, 1))
    ts(col(11), whole("thi"), -1.0, A.mult, 0.5, A.add)
    for n, a in (("ID64", 64), ("NID", -1), ("ID2", 2), ("ID98", 251 / 256), ("IDm16", -16), ("IDm256", -256), ("IDbig", BIG),
                 ("Cval", -192), ("Cnew", BIG - 96 - V0)):
        scl(n, "ID", float(a))
    for n, t, a, tri, b in (("TEo", "t0", 124, "SGT", -3.5), ("TFo", "t1", -256, "SLT", -3.5), ("THt", "t2", 143, "SGT", 7.0),
                            ("THo", "t3", 71.5, "SGT", 3.5)):
        scl(t, tri, b)
        scl(n, "ID", float(a))
        tt(sl(n), sl(n), sl(t), A.add)
    lin(10, 0, 7, -236)
    scl("DF", "ID", col(10))
    lin(23, 0, 7, -52.5)
    scl("DO", "ID", col(23))
    lin(22, 0, -3.5 * math.log(2.0), -76 * math.log(2.0))
    lin(13, 0, 2 ** 20, -15 * 2 ** 20)
    ts(col(14), col(13), col(1), A.mult)
    ts(col(15), col(0), 14.0, A.is_lt, col(1), A.mult)
    lin(16, 0, -64, -64)
    ts(col(17), col(15), col(16), A.mult)
    ts(col(18), col(2), 4128.0, A.mult)
    scl("CQ", "ID", col(18))
    scl("t4", "SH", col(17))
    scl("t5", "SL", col(14))
    tt(sl("t4"), sl("t4"), sl("t5"), A.add)
    tt(sl("CQ"), sl("CQ"), sl("t4"), A.add)
    fill(("CT", 0, R, 1), 1.0)
    ts(("CT", R, 2 * R, 1), sub(sl("ones"), 0, R), col(2), A.add)
    lin(19, 0, 8191.5, .5 - 8192 * 15)
    for o, t, top, low in ((4, 20, -15.75, 6144.0), (5, 21, 64 - .9765625, 189.0)):
        ts(col(t), col(19), top - low, A.add)
        ts(col(o), col(t), col(1), A.mult, low, A.add)
    ts(col(6), col(1), 2.0 ** 23 + 1, A.mult, -1.0, A.add)
    fill(whole("Z2"), 0.0)
    cp(("Z2", 15, 143, 16), bd8)
    ts(("Z2", 16, 144, 16), bd8, 2.0 ** -30, A.mult)
    for a in range(8):
        ts(("PQ", 128 * a, 128 * a + 128, 1), ("Z2", 15 - 2 * a, 143 - 2 * a, 1), 2.0 ** (56 - 14 * a), A.mult)
    fill(whole("ONE16"), -16.0)
    fill(whole("L2"), 256.0)
    add("G", 3.8, lambda: g.affine_select(T.L2[:, :], T.L2[:, :], [[-1, 16], [-16, 8], [0, 16]], A.is_equal, 0.0, 0, 1),
        (whole("L2"),), (whole("L2"),))
    ln2 = math.log(2.0)

    def row(buf, k):
        return (buf, 15 - k, 143 - k, 1)

    def cut(ws):
        return [(sum(ws[:j]), sum(ws[:j + 1])) for j in range(len(ws))]

    sends = {}

    def lead(e, c):
        first, last = e == 0, e == LE - 1
        r0, wa, wb = R * c, 4 * R * c, 4 * R * c + 4 * R

        def B(nm, a=0, b=None, st=1):
            w = PER_RACK[nm][0] * R if nm in PER_RACK else R // 16
            return (nm, w * c + a, w * c + (w if b is None else b), st)

        def P(b, j, n=1):
            return ("ps%d" % b, R * j, R * (j + n), 1)

        def Q(nm, j=0, n=1):
            b, s = PLACE[nm]
            return P(4 + c if b is None else b, s + j, n)

        def send(src, sem):
            to = ("HL", src[1] + 768, src[2] + 768, 1)
            sends[sem] = add("G", PAR["ISS"], lambda: g.remote_dma(
                out_ap=ap(to), in_ap=ap(src), remote_sem=T.sem[sem], local_sem=T.sem.loc, pid=pid, routing_id=rid,
                dma_engine_mask=emask), (src,), (), kind="s")

        def store(out, src, s):
            add("Y", .1, lambda: SY.dma_start(out, ap(src)), (src,), (), kind="d", sem="st%d" % (3 * c + s), val=16, lat=2.3)
        land = ("HL", 768 * e + 3 * r0, 768 * e + 3 * r0 + 3 * R, 1)
        hl, hi, lo, z = sub(land, 0, 2 * R), sub(land, 0, R), sub(land, R, 2 * R), sub(land, 2 * R, 3 * R)
        ones = sub(sl("ones"), 0, R)
        if not first:
            for o, s in ((land, "az%d_%d" % (e, c)),) if c in PAR["ONE"] else ((hl, "ah%d_%d" % (e, c)), (z, "az%d_%d" % (e, c))):
                add("R", 0, None, (), (o,), kind="r", sem=s, val=neng, lat=PAR["REM"], extra=(sends[s],))
        thr = col(11 if first else 12)
        if PAR["KF"]:
            mms(grp(Q("K"), (sl("ID"), hi), (sl("ID"), lo)))
            ts(B("K16"), Q("K"), -96 - V0, A.add)
            act(B("Kf"), Q("K"), AF.Copy, bias=-64 - V0)
        up = sub(Q("u"), 0, R // 16)
        mms(grp(up, *[(row("WZ", r), sub(z, r, R, 16)) for r in range(16)]))
        cp(B("ua"), up)
        ts(B("ub"), B("ua"), 63, A.bitwise_and)
        tt(B("uc"), B("ub"), B("ub"), A.mult)
        ts(B("ud"), B("uc"), 5, A.arith_shift_right, 3, A.bitwise_and)
        if PAR["C4"]:
            for a in range(R // 16):
                ts(B("c16", a, a + 1), B("ud", a, a + 1), col(3), A.add, 64.0 * a, A.add)
        else:
            tt(B("ub"), B("ud"), whole("I4"), A.add)
            cp(B("c16"), B("ub"))
        mms(([] if PAR["KF"] else grp(Q("K"), (sl("ID"), hi), (sl("ID"), lo))) +
            (grp(Q("lin"), (whole("W37"), z), (whole("W37"), z), (sl("ID64"), hi), (sl("ID64"), lo)) if PAR["LB"] else
             grp(Q("lin"), (whole("W37"), z), (sl("ID2"), hi), (sl("ID2"), lo))))
        if not PAR["KF"]:
            ts(B("K16"), Q("K"), -96 - V0, A.add)
        if PAR["LB"]:
            cp(B("la"), Q("lin"))
        if not PAR["KF"]:
            act(B("Kf"), Q("K"), AF.Copy, bias=-64 - V0)
        if PAR["LB"]:
            ts(B("lb"), B("la"), 131071, A.bitwise_and)
        tt(B("p1"), ("Gf", wa, wb, 1, B("c16")), B("Kf"), A.mult)
        if PAR["LB"]:
            tt(B("s1"), B("p1"), B("lb"), A.add)
        else:
            ts(B("lb"), B("p1"), 5, A.arith_shift_right)
            tt(B("s1"), B("lb"), Q("lin"), A.add)
        if PAR["LB"]:
            ts(B("s2"), B("s1"), 5, A.arith_shift_right, 4095, A.bitwise_and)
        else:
            ts(B("s2"), B("s1"), 4095, A.bitwise_and)
        cp(B("s16"), B("s2"))
        for j, (a, b) in enumerate(cut(PAR["XP"])):
            o, w = B("x", 16 * a, 16 * b), ("X", 0, 4096, 1, B("K16", a, b))
            if j in PAR["XV"]:
                cp(o, w)
            else:
                act(o, w, AF.Copy)
        act(B("Wo"), ("Wf", wa, wb, 1, B("c16")), AF.Copy, bias=V0)
        for j, (a, b) in enumerate(cut(PAR["YP"])):
            o, w, x = B("d", 16 * a, 16 * b), ("Y", 0, 4096, 1, B("s16", a, b)), B("x", 16 * a, 16 * b)
            if (j, c) in PAR["YS"]:
                act(o, w, AF.Copy)
                mms(grp(Q("yx", 0, (b - a) // 4), (sl("NID"), x), (sl("ID"), o)))
                act(o, Q("yx", 0, (b - a) // 4), AF.Abs)
            else:
                tt(o, w, x, A.subtract)
                act(o, o, AF.Abs)
        for j in range(4 if PAR["E4"] else 0):
            for k in range(4 * j, 4 * j + 4, 2):
                mms([m for k2 in (k, k + 1) for m in grp(P(j % 2, k2 % 4), (sl("NID"), z), (sl("ID"), B("x", k2, 16 * R, 16)))])
            for k in range(4 * j, 4 * j + 4, 2):
                act(B("sg", R * k, R * k + 2 * R), P(j % 2, k % 4, 2), AF.Sign, bias=0.5 - 16.0 * (7 - k // 2))
            if j % 2:
                mms([(sub(Q("cnt"), k, 128, (16, R)), B("sg", R * k, R * k + R), bd8, True, True) for k in range(4 * j - 4, 4 * j + 4)])
        cs = sub(B("cs"), 0, 128, (1, R))
        act(cs, sub(Q("cnt"), 0, 128, (1, R)), AF.Sign, bias=-1.0)
        un, ta = B("un"), B("ta")
        mms(grp(Q("D"), *[(row("Z1", k), B("d", k, 16 * R, 16)) for k in range(16)]))
        act(un, Q("D"), AF.Sign, bias=thr, accum=("Fs", c, c + 1, 1))
        mms(grp(Q("hd"), (cs, sub(sl("ID"), 0, R, (1, R))), (sl("NID"), un)))
        act(B("hd"), Q("hd"), AF.Relu, bias=-1.0)
        mms(grp(Q("F"), (sl("IDm16"), un), (sl("TGE"), B("hd"))))
        act(ta, Q("F"), AF.Sign, bias=-16.0, accum=("Fs", NC + c, NC + c + 1, 1))
        mms(grp(Q("ex", 0), (sl("DF"), ones), (sl("TFo"), un), (sl("IDm256"), ta)) + grp(Q("ex", 1), (sl("THo"), un), (sl("THt"), ta)) +
            grp(Q("ex", 2), (sl("DO"), ones), (sl("TEo"), un)))
        mms(grp(Q("val"), (sl("Cval"), ones), (sl("ID2"), hi), (sl("ID2"), lo), (sl("IDbig"), un), (sl("IDbig"), ta)) +
            grp(Q("new"), (sl("Cnew"), ones), (sl("ID"), hi), (sl("ID"), lo), (sl("IDbig"), un), (sl("IDbig"), ta)))
        count = c == NC - 1 and not last
        if count:
            part, fa = ("Fs", 0, 2 * NC - 1, 1), sub(Q("A"), 0, 1)
            add("V", .06, lambda: V.tensor_reduce(ap(whole("Ff")), ap(part), AxisListType.X, A.add), (part,), (whole("Ff"),))
            mms(grp(fa, (whole("ONE16"), whole("Ff")), (whole("ONE16"), ("Fs", 2 * NC - 1, 2 * NC, 1))))
        if PAR["VF"]:
            tt(B("val"), B("Wo"), Q("val"), A.max)
        act(B("EE"), Q("ex", 0, 3), AF.Exp, bias=col(22), scale=ln2)
        mms(grp(Q("E"), *[(sl("ID"), B("EE", R * j, R * j + R)) for j in range(3)]) +
            grp(Q("E98"), *[(sl("ID98"), B("EE", R * j, R * j + R)) for j in range(3)]))
        if not PAR["VF"]:
            tt(B("val"), B("Wo"), Q("val"), A.max)
        if count:
            cp(whole("Fi"), fa)
            ts(whole("Fj"), whole("Fi"), 511, A.bitwise_and)
            ts(col(12), whole("Fj"), -1.0, A.mult, col(11), A.add)
        tt(B("nw"), B("Wo"), Q("new"), A.min)
        tt(B("WW", 0, R), B("val"), Q("E98"), A.mult)
        tt(Q("V"), B("val"), Q("E"), A.mult)
        tt(B("WW", R, 2 * R), Q("V"), B("WW", 0, R), A.subtract)
        pair = Q("pair", 0, 2)
        for a in range(8):
            u = 2.0 ** (14 * a - 56)
            ts(B("CL", 2 * R * a, 2 * R * a + 2 * R), B("WW"), 64 * u, A.max, u * 2 ** 20, A.min)
            if a % 2:
                mms(([(pair, sl("CQ"), whole("CT"), True, False)] if a == 1 else []) +
                    [(pair, ("PQ", 128 * b, 128 * b + 128, 1), B("CL", 2 * R * b, 2 * R * b + 2 * R), False, b == 7) for b in (a - 1, a)])
        for j in range(2):
            if PAR["TV"]:
                ts(B("tq", R * j, R * j + R), Q("pair", j), col(6), A.mult, col(4 + j), A.add)
            else:
                act(B("tq", R * j, R * j + R), Q("pair", j), AF.Identity, bias=col(4 + j), scale=col(6))
        hs, nz = ("HS",) + hl[1:], ("HS",) + z[1:]
        tt(hs, B("tq"), pair, A.add)
        if not last and c not in PAR["ONE"]:
            send(hs, "ah%d_%d" % (e + 1, c))
        elif last:
            mms(grp(Q("yk"), (sl("ID"), sub(hs, 0, R)), (sl("ID"), sub(hs, R, 2 * R))))
            act(("YK", r0, r0 + R, 1), Q("yk"), AF.Copy, bias=-96 - V0)
            store(T.yk[:, r0:r0 + R], ("YK", r0, r0 + R, 1), 0)
        act(B("gw"), ta, AF.Abs, scale=V0)
        tt(("Wf", wa, wb, 1, B("c16")), B("nw"), B("gw"), A.subtract)
        if last:
            store(T.yw[:, wa:wb], ("Wf", wa, wb, 1), 1)
        for j in range(4):
            b = 2 + j % 2
            for k0 in (4 * j, 4 * j + 2):
                mms([m for k in (k0, k0 + 1) for m in grp(P(b, k % 4), (sl("ID"), B("x", k, 16 * R, 16)),
                                                          (("L2", 128 * k, 128 * k + 128, 1), ta))])
            if PAR["MG"] == 2:
                for h in range(2):
                    if j == 0 and h == 0:
                        ts(B("AC", 0, 2 * R), P(b, 0, 2), 256.0, A.max)
                    else:
                        tt(B("AC", 0, 2 * R), B("AC", 0, 2 * R), P(b, 2 * h, 2), A.max)
            elif j == 0:
                ts(B("AC"), P(b, 0, 4), 256.0, A.max)
            elif j < 3:
                tt(B("AC"), B("AC"), P(b, 0, 4), A.max)
        if PAR["MG"] == 2:
            tt(B("mz"), B("AC", 0, R), B("AC", R, 2 * R), A.max)
        elif PAR["MG"]:
            tt(Q("m", 0, 2), B("AC", 0, 2 * R), P(3, 0, 2), A.max)
            tt(B("AC", 2 * R, 4 * R), B("AC", 2 * R, 4 * R), P(3, 2, 2), A.max)
            tt(Q("m"), B("AC", 2 * R, 3 * R), Q("m"), A.max)
            tt(B("AC", 3 * R, 4 * R), B("AC", 3 * R, 4 * R), Q("m", 1), A.max)
            tt(B("mz"), B("AC", 3 * R, 4 * R), Q("m"), A.max)
        else:
            tt(P(3, 0, 2), B("AC", 0, 2 * R), P(3, 0, 2), A.max)
            tt(B("AC", 2 * R, 4 * R), B("AC", 2 * R, 4 * R), P(3, 2, 2), A.max)
            tt(B("AC", 0, 2 * R), B("AC", 2 * R, 4 * R), P(3, 0, 2), A.max)
            tt(B("mz"), B("AC", 0, R), B("AC", R, 2 * R), A.max)
        mms(grp(Q("z"), (sl("ID"), z), (sl("NID"), B("mz"))))
        act(nz, Q("z"), AF.Abs, bias=256.0)
        if not last:
            send(("HS",) + land[1:] if c in PAR["ONE"] else nz, "az%d_%d" % (e + 1, c))
        else:
            store(T.yz[:, r0:r0 + R], nz, 2)

    for e in range(LE):
        for c in range(NC):
            cur[0] = NC * e + c
            lead(e, c)

    if "o" not in _ORDER:
        _ORDER["o"] = schedule(ops)
    place = {"V": 0, "S": 0, "T": 0, "G": 0}
    known = {q: {} for q in QS}
    for i in _ORDER["o"]:
        o = ops[i]
        q = o["q"]
        if o["kind"] == "r":
            o["clk"] = {o["sem"]: o["val"]}
            continue
        kn, o["wait"] = known[q], {}
        for j in sorted((j for j, w in o["deps"].items() if w), key=lambda j: -ops[j].get("pos", 1 << 30)):
            p = ops[j]
            sem, val = (p["sem"], p["val"]) if p["kind"] != "c" else ("e" + p["q"], p["pos"])
            if kn.get(sem, 0) < val:
                o["wait"][sem] = p
                p["seen"] = True
                for s2, v2 in p["clk"].items():
                    if kn.get(s2, 0) < v2:
                        kn[s2] = v2
        o["clk"] = dict(kn)
        if o["kind"] == "c":
            place[q] += 1
            o["pos"] = o["clk"]["e" + q] = place[q]
        elif o["kind"] == "d":
            o["clk"][o["sem"]] = o["val"]
    count = {"V": 0, "S": 0, "T": 0, "G": 0}
    nsend = 0
    for i in _ORDER["o"]:
        o = ops[i]
        q = o["q"]
        if o["kind"] == "r":
            continue
        for sem, p in o["wait"].items():
            QS[q].wait_ge(T.sem[sem], p["val"])
        ins = o["emit"]()
        if o["kind"] == "c":
            if "seen" in o or o["pos"] == place[q]:
                count[q] += 1
                o["val"] = count[q]
                ins.then_inc(T.sem["e" + q], 1)
        elif o["kind"] == "d":
            ins.then_inc(T.sem[o["sem"]], 16)
        else:
            nsend += 1
    kn = known["Y"]
    for q in ("V", "S", "T", "G"):
        SY.wait_ge(T.sem["e" + q], count[q])
    for o in ops:
        if o["kind"] in ("d", "r") and kn.get(o["sem"], 0) < o["val"]:
            SY.wait_ge(T.sem[o["sem"]], o["val"])
            kn[o["sem"]] = o["val"]
    g.wait_ge(T.sem.loc, neng * nsend)


def schedule(ops):
    n = len(ops)
    pred = [[(j, PAR["HOP"] if ops[j]["q"] != o["q"] else PAR["HOPS"] if w else 0.0) for j, w in o["deps"].items()] for o in ops]
    succ = [[] for _ in range(n)]
    for i in range(n):
        for j, h in pred[i]:
            succ[j].append((i, h))

    def run(nxt, prv, prio, back, look=0.0):
        cnt = [len(p) for p in prv]
        ready, free, cand, fin, order = [0.0] * n, {}, {}, [0.0] * n, []
        for i in range(n):
            if cnt[i] == 0:
                ready[i] = ops[i]["lat"] if back else 0.0
                cand.setdefault(ops[i]["q"], []).append(i)
        end_all = 0.0
        while len(order) < n:
            st, q = min((max(free.get(q, 0.0), min(ready[i] for i in lst)), q) for q, lst in cand.items() if lst)
            i = max((i for i in cand[q] if ready[i] <= st + 0.02), key=lambda i: (prio[i], -i))
            soon = [j for j in cand[q] if st < ready[j] < st + ops[i]["dur"] and prio[j] > prio[i]]
            if soon and look:
                j = max(soon, key=lambda j: (prio[j], -j))
                if max(ready[j] + prio[j], ready[j] + ops[j]["dur"] + prio[i]) < st + ops[i]["dur"] + prio[j] - look:
                    fit = [k for k in cand[q] if ready[k] <= st and st + ops[k]["dur"] <= ready[j] + look]
                    i = max(fit, key=lambda k: (prio[k], -k)) if fit else j
            cand[q].remove(i)
            end = fin[i] = max(free.get(q, 0.0), ready[i]) + ops[i]["dur"]
            if q != "R":
                free[q] = end
            if not back:
                end += ops[i]["lat"]
            end_all = max(end_all, end)
            order.append(i)
            for k, h in nxt[i]:
                ready[k] = max(ready[k], end + h + (ops[k]["lat"] if back else 0.0))
                cnt[k] -= 1
                if cnt[k] == 0:
                    cand.setdefault(ops[k]["q"], []).append(k)
        return end_all, order, fin

    def replay(order, speed, far=1.0):
        free, end = {}, [0.0] * n
        for i in order:
            o = ops[i]
            t = max([end[j] + h for j, h in pred[i]] + [free.get(o["q"], 0.0)]) + o[speed]
            if o["q"] != "R":
                free[o["q"]] = t
            end[i] = t + o["lat"] * (far if o["grp"] >= 0 else 1.0)
        return max(end)

    best = None
    for skew in PAR["S"]:
        loc, prio = [0.0] * n, [0.0] * n
        for i in range(n - 1, -1, -1):
            gp, d = ops[i]["grp"], ops[i]["dur"] + ops[i]["lat"]
            loc[i] = d + max([loc[k] + h for k, h in succ[i] if ops[k]["grp"] == gp] + [0.0])
            if gp >= 0:
                prio[i] = loc[i] - (gp // NC) * PAR["T"] - (gp % NC) * skew
            else:
                prio[i] = d + max([prio[k] + h for k, h in succ[i]] + [-99.0])
        for look in PAR["LOOK"]:
            cur = run(succ, pred, prio, False)
            for _ in range(PAR["PASS"]):
                cur = run(succ, pred, run(pred, succ, cur[2], True, look)[2], False, look)
                score = replay(cur[1], "fast") + replay(cur[1], "slow") / 1.5 + PAR["FAR"] * replay(cur[1], "fast", 1.8)
                if best is None or score < best[0]:
                    best = (score, cur[1], cur[0])
    _ORDER["est"] = best[2]
    _ORDER["ops"] = ops
    return best[1]
